import numpy as np
import ml_dtypes


def mxq(x, axis, fmt="e4m3"):
    dtype, down = {"e4m3": (ml_dtypes.float8_e4m3fn, 7), "e5m2": (ml_dtypes.float8_e5m2, 14)}[fmt]
    v = np.moveaxis(np.asarray(x, np.float32).astype(ml_dtypes.bfloat16).astype(np.float64), axis, -1)
    blocks = v.reshape(v.shape[:-1] + (-1, 32))
    amax = np.abs(blocks).max(-1, keepdims=True)
    byte = np.maximum(np.where(amax > 0, np.frexp(amax)[1] - 1 + 127, 0) - down, 1)
    scale = np.exp2(byte - 127.0)
    codes = (blocks / scale).astype(np.float32).astype(dtype).astype(np.float64)
    return np.moveaxis((codes * scale).reshape(v.shape), -1, axis)


WIDE = False


def mx_kscale(k):
    if not WIDE:
        return np.ones(k)
    levels = np.array([10, -10, 5, -5, 0])
    if k % 512:
        return np.exp2(np.random.permutation(np.resize(levels, k // 32))).repeat(32)
    a = np.empty((k // 512, 16))
    for p in range(k // 512):
        a[p, :8] = np.random.permutation(np.resize(levels, 8))
        for g in range(8):
            far = levels[np.abs(levels - a[p, g]) >= 10]
            a[p, g + 8] = far[np.random.randint(len(far))]
    return np.exp2(a.ravel()).repeat(32)


def f64(x):
    return np.asarray(x).astype(np.float64)


def striped(idx):
    return np.tile(idx.reshape(-1, 16).T, (8, 1)).astype(np.uint16)


def unstriped(offs):
    return offs[:16].T.reshape(-1).astype(np.int64)


E2M1 = np.array([0.0, 0.5, 1.0, 1.5, 2.0, 3.0, 4.0, 6.0, -0.0, -0.5, -1.0, -1.5, -2.0, -3.0, -4.0, -6.0])


def pack_weight(w, fmt):
    k, n = w.shape
    w = f64(np.asarray(w, np.float32).astype(ml_dtypes.bfloat16)).reshape(k // 32, 32, n)
    amax = np.abs(w).max(1)
    if fmt == "e4m3":
        byte = np.frexp(amax)[1] - 1 + 127 - 7
    else:
        mant, ex = np.frexp(amax / 6.0)
        byte = np.where(mant > 0.5, ex, ex - 1) + 127
    byte = np.clip(np.where(amax > 0, byte, 1), 1, 254)
    scaled = (w * np.exp2(127.0 - byte)[:, None, :]).reshape(k, n).astype(np.float32)
    by_word = np.ascontiguousarray(scaled.reshape(k // 512, 128, 4, n).transpose(0, 1, 3, 2))
    if fmt == "e4m3":
        words = by_word.astype(ml_dtypes.float8_e4m3fn).view(np.uint8)
    else:
        c = by_word.astype(ml_dtypes.float4_e2m1fn).view(np.uint8) & 0xF
        words = (c[..., 0::2] | (c[..., 1::2] << 4)).reshape(k // 512, 128, 2 * n)
    return np.ascontiguousarray(words), np.ascontiguousarray(byte.astype(np.uint8).reshape(k // 512, 16, n))


def unpack_weight(words, scales, fmt):
    g, _, n = scales.shape
    words = np.ascontiguousarray(words).reshape(g, 128, n, -1)
    if fmt == "e4m3":
        vals = words.view(ml_dtypes.float8_e4m3fn).astype(np.float64)
    else:
        nib = np.empty((g, 128, n, 4), np.uint8)
        nib[..., 0::2] = words & 0xF
        nib[..., 1::2] = words >> 4
        vals = E2M1[nib]
    vals = vals * np.repeat(np.exp2(scales.astype(np.float64) - 127.0), 8, axis=1)[..., None]
    return vals.transpose(0, 1, 3, 2).reshape(g * 512, n)


def gelu(v):
    return 0.5 * v * (1.0 + np.tanh(np.sqrt(2.0 / np.pi) * (v + 0.044715 * v**3)))


def striped8(idx):
    return np.concatenate([v.reshape(-1, 16).T for v in idx]).astype(np.uint16)


def unstriped8(offs):
    return np.stack([offs[16 * g:16 * g + 16].T.reshape(-1) for g in range(8)]).astype(np.int64)


def runs(v, idx8):
    k = np.arange(v.shape[0])
    return v[k[:, None], idx8[k % 512 // 64]]


K, T, S, H, N = 512, 2048, 1024, 1024, 512


def setup_inputs():
    n = np.random.standard_normal
    s = mx_kscale(K)[:, None]
    u = mx_kscale(H)[:, None]
    tab_words, tab_scales = pack_weight(n((K, T)) * s, "e4m3")
    tab2_words, tab2_scales = pack_weight(n((K, T)) * s, "e4m3")
    wm_words, wm_scales = pack_weight(n((K, H)) / np.sqrt(K) / s, "e2m1")
    we = (n((K, H)) / np.sqrt(K) / s).astype(np.float32)
    gain = (np.exp(0.3 * n(H)) * u[:, 0]).astype(np.float32)
    wc_words, wc_scales = pack_weight(2.0 * n((H, N)) / np.sqrt(H) / u, "e4m3")
    offs = striped8(np.stack([np.random.permutation(T)[:S] for _ in range(8)]))
    offs2 = striped(np.random.permutation(T)[:S])
    return {"tab_words": tab_words, "tab_scales": tab_scales,
            "tab2_words": tab2_words, "tab2_scales": tab2_scales,
            "wm_words": wm_words, "wm_scales": wm_scales,
            "we": we, "gain": gain,
            "wc_words": wc_words, "wc_scales": wc_scales,
            "offs": offs, "offs2": offs2}


def reference(tab_words, tab_scales, tab2_words, tab2_scales, wm_words, wm_scales,
              we, gain, wc_words, wc_scales, offs, offs2):
    v = runs(unpack_weight(tab_words, tab_scales, "e4m3"), unstriped8(offs))
    v2 = unpack_weight(tab2_words, tab2_scales, "e4m3")[:, unstriped(offs2)]
    wm = unpack_weight(wm_words, wm_scales, "e2m1")
    a = wm.T @ v
    b = wm.T @ v2
    e = mxq(f64(we), 0, "e4m3").T @ v
    d = a - b
    h = f64(gain)[:, None] * (np.tanh(e) / (1.0 + d * d))
    wc = unpack_weight(wc_words, wc_scales, "e4m3")
    return wc.T @ mxq(h, 0, "e4m3")

@@ -1,0 +1,263 @@
+from contextlib import ExitStack
+
+import concourse.mybir as mybir
+
+K, T, S, H, N = 512, 2048, 1024, 1024, 512
+FLOPS = 2 * (3 * K * H * S + H * N * S)
+
+F32 = mybir.dt.float32
+BF16 = mybir.dt.bfloat16
+I32 = mybir.dt.int32
+U32 = mybir.dt.uint32
+U16 = mybir.dt.uint16
+U8 = mybir.dt.uint8
+FP8X4 = mybir.dt.float8_e4m3fn_x4
+FP4X4 = mybir.dt.float4_e2m1fn_x4
+ACT = mybir.ActivationFunctionType
+ALU = mybir.AluOpType
+
+P = 128
+PACK = 4
+PASS = P * PACK
+R_PASSES = H // PASS
+HALF = 512
+HALVES = S // HALF
+QUARTER = 256
+WE_COLS = 256
+TINY = 2.0 ** -100
+
+
+def tile_list_fold_match_evidence_kernel(
+    tc, tab_words, tab_scales, tab2_words, tab2_scales, wm_words, wm_scales,
+    we, gain, wc_words, wc_scales, offs, offs2, out,
+):
+    nc = tc.nc
+    with ExitStack() as ctx:
+        lists = ctx.enter_context(tc.tile_pool(name="lists", bufs=1))
+        keep = ctx.enter_context(tc.tile_pool(name="keep", bufs=1))
+        ring = ctx.enter_context(tc.tile_pool(name="ring", bufs=3))
+        psum_ab = ctx.enter_context(tc.psum_pool(name="psum_ab", bufs=2))
+        psum_eo = ctx.enter_context(tc.psum_pool(name="psum_eo", bufs=4))
+
+        def held(shape, dtype, name, tag=""):
+            return keep.tile(shape, dtype, name=name, tag=tag or name, align_bytes=64)
+
+        fold_list = lists.tile([P, S // 16], U16, name="fold_list")
+        query_list = lists.tile([P, S // 16], U16, name="query_list")
+
+        fold_words = held([P, T], U32, "fold_words")
+        fold_bytes = held([P, T], U8, "fold_bytes")
+        fold_plane = held([P, S], U8, "fold_plane")
+        query_bytes = held([P, T], U8, "query_bytes")
+        wm_raw = held([P, 2 * H], U8, "wm_raw")
+        wm_raw_scales = held([P, H], U8, "wm_raw_scales")
+        gain_cols = held([P, R_PASSES, PACK], F32, "gain_cols")
+        we_first = [held([P, PACK, WE_COLS], F32, "we_first%d" % c) for c in range(PASS // WE_COLS)]
+
+        nc.vector.memset(fold_bytes[:].bitcast(I32), 0)
+        nc.vector.memset(query_bytes[:].bitcast(I32), 0)
+        nc.vector.memset(wm_raw_scales[:].bitcast(I32), 0)
+        nc.vector.memset(fold_plane[:].bitcast(I32), 0)
+
+        def load_we(dst, c0, width):
+            cols = we[:, c0:c0 + width]
+            nc.sync.dma_start(out=dst[:], in_=cols.rearrange("(p i) w -> p i w", i=PACK))
+
+        def table_words(words):
+            return words[0].rearrange("p t i -> p (t i)").bitcast(I32)
+
+        nc.sync.dma_start(fold_list[:], offs)
+        nc.scalar.dma_start(out=fold_bytes[0:P:8, :].bitcast(I32), in_=tab_scales[0].bitcast(I32))
+        load_we(we_first[0], 0, WE_COLS)
+        nc.sync.dma_start(query_list[:], offs2)
+        nc.sync.dma_start(out=gain_cols[:], in_=gain.rearrange("(g p t) -> p g t", p=P, t=PACK))
+        load_we(we_first[1], WE_COLS, WE_COLS)
+        nc.sync.dma_start(out=fold_words[:].bitcast(I32), in_=table_words(tab_words))
+        nc.sync.dma_start(out=wm_raw[:].bitcast(I32), in_=wm_words[0].bitcast(I32))
+        for d in range(4):
+            nc.gpsimd.dma_start(
+                out=query_bytes[32 * d:32 * d + 4, :].bitcast(I32),
+                in_=tab2_scales[0, 4 * d:4 * d + 4, :].bitcast(I32),
+            )
+        for d in range(4):
+            nc.gpsimd.dma_start(
+                out=wm_raw_scales[32 * d:32 * d + 4, :].bitcast(I32),
+                in_=wm_scales[0, 4 * d:4 * d + 4, :].bitcast(I32),
+            )
+
+        gain_flat = gain_cols[:].rearrange("p g t -> p (g t)")
+        row_factor = held([P, R_PASSES * PACK], F32, "row_factor")
+        gain_abs = held([P, R_PASSES * PACK], F32, "gain_abs")
+        gain_floor = held([P, R_PASSES * PACK], F32, "gain_floor")
+        gain_inv = held([P, R_PASSES * PACK], F32, "gain_inv")
+        nc.scalar.activation(row_factor[:], gain_flat, ACT.Sign)
+
+        fold_picked = held([P, S], U8, "fold_picked")
+        nc.vector.tensor_copy(fold_picked[:], fold_bytes[:].indirect(fold_list[:]))
+        for r in range(4):
+            nc.sync.dma_start(
+                out=fold_plane[r:P:32, :].bitcast(I32),
+                in_=fold_picked[8 * r:P:32, :].bitcast(I32),
+            )
+        we_second = held([P, PACK, PASS], F32, "we_second", tag="fold_bytes")
+        load_we(we_second, PASS, PASS)
+
+        we_bf = [held([P, PACK, P, PACK], BF16, "we_bf%d" % g) for g in range(R_PASSES)]
+        we_codes = [held([P, PASS], U32, "we_codes%d" % g) for g in range(R_PASSES)]
+        we_plane = [held([P, PASS], U8, "we_plane%d" % g) for g in range(R_PASSES)]
+
+        def round_we(c):
+            g, part = divmod(c, PASS // WE_COLS)
+            width = WE_COLS // PACK
+            raw = we_first[part][:] if g == 0 else we_second[:, :, part * WE_COLS:(part + 1) * WE_COLS]
+            nc.scalar.activation(
+                we_bf[g][:, :, part * width:(part + 1) * width, :].rearrange("p t m i -> p m i t"),
+                raw.rearrange("p i (m t) -> p m i t", t=PACK),
+                ACT.Copy,
+            )
+
+        def quantize_we(g):
+            nc.vector.quantize_mx(
+                out=we_codes[g][:].bitcast(FP8X4),
+                scales=we_plane[g][:],
+                in_=we_bf[g][:].rearrange("p t m i -> p (t m i)"),
+            )
+
+        fold_cols = [held([P, HALF], U32, "fold_cols%d" % j) for j in range(HALVES)]
+        query_cols = [held([P, HALF], U32, "query_cols%d" % j) for j in range(HALVES)]
+        query_plane = held([P, S], U8, "query_plane")
+
+        def gather_words(dst, words, picks, j):
+            per = HALF // 16
+            nc.vector.tensor_copy(dst[j][:], words[:].indirect(picks[:, j * per:(j + 1) * per]))
+
+        evidence = [[held([P, PACK, HALF], F32, "evidence%d%d" % (g, j)) for j in range(HALVES)]
+                    for g in range(R_PASSES)]
+        match = [[held([P, PACK, HALF], F32, "match%d%d" % (g, j)) for j in range(HALVES)]
+                 for g in range(R_PASSES)]
+
+        def evidence_rows(g, j):
+            for t in range(PACK):
+                e = psum_eo.tile([P, HALF], F32, name="eo")
+                nc.tensor.matmul_mx(
+                    out=e[:],
+                    lhsT=we_codes[g][:, t * P:(t + 1) * P].bitcast(FP8X4),
+                    lhsT_scale=we_plane[g][:, t * P:(t + 1) * P],
+                    rhs=fold_cols[j][:].bitcast(FP8X4),
+                    rhs_scale=fold_plane[:, j * HALF:(j + 1) * HALF],
+                    start=True, stop=True,
+                )
+                col = g * PACK + t
+                nc.scalar.activation(evidence[g][j][:, t, :], e[:], ACT.Tanh,
+                                     scale=row_factor[:, col:col + 1])
+
+        round_we(0)
+        round_we(1)
+        query_words = held([P, T], U32, "query_words", tag="we_first1")
+        nc.sync.dma_start(out=query_words[:].bitcast(I32), in_=table_words(tab2_words))
+        nc.vector.tensor_copy(query_plane[:], query_bytes[:].indirect(query_list[:]))
+        quantize_we(0)
+        gather_words(fold_cols, fold_words, fold_list, 0)
+        evidence_rows(0, 0)
+        gather_words(fold_cols, fold_words, fold_list, 1)
+        wc_codes = held([P, R_PASSES, N], U32, "wc_codes", tag="fold_words")
+        wc_plane = held([P, R_PASSES, N], U8, "wc_plane", tag="query_bytes")
+        nc.sync.dma_start(
+            out=wc_codes[:].bitcast(I32),
+            in_=wc_words.rearrange("g p n i -> p g (n i)").bitcast(I32),
+        )
+        nc.vector.memset(wc_plane[:].rearrange("p g n -> p (g n)").bitcast(I32), 0)
+        for d in range(4):
+            nc.sync.dma_start(
+                out=wc_plane[32 * d:32 * d + 4, :, :].bitcast(I32),
+                in_=wc_scales[:, 4 * d:4 * d + 4, :].rearrange("g q n -> q g n").bitcast(I32),
+            )
+        round_we(2)
+        round_we(3)
+        evidence_rows(0, 1)
+
+        wm_codes = held([P, 2 * H], U8, "wm_codes")
+        wm_plane = held([P, H], U8, "wm_plane")
+        nc.vector.tensor_copy(
+            wm_codes[:].bitcast(U16).rearrange("p (g t m) -> p g t m", g=R_PASSES, t=PACK),
+            wm_raw[:].bitcast(U16).rearrange("p (g m t) -> p g t m", g=R_PASSES, t=PACK),
+        )
+        nc.vector.tensor_copy(
+            wm_plane[:].rearrange("p (g t m) -> p g t m", g=R_PASSES, t=PACK),
+            wm_raw_scales[:].rearrange("p (g m t) -> p g t m", g=R_PASSES, t=PACK),
+        )
+        nc.vector.scalar_tensor_tensor(gain_abs[:], gain_flat, -1.0, gain_flat, ALU.mult, ALU.max)
+        nc.vector.tensor_scalar_max(gain_floor[:], gain_abs[:], TINY)
+        nc.vector.reciprocal(gain_inv[:], gain_floor[:])
+        gather_words(query_cols, query_words, query_list, 0)
+        quantize_we(1)
+        evidence_rows(1, 0)
+        evidence_rows(1, 1)
+        nc.scalar.copy(row_factor[:], gain_inv[:])
+
+        def match_rows(g, j):
+            for t in range(PACK):
+                col = g * PACK + t
+                a = psum_ab.tile([P, HALF], F32, name="a")
+                b = psum_ab.tile([P, HALF], F32, name="b")
+                for acc, cols, plane in ((b, query_cols, query_plane), (a, fold_cols, fold_plane)):
+                    nc.tensor.matmul_mx(
+                        out=acc[:],
+                        lhsT=wm_codes[:, 2 * P * col:2 * P * (col + 1)].bitcast(FP4X4),
+                        lhsT_scale=wm_plane[:, P * col:P * (col + 1)],
+                        rhs=cols[j][:].bitcast(FP8X4),
+                        rhs_scale=plane[:, j * HALF:(j + 1) * HALF],
+                        start=True, stop=True,
+                    )
+                b_out = ring.tile([P, HALF], F32, name="b_out")
+                rows = match[g][j][:, t, :]
+                nc.vector.tensor_copy(b_out[:], b[:])
+                nc.vector.tensor_tensor(rows, a[:], b_out[:], ALU.subtract)
+                nc.gpsimd.tensor_tensor(rows, rows, rows, ALU.mult)
+                nc.scalar.activation(rows, rows, ACT.Abs_reciprocal_sqrt,
+                                     bias=row_factor[:, col:col + 1], scale=row_factor[:, col:col + 1])
+
+        match_rows(0, 0)
+        gather_words(query_cols, query_words, query_list, 1)
+        match_rows(1, 0)
+        match_rows(0, 1)
+        match_rows(1, 1)
+
+        for q in range(S // QUARTER):
+            j, part = divmod(q, HALF // QUARTER)
+            cols = slice(part * QUARTER, (part + 1) * QUARTER)
+            h_codes = []
+            h_plane = []
+            for g in range(R_PASSES):
+                agree = ring.tile([P, PACK, QUARTER], F32, name="agree")
+                nc.scalar.activation(agree[:], match[g][j][:, :, cols], ACT.Square)
+                h = ring.tile([P, QUARTER, PACK], BF16, name="h", align_bytes=64)
+                nc.vector.tensor_tensor(
+                    h[:].rearrange("p (c i) t -> p c t i", i=4),
+                    agree[:].rearrange("p t (c i) -> p c t i", i=4),
+                    evidence[g][j][:, :, cols].rearrange("p t (c i) -> p c t i", i=4),
+                    ALU.mult,
+                )
+                codes = held([P, QUARTER], U32, "h_codes%d%d" % (q, g))
+                plane = held([P, QUARTER], U8, "h_plane%d%d" % (q, g))
+                nc.vector.quantize_mx(out=codes[:].bitcast(FP8X4), scales=plane[:],
+                                      in_=h[:].rearrange("p j t -> p (j t)"))
+                h_codes.append(codes)
+                h_plane.append(plane)
+            for pair in range(N // (2 * P)):
+                acc = psum_eo.tile([P, 2, QUARTER], F32, name="eo")
+                for u in range(2):
+                    n0 = (2 * pair + u) * P
+                    for g in range(R_PASSES):
+                        nc.tensor.matmul_mx(
+                            out=acc[:, u, :],
+                            lhsT=wc_codes[:, g, n0:n0 + P].bitcast(FP8X4),
+                            lhsT_scale=wc_plane[:, g, n0:n0 + P],
+                            rhs=h_codes[g][:].bitcast(FP8X4),
+                            rhs_scale=h_plane[g][:],
+                            start=(g == 0), stop=(g == R_PASSES - 1),
+                        )
+                result = ring.tile([P, 2, QUARTER], F32, name="result")
+                nc.scalar.copy(result[:], acc[:])
+                rows = out[2 * P * pair:2 * P * (pair + 1), q * QUARTER:(q + 1) * QUARTER]
+                nc.sync.dma_start(out=rows.rearrange("(u p) j -> p u j", p=P), in_=result[:])

@@ -35,7 +35,7 @@ def tile_list_fold_match_evidence_kernel(
     with ExitStack() as ctx:
         lists = ctx.enter_context(tc.tile_pool(name="lists", bufs=1))
         keep = ctx.enter_context(tc.tile_pool(name="keep", bufs=1))
-        ring = ctx.enter_context(tc.tile_pool(name="ring", bufs=3))
+        ring = ctx.enter_context(tc.tile_pool(name="ring", bufs=4))
         psum_ab = ctx.enter_context(tc.psum_pool(name="psum_ab", bufs=2))
         psum_eo = ctx.enter_context(tc.psum_pool(name="psum_eo", bufs=4))
 
@@ -45,40 +45,43 @@ def tile_list_fold_match_evidence_kernel(
         fold_list = lists.tile([P, S // 16], U16, name="fold_list")
         query_list = lists.tile([P, S // 16], U16, name="query_list")
 
-        fold_words = held([P, T], U32, "fold_words")
         fold_bytes = held([P, T], U8, "fold_bytes")
-        fold_plane = held([P, S], U8, "fold_plane")
         query_bytes = held([P, T], U8, "query_bytes")
+        fold_plane = held([P, S], U8, "fold_plane")
+        query_plane = held([P, S], U8, "query_plane")
         wm_raw = held([P, 2 * H], U8, "wm_raw")
         wm_raw_scales = held([P, H], U8, "wm_raw_scales")
         gain_cols = held([P, R_PASSES, PACK], F32, "gain_cols")
-        we_first = [held([P, PACK, WE_COLS], F32, "we_first%d" % c) for c in range(PASS // WE_COLS)]
+        blanks = [held([P, S // 4], I32, "blank%d" % u) for u in range(2)]
 
-        nc.vector.memset(fold_bytes[:].bitcast(I32), 0)
+        nc.gpsimd.memset(fold_bytes[:].bitcast(I32), 0)
+        for blank in blanks:
+            nc.gpsimd.memset(blank[:], 0)
+        nc.gpsimd.memset(wm_raw_scales[:].bitcast(I32), 0)
         nc.vector.memset(query_bytes[:].bitcast(I32), 0)
-        nc.vector.memset(wm_raw_scales[:].bitcast(I32), 0)
-        nc.vector.memset(fold_plane[:].bitcast(I32), 0)
+        nc.vector.tensor_copy(fold_plane[:].bitcast(I32), blanks[0][:])
+        nc.vector.tensor_copy(query_plane[:].bitcast(I32), blanks[1][:])
+
+        we_first = held([P, PASS // WE_COLS, PACK, WE_COLS], F32, "we_first", tag="blank0")
+        fold_words = held([P, T], U32, "fold_words", tag="blank1")
 
         def load_we(dst, c0, width):
             cols = we[:, c0:c0 + width]
-            nc.sync.dma_start(out=dst[:], in_=cols.rearrange("(p i) w -> p i w", i=PACK))
+            nc.sync.dma_start(out=dst, in_=cols.rearrange("(p i) w -> p i w", i=PACK))
 
-        def table_words(words):
-            return words[0].rearrange("p t i -> p (t i)").bitcast(I32)
+        def load_words(dst, words):
+            nc.sync.dma_start(out=dst[:].bitcast(I32),
+                              in_=words[0].rearrange("p t i -> p (t i)").bitcast(I32))
 
         nc.sync.dma_start(fold_list[:], offs)
-        nc.scalar.dma_start(out=fold_bytes[0:P:8, :].bitcast(I32), in_=tab_scales[0].bitcast(I32))
-        load_we(we_first[0], 0, WE_COLS)
+        nc.sync.dma_start(out=wm_raw[:].bitcast(I32), in_=wm_words[0].bitcast(I32))
+        nc.sync.dma_start(out=fold_bytes[0:P:8, :].bitcast(I32), in_=tab_scales[0].bitcast(I32))
         nc.sync.dma_start(query_list[:], offs2)
         nc.sync.dma_start(out=gain_cols[:], in_=gain.rearrange("(g p t) -> p g t", p=P, t=PACK))
-        load_we(we_first[1], WE_COLS, WE_COLS)
-        nc.sync.dma_start(out=fold_words[:].bitcast(I32), in_=table_words(tab_words))
-        nc.sync.dma_start(out=wm_raw[:].bitcast(I32), in_=wm_words[0].bitcast(I32))
-        for d in range(4):
-            nc.gpsimd.dma_start(
-                out=query_bytes[32 * d:32 * d + 4, :].bitcast(I32),
-                in_=tab2_scales[0, 4 * d:4 * d + 4, :].bitcast(I32),
-            )
+        nc.sync.dma_start(out=query_bytes[0:P:8, :].bitcast(I32), in_=tab2_scales[0].bitcast(I32))
+        for part in range(PASS // WE_COLS):
+            load_we(we_first[:, part], part * WE_COLS, WE_COLS)
+        load_words(fold_words, tab_words)
         for d in range(4):
             nc.gpsimd.dma_start(
                 out=wm_raw_scales[32 * d:32 * d + 4, :].bitcast(I32),
@@ -87,33 +90,40 @@ def tile_list_fold_match_evidence_kernel(
 
         gain_flat = gain_cols[:].rearrange("p g t -> p (g t)")
         row_factor = held([P, R_PASSES * PACK], F32, "row_factor")
-        gain_abs = held([P, R_PASSES * PACK], F32, "gain_abs")
         gain_floor = held([P, R_PASSES * PACK], F32, "gain_floor")
         gain_inv = held([P, R_PASSES * PACK], F32, "gain_inv")
         nc.scalar.activation(row_factor[:], gain_flat, ACT.Sign)
 
-        fold_picked = held([P, S], U8, "fold_picked")
-        nc.vector.tensor_copy(fold_picked[:], fold_bytes[:].indirect(fold_list[:]))
-        for r in range(4):
-            nc.sync.dma_start(
-                out=fold_plane[r:P:32, :].bitcast(I32),
-                in_=fold_picked[8 * r:P:32, :].bitcast(I32),
-            )
-        we_second = held([P, PACK, PASS], F32, "we_second", tag="fold_bytes")
-        load_we(we_second, PASS, PASS)
+        def gather_scales(plane, rows, picks, name):
+            picked = held([P, S], U8, name)
+            nc.vector.tensor_copy(picked[:], rows[:].indirect(picks[:]))
+            for r in range(4):
+                nc.sync.dma_start(out=plane[r:P:32, :].bitcast(I32),
+                                  in_=picked[8 * r:P:32, :].bitcast(I32))
+
+        gather_scales(fold_plane, fold_bytes, fold_list, "fold_picked")
+        query_words = held([P, T], U32, "query_words", tag="fold_bytes")
+        load_words(query_words, tab2_words)
+        gather_scales(query_plane, query_bytes, query_list, "query_picked")
+        we_second = held([P, PACK, PASS], F32, "we_second", tag="query_bytes")
+        load_we(we_second[:], PASS, PASS)
 
         we_bf = [held([P, PACK, P, PACK], BF16, "we_bf%d" % g) for g in range(R_PASSES)]
         we_codes = [held([P, PASS], U32, "we_codes%d" % g) for g in range(R_PASSES)]
         we_plane = [held([P, PASS], U8, "we_plane%d" % g) for g in range(R_PASSES)]
 
-        def round_we(c):
-            g, part = divmod(c, PASS // WE_COLS)
+        def round_we_first(part):
             width = WE_COLS // PACK
-            raw = we_first[part][:] if g == 0 else we_second[:, :, part * WE_COLS:(part + 1) * WE_COLS]
             nc.scalar.activation(
-                we_bf[g][:, :, part * width:(part + 1) * width, :].rearrange("p t m i -> p m i t"),
-                raw.rearrange("p i (m t) -> p m i t", t=PACK),
+                we_bf[0][:, :, part * width:(part + 1) * width, :].rearrange("p t m i -> p m i t"),
+                we_first[:, part].rearrange("p i (m t) -> p m i t", t=PACK),
                 ACT.Copy,
+            )
+
+        def round_we_second():
+            nc.vector.tensor_copy(
+                we_bf[1][:].rearrange("p t m i -> p m i t"),
+                we_second[:].rearrange("p i (m t) -> p m i t", t=PACK),
             )
 
         def quantize_we(g):
@@ -122,10 +132,6 @@ def tile_list_fold_match_evidence_kernel(
                 scales=we_plane[g][:],
                 in_=we_bf[g][:].rearrange("p t m i -> p (t m i)"),
             )
-
-        fold_cols = [held([P, HALF], U32, "fold_cols%d" % j) for j in range(HALVES)]
-        query_cols = [held([P, HALF], U32, "query_cols%d" % j) for j in range(HALVES)]
-        query_plane = held([P, S], U8, "query_plane")
 
         def gather_words(dst, words, picks, j):
             per = HALF // 16
@@ -151,33 +157,42 @@ def tile_list_fold_match_evidence_kernel(
                 nc.scalar.activation(evidence[g][j][:, t, :], e[:], ACT.Tanh,
                                      scale=row_factor[:, col:col + 1])
 
-        round_we(0)
-        round_we(1)
-        query_words = held([P, T], U32, "query_words", tag="we_first1")
-        nc.sync.dma_start(out=query_words[:].bitcast(I32), in_=table_words(tab2_words))
-        nc.vector.tensor_copy(query_plane[:], query_bytes[:].indirect(query_list[:]))
+        for part in range(PASS // WE_COLS):
+            round_we_first(part)
+        wm_codes = held([P, 2 * H], U8, "wm_codes")
         quantize_we(0)
+
+        fold_cols = [held([P, HALF], U32, "fold_cols%d" % j) for j in range(HALVES)]
+        query_cols = [held([P, HALF], U32, "query_cols%d" % j) for j in range(HALVES)]
+
+        def difference_rows(g, j, t, b_out):
+            col = g * PACK + t
+            a = psum_ab.tile([P, HALF], F32, name="a")
+            b = psum_ab.tile([P, HALF], F32, name="b")
+            for acc, cols, plane in ((b, query_cols, query_plane), (a, fold_cols, fold_plane)):
+                nc.tensor.matmul_mx(
+                    out=acc[:],
+                    lhsT=wm_codes[:, 2 * P * col:2 * P * (col + 1)].bitcast(FP4X4),
+                    lhsT_scale=wm_plane[:, P * col:P * (col + 1)],
+                    rhs=cols[j][:].bitcast(FP8X4),
+                    rhs_scale=plane[:, j * HALF:(j + 1) * HALF],
+                    start=True, stop=True,
+                )
+            nc.vector.tensor_copy(b_out[:], b[:])
+            nc.vector.tensor_tensor(match[g][j][:, t, :], a[:], b_out[:], ALU.subtract)
+            if t % 2 == 1:
+                both = match[g][j][:, t - 1:t + 1, :]
+                nc.gpsimd.tensor_tensor(both, both, both, ALU.mult)
+
+        def difference_pass(g, j, first=0):
+            for t in range(first, PACK):
+                difference_rows(g, j, t, ring.tile([P, HALF], F32, name="b_out"))
+
         gather_words(fold_cols, fold_words, fold_list, 0)
         evidence_rows(0, 0)
         gather_words(fold_cols, fold_words, fold_list, 1)
-        wc_codes = held([P, R_PASSES, N], U32, "wc_codes", tag="fold_words")
-        wc_plane = held([P, R_PASSES, N], U8, "wc_plane", tag="query_bytes")
-        nc.sync.dma_start(
-            out=wc_codes[:].bitcast(I32),
-            in_=wc_words.rearrange("g p n i -> p g (n i)").bitcast(I32),
-        )
-        nc.vector.memset(wc_plane[:].rearrange("p g n -> p (g n)").bitcast(I32), 0)
-        for d in range(4):
-            nc.sync.dma_start(
-                out=wc_plane[32 * d:32 * d + 4, :, :].bitcast(I32),
-                in_=wc_scales[:, 4 * d:4 * d + 4, :].rearrange("g q n -> q g n").bitcast(I32),
-            )
-        round_we(2)
-        round_we(3)
         evidence_rows(0, 1)
-
-        wm_codes = held([P, 2 * H], U8, "wm_codes")
-        wm_plane = held([P, H], U8, "wm_plane")
+        wm_plane = held([P, H], U8, "wm_plane", tag="we_bf0")
         nc.vector.tensor_copy(
             wm_codes[:].bitcast(U16).rearrange("p (g t m) -> p g t m", g=R_PASSES, t=PACK),
             wm_raw[:].bitcast(U16).rearrange("p (g m t) -> p g t m", g=R_PASSES, t=PACK),
@@ -186,62 +201,67 @@ def tile_list_fold_match_evidence_kernel(
             wm_plane[:].rearrange("p (g t m) -> p g t m", g=R_PASSES, t=PACK),
             wm_raw_scales[:].rearrange("p (g m t) -> p g t m", g=R_PASSES, t=PACK),
         )
+        gain_abs = held([P, R_PASSES * PACK], F32, "gain_abs", tag="fold_picked")
         nc.vector.scalar_tensor_tensor(gain_abs[:], gain_flat, -1.0, gain_flat, ALU.mult, ALU.max)
         nc.vector.tensor_scalar_max(gain_floor[:], gain_abs[:], TINY)
         nc.vector.reciprocal(gain_inv[:], gain_floor[:])
+
         gather_words(query_cols, query_words, query_list, 0)
+        round_we_second()
         quantize_we(1)
         evidence_rows(1, 0)
+        difference_pass(0, 0)
         evidence_rows(1, 1)
-        nc.scalar.copy(row_factor[:], gain_inv[:])
-
-        def match_rows(g, j):
-            for t in range(PACK):
-                col = g * PACK + t
-                a = psum_ab.tile([P, HALF], F32, name="a")
-                b = psum_ab.tile([P, HALF], F32, name="b")
-                for acc, cols, plane in ((b, query_cols, query_plane), (a, fold_cols, fold_plane)):
-                    nc.tensor.matmul_mx(
-                        out=acc[:],
-                        lhsT=wm_codes[:, 2 * P * col:2 * P * (col + 1)].bitcast(FP4X4),
-                        lhsT_scale=wm_plane[:, P * col:P * (col + 1)],
-                        rhs=cols[j][:].bitcast(FP8X4),
-                        rhs_scale=plane[:, j * HALF:(j + 1) * HALF],
-                        start=True, stop=True,
-                    )
-                b_out = ring.tile([P, HALF], F32, name="b_out")
-                rows = match[g][j][:, t, :]
-                nc.vector.tensor_copy(b_out[:], b[:])
-                nc.vector.tensor_tensor(rows, a[:], b_out[:], ALU.subtract)
-                nc.gpsimd.tensor_tensor(rows, rows, rows, ALU.mult)
-                nc.scalar.activation(rows, rows, ACT.Abs_reciprocal_sqrt,
-                                     bias=row_factor[:, col:col + 1], scale=row_factor[:, col:col + 1])
-
-        match_rows(0, 0)
         gather_words(query_cols, query_words, query_list, 1)
-        match_rows(1, 0)
-        match_rows(0, 1)
-        match_rows(1, 1)
+        difference_pass(1, 0)
+        difference_pass(0, 1)
+        difference_pass(1, 1)
+
+        wc_codes = held([P, R_PASSES, N], U32, "wc_codes", tag="blank1")
+        wc_plane = held([P, R_PASSES, N], U8, "wc_plane", tag="query_picked")
+        nc.sync.dma_start(
+            out=wc_codes[:].bitcast(I32),
+            in_=wc_words.rearrange("g p n i -> p g (n i)").bitcast(I32),
+        )
+        nc.gpsimd.memset(wc_plane[:].rearrange("p g n -> p (g n)").bitcast(I32), 0)
+        for d in range(4):
+            nc.sync.dma_start(
+                out=wc_plane[32 * d:32 * d + 4, :, :].bitcast(I32),
+                in_=wc_scales[:, 4 * d:4 * d + 4, :].rearrange("g q n -> q g n").bitcast(I32),
+            )
+
+        nc.scalar.copy(row_factor[:], gain_inv[:])
+        for j in range(HALVES):
+            for g in range(R_PASSES):
+                for t in range(PACK):
+                    factor = row_factor[:, g * PACK + t:g * PACK + t + 1]
+                    rows = match[g][j][:, t, :]
+                    nc.scalar.activation(rows, rows, ACT.Abs_reciprocal_sqrt, bias=factor, scale=factor)
+                for part in range(HALF // QUARTER):
+                    agree = match[g][j][:, :, part * QUARTER:(part + 1) * QUARTER]
+                    nc.scalar.activation(agree, agree, ACT.Square)
 
         for q in range(S // QUARTER):
             j, part = divmod(q, HALF // QUARTER)
             cols = slice(part * QUARTER, (part + 1) * QUARTER)
             h_codes = []
             h_plane = []
+            h_rounded = []
             for g in range(R_PASSES):
-                agree = ring.tile([P, PACK, QUARTER], F32, name="agree")
-                nc.scalar.activation(agree[:], match[g][j][:, :, cols], ACT.Square)
+                agree = match[g][j][:, :, cols]
                 h = ring.tile([P, QUARTER, PACK], BF16, name="h", align_bytes=64)
                 nc.vector.tensor_tensor(
                     h[:].rearrange("p (c i) t -> p c t i", i=4),
-                    agree[:].rearrange("p t (c i) -> p c t i", i=4),
+                    agree.rearrange("p t (c i) -> p c t i", i=4),
                     evidence[g][j][:, :, cols].rearrange("p t (c i) -> p c t i", i=4),
                     ALU.mult,
                 )
+                h_rounded.append(h)
+            for g in range(R_PASSES):
                 codes = held([P, QUARTER], U32, "h_codes%d%d" % (q, g))
                 plane = held([P, QUARTER], U8, "h_plane%d%d" % (q, g))
                 nc.vector.quantize_mx(out=codes[:].bitcast(FP8X4), scales=plane[:],
-                                      in_=h[:].rearrange("p j t -> p (j t)"))
+                                      in_=h_rounded[g][:].rearrange("p j t -> p (j t)"))
                 h_codes.append(codes)
                 h_plane.append(plane)
             for pair in range(N // (2 * P)):
@@ -258,6 +278,9 @@ def tile_list_fold_match_evidence_kernel(
                             start=(g == 0), stop=(g == R_PASSES - 1),
                         )
                 result = ring.tile([P, 2, QUARTER], F32, name="result")
-                nc.scalar.copy(result[:], acc[:])
+                if q == S // QUARTER - 1 and pair == 1:
+                    nc.vector.tensor_copy(result[:], acc[:])
+                else:
+                    nc.scalar.copy(result[:], acc[:])
                 rows = out[2 * P * pair:2 * P * (pair + 1), q * QUARTER:(q + 1) * QUARTER]
                 nc.sync.dma_start(out=rows.rearrange("(u p) j -> p u j", p=P), in_=result[:])

@@ -24,6 +24,7 @@ HALF = 512
 HALVES = S // HALF
 QUARTER = 256
 WE_COLS = 256
+BANKS = 8
 TINY = 2.0 ** -100
 
 
@@ -36,8 +37,13 @@ def tile_list_fold_match_evidence_kernel(
         lists = ctx.enter_context(tc.tile_pool(name="lists", bufs=1))
         keep = ctx.enter_context(tc.tile_pool(name="keep", bufs=1))
         ring = ctx.enter_context(tc.tile_pool(name="ring", bufs=4))
-        psum_ab = ctx.enter_context(tc.psum_pool(name="psum_ab", bufs=2))
-        psum_eo = ctx.enter_context(tc.psum_pool(name="psum_eo", bufs=4))
+        psum = ctx.enter_context(tc.psum_pool(name="psum", bufs=1))
+        taken = []
+
+        def next_bank(width):
+            bank = psum.tile([P, width], F32, name="sums", tag="bank%d" % (len(taken) % BANKS))
+            taken.append(bank)
+            return bank
 
         def held(shape, dtype, name, tag=""):
             return keep.tile(shape, dtype, name=name, tag=tag or name, align_bytes=64)
@@ -48,7 +54,6 @@ def tile_list_fold_match_evidence_kernel(
         fold_bytes = held([P, T], U8, "fold_bytes")
         query_bytes = held([P, T], U8, "query_bytes")
         fold_plane = held([P, S], U8, "fold_plane")
-        query_plane = held([P, S], U8, "query_plane")
         wm_raw = held([P, 2 * H], U8, "wm_raw")
         wm_raw_scales = held([P, H], U8, "wm_raw_scales")
         gain_cols = held([P, R_PASSES, PACK], F32, "gain_cols")
@@ -57,10 +62,9 @@ def tile_list_fold_match_evidence_kernel(
         nc.gpsimd.memset(fold_bytes[:].bitcast(I32), 0)
         for blank in blanks:
             nc.gpsimd.memset(blank[:], 0)
-        nc.gpsimd.memset(wm_raw_scales[:].bitcast(I32), 0)
         nc.vector.memset(query_bytes[:].bitcast(I32), 0)
         nc.vector.tensor_copy(fold_plane[:].bitcast(I32), blanks[0][:])
-        nc.vector.tensor_copy(query_plane[:].bitcast(I32), blanks[1][:])
+        nc.vector.tensor_copy(wm_raw_scales[:].bitcast(I32), blanks[1][:])
 
         we_first = held([P, PASS // WE_COLS, PACK, WE_COLS], F32, "we_first", tag="blank0")
         fold_words = held([P, T], U32, "fold_words", tag="blank1")
@@ -78,15 +82,15 @@ def tile_list_fold_match_evidence_kernel(
         nc.sync.dma_start(out=fold_bytes[0:P:8, :].bitcast(I32), in_=tab_scales[0].bitcast(I32))
         nc.sync.dma_start(query_list[:], offs2)
         nc.sync.dma_start(out=gain_cols[:], in_=gain.rearrange("(g p t) -> p g t", p=P, t=PACK))
-        nc.sync.dma_start(out=query_bytes[0:P:8, :].bitcast(I32), in_=tab2_scales[0].bitcast(I32))
         for part in range(PASS // WE_COLS):
             load_we(we_first[:, part], part * WE_COLS, WE_COLS)
         load_words(fold_words, tab_words)
-        for d in range(4):
-            nc.gpsimd.dma_start(
-                out=wm_raw_scales[32 * d:32 * d + 4, :].bitcast(I32),
-                in_=wm_scales[0, 4 * d:4 * d + 4, :].bitcast(I32),
-            )
+        for rows, scales in ((query_bytes, tab2_scales), (wm_raw_scales, wm_scales)):
+            for d in range(4):
+                nc.gpsimd.dma_start(
+                    out=rows[32 * d:32 * d + 4, :].bitcast(I32),
+                    in_=scales[0, 4 * d:4 * d + 4, :].bitcast(I32),
+                )
 
         gain_flat = gain_cols[:].rearrange("p g t -> p (g t)")
         row_factor = held([P, R_PASSES * PACK], F32, "row_factor")
@@ -94,36 +98,30 @@ def tile_list_fold_match_evidence_kernel(
         gain_inv = held([P, R_PASSES * PACK], F32, "gain_inv")
         nc.scalar.activation(row_factor[:], gain_flat, ACT.Sign)
 
-        def gather_scales(plane, rows, picks, name):
-            picked = held([P, S], U8, name)
-            nc.vector.tensor_copy(picked[:], rows[:].indirect(picks[:]))
-            for r in range(4):
-                nc.sync.dma_start(out=plane[r:P:32, :].bitcast(I32),
-                                  in_=picked[8 * r:P:32, :].bitcast(I32))
-
-        gather_scales(fold_plane, fold_bytes, fold_list, "fold_picked")
-        query_words = held([P, T], U32, "query_words", tag="fold_bytes")
-        load_words(query_words, tab2_words)
-        gather_scales(query_plane, query_bytes, query_list, "query_picked")
-        we_second = held([P, PACK, PASS], F32, "we_second", tag="query_bytes")
+        fold_picked = held([P, S], U8, "fold_picked")
+        nc.vector.tensor_copy(fold_picked[:], fold_bytes[:].indirect(fold_list[:]))
+        for r in range(4):
+            nc.sync.dma_start(out=fold_plane[r:P:32, :].bitcast(I32),
+                              in_=fold_picked[8 * r:P:32, :].bitcast(I32))
+        we_second = held([P, PACK, PASS], F32, "we_second", tag="fold_bytes")
         load_we(we_second[:], PASS, PASS)
+        query_words = held([P, T], U32, "query_words", tag="fold_picked")
+        load_words(query_words, tab2_words)
 
         we_bf = [held([P, PACK, P, PACK], BF16, "we_bf%d" % g) for g in range(R_PASSES)]
         we_codes = [held([P, PASS], U32, "we_codes%d" % g) for g in range(R_PASSES)]
         we_plane = [held([P, PASS], U8, "we_plane%d" % g) for g in range(R_PASSES)]
 
-        def round_we_first(part):
+        def round_we(g, part):
             width = WE_COLS // PACK
+            if g == 0:
+                raw = we_first[:, part]
+            else:
+                raw = we_second[:, :, part * WE_COLS:(part + 1) * WE_COLS]
             nc.scalar.activation(
-                we_bf[0][:, :, part * width:(part + 1) * width, :].rearrange("p t m i -> p m i t"),
-                we_first[:, part].rearrange("p i (m t) -> p m i t", t=PACK),
+                we_bf[g][:, :, part * width:(part + 1) * width, :].rearrange("p t m i -> p m i t"),
+                raw.rearrange("p i (m t) -> p m i t", t=PACK),
                 ACT.Copy,
-            )
-
-        def round_we_second():
-            nc.vector.tensor_copy(
-                we_bf[1][:].rearrange("p t m i -> p m i t"),
-                we_second[:].rearrange("p i (m t) -> p m i t", t=PACK),
             )
 
         def quantize_we(g):
@@ -144,7 +142,7 @@ def tile_list_fold_match_evidence_kernel(
 
         def evidence_rows(g, j):
             for t in range(PACK):
-                e = psum_eo.tile([P, HALF], F32, name="eo")
+                e = next_bank(HALF)
                 nc.tensor.matmul_mx(
                     out=e[:],
                     lhsT=we_codes[g][:, t * P:(t + 1) * P].bitcast(FP8X4),
@@ -158,67 +156,82 @@ def tile_list_fold_match_evidence_kernel(
                                      scale=row_factor[:, col:col + 1])
 
         for part in range(PASS // WE_COLS):
-            round_we_first(part)
+            round_we(0, part)
         wm_codes = held([P, 2 * H], U8, "wm_codes")
+        nc.vector.tensor_copy(
+            wm_codes[:].bitcast(U16).rearrange("p (g t m) -> p g t m", g=R_PASSES, t=PACK),
+            wm_raw[:].bitcast(U16).rearrange("p (g m t) -> p g t m", g=R_PASSES, t=PACK),
+        )
         quantize_we(0)
 
         fold_cols = [held([P, HALF], U32, "fold_cols%d" % j) for j in range(HALVES)]
         query_cols = [held([P, HALF], U32, "query_cols%d" % j) for j in range(HALVES)]
 
-        def difference_rows(g, j, t, b_out):
-            col = g * PACK + t
-            a = psum_ab.tile([P, HALF], F32, name="a")
-            b = psum_ab.tile([P, HALF], F32, name="b")
-            for acc, cols, plane in ((b, query_cols, query_plane), (a, fold_cols, fold_plane)):
-                nc.tensor.matmul_mx(
-                    out=acc[:],
-                    lhsT=wm_codes[:, 2 * P * col:2 * P * (col + 1)].bitcast(FP4X4),
-                    lhsT_scale=wm_plane[:, P * col:P * (col + 1)],
-                    rhs=cols[j][:].bitcast(FP8X4),
-                    rhs_scale=plane[:, j * HALF:(j + 1) * HALF],
-                    start=True, stop=True,
-                )
-            nc.vector.tensor_copy(b_out[:], b[:])
+        def subtract(g, j, t, a, b_out):
             nc.vector.tensor_tensor(match[g][j][:, t, :], a[:], b_out[:], ALU.subtract)
             if t % 2 == 1:
                 both = match[g][j][:, t - 1:t + 1, :]
-                nc.gpsimd.tensor_tensor(both, both, both, ALU.mult)
+                if (g, j, t) != last_rows:
+                    nc.gpsimd.tensor_tensor(both, both, both, ALU.mult)
+                else:
+                    nc.scalar.activation(both, both, ACT.Square)
 
-        def difference_pass(g, j, first=0):
-            for t in range(first, PACK):
-                difference_rows(g, j, t, ring.tile([P, HALF], F32, name="b_out"))
+        last_rows = (R_PASSES - 1, HALVES - 1, PACK - 1)
+
+        def difference_pass(g, j):
+            copied = []
+            for t in range(PACK):
+                col = g * PACK + t
+                b = next_bank(HALF)
+                a = next_bank(HALF)
+                for acc, cols, plane in ((b, query_cols, query_plane), (a, fold_cols, fold_plane)):
+                    nc.tensor.matmul_mx(
+                        out=acc[:],
+                        lhsT=wm_codes[:, 2 * P * col:2 * P * (col + 1)].bitcast(FP4X4),
+                        lhsT_scale=wm_plane[:, P * col:P * (col + 1)],
+                        rhs=cols[j][:].bitcast(FP8X4),
+                        rhs_scale=plane[:, j * HALF:(j + 1) * HALF],
+                        start=True, stop=True,
+                    )
+                if (g, j, t) == last_rows:
+                    b_out = held([P, HALF], F32, "b_last")
+                else:
+                    b_out = ring.tile([P, HALF], F32, name="b_out")
+                nc.vector.tensor_copy(b_out[:], b[:])
+                copied.append((a, b_out))
+                if t > 0:
+                    subtract(g, j, t - 1, *copied[t - 1])
+            subtract(g, j, PACK - 1, *copied[PACK - 1])
 
         gather_words(fold_cols, fold_words, fold_list, 0)
         evidence_rows(0, 0)
         gather_words(fold_cols, fold_words, fold_list, 1)
+        for part in range(PASS // WE_COLS):
+            round_we(1, part)
         evidence_rows(0, 1)
-        wm_plane = held([P, H], U8, "wm_plane", tag="we_bf0")
-        nc.vector.tensor_copy(
-            wm_codes[:].bitcast(U16).rearrange("p (g t m) -> p g t m", g=R_PASSES, t=PACK),
-            wm_raw[:].bitcast(U16).rearrange("p (g m t) -> p g t m", g=R_PASSES, t=PACK),
-        )
+        query_plane = held([P, S], U8, "query_plane", tag="blank1")
+        nc.vector.tensor_copy(query_plane[:], query_bytes[:].indirect(query_list[:]))
+        quantize_we(1)
+        wm_plane = held([P, H], U8, "wm_plane", tag="query_bytes")
         nc.vector.tensor_copy(
             wm_plane[:].rearrange("p (g t m) -> p g t m", g=R_PASSES, t=PACK),
             wm_raw_scales[:].rearrange("p (g m t) -> p g t m", g=R_PASSES, t=PACK),
         )
-        gain_abs = held([P, R_PASSES * PACK], F32, "gain_abs", tag="fold_picked")
+        gather_words(query_cols, query_words, query_list, 0)
+        gain_abs = held([P, R_PASSES * PACK], F32, "gain_abs", tag="wm_raw_scales")
         nc.vector.scalar_tensor_tensor(gain_abs[:], gain_flat, -1.0, gain_flat, ALU.mult, ALU.max)
         nc.vector.tensor_scalar_max(gain_floor[:], gain_abs[:], TINY)
         nc.vector.reciprocal(gain_inv[:], gain_floor[:])
-
-        gather_words(query_cols, query_words, query_list, 0)
-        round_we_second()
-        quantize_we(1)
-        evidence_rows(1, 0)
-        difference_pass(0, 0)
-        evidence_rows(1, 1)
         gather_words(query_cols, query_words, query_list, 1)
+        difference_pass(0, 0)
+        evidence_rows(1, 0)
+        evidence_rows(1, 1)
         difference_pass(1, 0)
         difference_pass(0, 1)
         difference_pass(1, 1)
 
-        wc_codes = held([P, R_PASSES, N], U32, "wc_codes", tag="blank1")
-        wc_plane = held([P, R_PASSES, N], U8, "wc_plane", tag="query_picked")
+        wc_codes = held([P, R_PASSES, N], U32, "wc_codes", tag="fold_picked")
+        wc_plane = held([P, R_PASSES, N], U8, "wc_plane", tag="we_bf1")
         nc.sync.dma_start(
             out=wc_codes[:].bitcast(I32),
             in_=wc_words.rearrange("g p n i -> p g (n i)").bitcast(I32),
@@ -241,6 +254,8 @@ def tile_list_fold_match_evidence_kernel(
                     agree = match[g][j][:, :, part * QUARTER:(part + 1) * QUARTER]
                     nc.scalar.activation(agree, agree, ACT.Square)
 
+        h_shape = [P, HALF // QUARTER, R_PASSES, QUARTER, PACK]
+        h_halves = [held(h_shape, BF16, "h_half0", tag="b_last"), held(h_shape, BF16, "h_half1")]
         for q in range(S // QUARTER):
             j, part = divmod(q, HALF // QUARTER)
             cols = slice(part * QUARTER, (part + 1) * QUARTER)
@@ -249,9 +264,9 @@ def tile_list_fold_match_evidence_kernel(
             h_rounded = []
             for g in range(R_PASSES):
                 agree = match[g][j][:, :, cols]
-                h = ring.tile([P, QUARTER, PACK], BF16, name="h", align_bytes=64)
+                h = h_halves[j][:, part, g]
                 nc.vector.tensor_tensor(
-                    h[:].rearrange("p (c i) t -> p c t i", i=4),
+                    h.rearrange("p (c i) t -> p c t i", i=4),
                     agree.rearrange("p t (c i) -> p c t i", i=4),
                     evidence[g][j][:, :, cols].rearrange("p t (c i) -> p c t i", i=4),
                     ALU.mult,
@@ -261,26 +276,26 @@ def tile_list_fold_match_evidence_kernel(
                 codes = held([P, QUARTER], U32, "h_codes%d%d" % (q, g))
                 plane = held([P, QUARTER], U8, "h_plane%d%d" % (q, g))
                 nc.vector.quantize_mx(out=codes[:].bitcast(FP8X4), scales=plane[:],
-                                      in_=h_rounded[g][:].rearrange("p j t -> p (j t)"))
+                                      in_=h_rounded[g].rearrange("p j t -> p (j t)"))
                 h_codes.append(codes)
                 h_plane.append(plane)
+            sums = [next_bank(QUARTER) for n in range(N // P)]
+            for g in range(R_PASSES):
+                for n in range(N // P):
+                    nc.tensor.matmul_mx(
+                        out=sums[n][:],
+                        lhsT=wc_codes[:, g, n * P:(n + 1) * P].bitcast(FP8X4),
+                        lhsT_scale=wc_plane[:, g, n * P:(n + 1) * P],
+                        rhs=h_codes[g][:].bitcast(FP8X4),
+                        rhs_scale=h_plane[g][:],
+                        start=(g == 0), stop=(g == R_PASSES - 1),
+                    )
             for pair in range(N // (2 * P)):
-                acc = psum_eo.tile([P, 2, QUARTER], F32, name="eo")
-                for u in range(2):
-                    n0 = (2 * pair + u) * P
-                    for g in range(R_PASSES):
-                        nc.tensor.matmul_mx(
-                            out=acc[:, u, :],
-                            lhsT=wc_codes[:, g, n0:n0 + P].bitcast(FP8X4),
-                            lhsT_scale=wc_plane[:, g, n0:n0 + P],
-                            rhs=h_codes[g][:].bitcast(FP8X4),
-                            rhs_scale=h_plane[g][:],
-                            start=(g == 0), stop=(g == R_PASSES - 1),
-                        )
                 result = ring.tile([P, 2, QUARTER], F32, name="result")
-                if q == S // QUARTER - 1 and pair == 1:
-                    nc.vector.tensor_copy(result[:], acc[:])
+                nc.scalar.copy(result[:, 0, :], sums[2 * pair][:])
+                if q == S // QUARTER - 1:
+                    nc.vector.tensor_copy(result[:, 1, :], sums[2 * pair + 1][:])
                 else:
-                    nc.scalar.copy(result[:], acc[:])
+                    nc.scalar.copy(result[:, 1, :], sums[2 * pair + 1][:])
                 rows = out[2 * P * pair:2 * P * (pair + 1), q * QUARTER:(q + 1) * QUARTER]
                 nc.sync.dma_start(out=rows.rearrange("(u p) j -> p u j", p=P), in_=result[:])

@@ -22,7 +22,7 @@ PASS = P * PACK
 R_PASSES = H // PASS
 HALF = 512
 HALVES = S // HALF
-QUARTER = 256
+PIECES = [(0, 0, 256), (0, 256, 256), (1, 0, 256), (1, 256, 128), (1, 384, 128)]
 WE_COLS = 256
 BANKS = 8
 TINY = 2.0 ** -100
@@ -112,15 +112,11 @@ def tile_list_fold_match_evidence_kernel(
         we_codes = [held([P, PASS], U32, "we_codes%d" % g) for g in range(R_PASSES)]
         we_plane = [held([P, PASS], U8, "we_plane%d" % g) for g in range(R_PASSES)]
 
-        def round_we(g, part):
+        def round_we_first(part):
             width = WE_COLS // PACK
-            if g == 0:
-                raw = we_first[:, part]
-            else:
-                raw = we_second[:, :, part * WE_COLS:(part + 1) * WE_COLS]
             nc.scalar.activation(
-                we_bf[g][:, :, part * width:(part + 1) * width, :].rearrange("p t m i -> p m i t"),
-                raw.rearrange("p i (m t) -> p m i t", t=PACK),
+                we_bf[0][:, :, part * width:(part + 1) * width, :].rearrange("p t m i -> p m i t"),
+                we_first[:, part].rearrange("p i (m t) -> p m i t", t=PACK),
                 ACT.Copy,
             )
 
@@ -156,7 +152,7 @@ def tile_list_fold_match_evidence_kernel(
                                      scale=row_factor[:, col:col + 1])
 
         for part in range(PASS // WE_COLS):
-            round_we(0, part)
+            round_we_first(part)
         wm_codes = held([P, 2 * H], U8, "wm_codes")
         nc.vector.tensor_copy(
             wm_codes[:].bitcast(U16).rearrange("p (g t m) -> p g t m", g=R_PASSES, t=PACK),
@@ -171,16 +167,17 @@ def tile_list_fold_match_evidence_kernel(
             nc.vector.tensor_tensor(match[g][j][:, t, :], a[:], b_out[:], ALU.subtract)
             if t % 2 == 1:
                 both = match[g][j][:, t - 1:t + 1, :]
-                if (g, j, t) != last_rows:
+                if (g, j, t) not in (second_pair, last_rows):
                     nc.gpsimd.tensor_tensor(both, both, both, ALU.mult)
                 else:
                     nc.scalar.activation(both, both, ACT.Square)
 
+        second_pair = (0, 0, PACK - 1)
         last_rows = (R_PASSES - 1, HALVES - 1, PACK - 1)
 
-        def difference_pass(g, j):
-            copied = []
-            for t in range(PACK):
+        def difference_rows(g, j, slots):
+            copied = {}
+            for t in slots:
                 col = g * PACK + t
                 b = next_bank(HALF)
                 a = next_bank(HALF)
@@ -198,21 +195,24 @@ def tile_list_fold_match_evidence_kernel(
                 else:
                     b_out = ring.tile([P, HALF], F32, name="b_out")
                 nc.vector.tensor_copy(b_out[:], b[:])
-                copied.append((a, b_out))
-                if t > 0:
+                copied[t] = (a, b_out)
+                if t > slots.start:
                     subtract(g, j, t - 1, *copied[t - 1])
-            subtract(g, j, PACK - 1, *copied[PACK - 1])
+            subtract(g, j, slots.stop - 1, *copied[slots.stop - 1])
 
         gather_words(fold_cols, fold_words, fold_list, 0)
         evidence_rows(0, 0)
         gather_words(fold_cols, fold_words, fold_list, 1)
-        for part in range(PASS // WE_COLS):
-            round_we(1, part)
         evidence_rows(0, 1)
         query_plane = held([P, S], U8, "query_plane", tag="blank1")
         nc.vector.tensor_copy(query_plane[:], query_bytes[:].indirect(query_list[:]))
+        nc.vector.tensor_copy(
+            we_bf[1][:].rearrange("p t m i -> p m i t"),
+            we_second[:].rearrange("p i (m t) -> p m i t", t=PACK),
+        )
         quantize_we(1)
-        wm_plane = held([P, H], U8, "wm_plane", tag="query_bytes")
+        evidence_rows(1, 0)
+        wm_plane = held([P, H], U8, "wm_plane", tag="we_bf1")
         nc.vector.tensor_copy(
             wm_plane[:].rearrange("p (g t m) -> p g t m", g=R_PASSES, t=PACK),
             wm_raw_scales[:].rearrange("p (g m t) -> p g t m", g=R_PASSES, t=PACK),
@@ -223,15 +223,15 @@ def tile_list_fold_match_evidence_kernel(
         nc.vector.tensor_scalar_max(gain_floor[:], gain_abs[:], TINY)
         nc.vector.reciprocal(gain_inv[:], gain_floor[:])
         gather_words(query_cols, query_words, query_list, 1)
-        difference_pass(0, 0)
-        evidence_rows(1, 0)
+        difference_rows(0, 0, range(0, 2))
         evidence_rows(1, 1)
-        difference_pass(1, 0)
-        difference_pass(0, 1)
-        difference_pass(1, 1)
+        difference_rows(0, 0, range(2, PACK))
+        difference_rows(1, 0, range(PACK))
+        difference_rows(0, 1, range(PACK))
+        difference_rows(1, 1, range(PACK))
 
         wc_codes = held([P, R_PASSES, N], U32, "wc_codes", tag="fold_picked")
-        wc_plane = held([P, R_PASSES, N], U8, "wc_plane", tag="we_bf1")
+        wc_plane = held([P, R_PASSES, N], U8, "wc_plane", tag="query_bytes")
         nc.sync.dma_start(
             out=wc_codes[:].bitcast(I32),
             in_=wc_words.rearrange("g p n i -> p g (n i)").bitcast(I32),
@@ -250,52 +250,52 @@ def tile_list_fold_match_evidence_kernel(
                     factor = row_factor[:, g * PACK + t:g * PACK + t + 1]
                     rows = match[g][j][:, t, :]
                     nc.scalar.activation(rows, rows, ACT.Abs_reciprocal_sqrt, bias=factor, scale=factor)
-                for part in range(HALF // QUARTER):
-                    agree = match[g][j][:, :, part * QUARTER:(part + 1) * QUARTER]
-                    nc.scalar.activation(agree, agree, ACT.Square)
+                for half, c0, width in PIECES:
+                    if half == j:
+                        agree = match[g][j][:, :, c0:c0 + width]
+                        nc.scalar.activation(agree, agree, ACT.Square)
 
-        h_shape = [P, HALF // QUARTER, R_PASSES, QUARTER, PACK]
+        h_shape = [P, R_PASSES, HALF, PACK]
         h_halves = [held(h_shape, BF16, "h_half0", tag="b_last"), held(h_shape, BF16, "h_half1")]
-        for q in range(S // QUARTER):
-            j, part = divmod(q, HALF // QUARTER)
-            cols = slice(part * QUARTER, (part + 1) * QUARTER)
-            h_codes = []
-            h_plane = []
-            h_rounded = []
+        n_tiles = N // P
+        for q, (j, c0, width) in enumerate(PIECES):
+            cols = slice(c0, c0 + width)
+            last = q == len(PIECES) - 1
             for g in range(R_PASSES):
-                agree = match[g][j][:, :, cols]
-                h = h_halves[j][:, part, g]
                 nc.vector.tensor_tensor(
-                    h.rearrange("p (c i) t -> p c t i", i=4),
-                    agree.rearrange("p t (c i) -> p c t i", i=4),
+                    h_halves[j][:, g, cols, :].rearrange("p (c i) t -> p c t i", i=4),
+                    match[g][j][:, :, cols].rearrange("p t (c i) -> p c t i", i=4),
                     evidence[g][j][:, :, cols].rearrange("p t (c i) -> p c t i", i=4),
                     ALU.mult,
                 )
-                h_rounded.append(h)
+            h_codes = [held([P, width], U32, "h_codes%d%d" % (q, g)) for g in range(R_PASSES)]
+            h_plane = [held([P, width], U8, "h_plane%d%d" % (q, g)) for g in range(R_PASSES)]
             for g in range(R_PASSES):
-                codes = held([P, QUARTER], U32, "h_codes%d%d" % (q, g))
-                plane = held([P, QUARTER], U8, "h_plane%d%d" % (q, g))
-                nc.vector.quantize_mx(out=codes[:].bitcast(FP8X4), scales=plane[:],
-                                      in_=h_rounded[g].rearrange("p j t -> p (j t)"))
-                h_codes.append(codes)
-                h_plane.append(plane)
-            sums = [next_bank(QUARTER) for n in range(N // P)]
-            for g in range(R_PASSES):
-                for n in range(N // P):
-                    nc.tensor.matmul_mx(
-                        out=sums[n][:],
-                        lhsT=wc_codes[:, g, n * P:(n + 1) * P].bitcast(FP8X4),
-                        lhsT_scale=wc_plane[:, g, n * P:(n + 1) * P],
-                        rhs=h_codes[g][:].bitcast(FP8X4),
-                        rhs_scale=h_plane[g][:],
-                        start=(g == 0), stop=(g == R_PASSES - 1),
-                    )
-            for pair in range(N // (2 * P)):
-                result = ring.tile([P, 2, QUARTER], F32, name="result")
-                nc.scalar.copy(result[:, 0, :], sums[2 * pair][:])
-                if q == S // QUARTER - 1:
-                    nc.vector.tensor_copy(result[:, 1, :], sums[2 * pair + 1][:])
+                nc.vector.quantize_mx(out=h_codes[g][:].bitcast(FP8X4), scales=h_plane[g][:],
+                                      in_=h_halves[j][:, g, cols, :].rearrange("p j t -> p (j t)"))
+
+            per_bank = 1 if last else HALF // width
+            banks = [next_bank(per_bank * width) for n in range(0, n_tiles, per_bank)]
+            for slot in range(per_bank):
+                for g in range(R_PASSES):
+                    for u, bank in enumerate(banks):
+                        n0 = (u * per_bank + slot) * P
+                        nc.tensor.matmul_mx(
+                            out=bank[:, slot * width:(slot + 1) * width],
+                            lhsT=wc_codes[:, g, n0:n0 + P].bitcast(FP8X4),
+                            lhsT_scale=wc_plane[:, g, n0:n0 + P],
+                            rhs=h_codes[g][:].bitcast(FP8X4),
+                            rhs_scale=h_plane[g][:],
+                            start=(g == 0), stop=(g == R_PASSES - 1),
+                        )
+            per_store = 2 if last else per_bank
+            for n in range(0, n_tiles, per_store):
+                result = ring.tile([P, per_store * width], F32, name="result")
+                if last:
+                    nc.scalar.copy(result[:, 0:width], banks[n][:])
+                    nc.vector.tensor_copy(result[:, width:2 * width], banks[n + 1][:])
                 else:
-                    nc.scalar.copy(result[:, 1, :], sums[2 * pair + 1][:])
-                rows = out[2 * P * pair:2 * P * (pair + 1), q * QUARTER:(q + 1) * QUARTER]
-                nc.sync.dma_start(out=rows.rearrange("(u p) j -> p u j", p=P), in_=result[:])
+                    nc.scalar.copy(result[:], banks[n // per_bank][:])
+                rows = out[n * P:(n + per_store) * P, j * HALF + c0:j * HALF + c0 + width]
+                nc.sync.dma_start(out=rows.rearrange("(u p) j -> p u j", p=P),
+                                  in_=result[:].rearrange("p (u j) -> p u j", u=per_store))

@@ -20,11 +20,17 @@ P = 128
 PACK = 4
 PASS = P * PACK
 R_PASSES = H // PASS
+QUAD = 32
+QUADS = P // QUAD
+BLOCK_ROWS = 8
+GROUP = 16
 HALF = 512
 HALVES = S // HALF
-PIECES = [(0, 0, 256), (0, 256, 256), (1, 0, 256), (1, 256, 128), (1, 384, 128)]
+QUARTER = 256
 WE_COLS = 256
+LINE = 4
 BANKS = 8
+RING = 4
 TINY = 2.0 ** -100
 
 
@@ -36,7 +42,7 @@ def tile_list_fold_match_evidence_kernel(
     with ExitStack() as ctx:
         lists = ctx.enter_context(tc.tile_pool(name="lists", bufs=1))
         keep = ctx.enter_context(tc.tile_pool(name="keep", bufs=1))
-        ring = ctx.enter_context(tc.tile_pool(name="ring", bufs=4))
+        ring = ctx.enter_context(tc.tile_pool(name="ring", bufs=RING))
         psum = ctx.enter_context(tc.psum_pool(name="psum", bufs=1))
         taken = []
 
@@ -45,17 +51,17 @@ def tile_list_fold_match_evidence_kernel(
             taken.append(bank)
             return bank
 
-        def held(shape, dtype, name, tag=""):
-            return keep.tile(shape, dtype, name=name, tag=tag or name, align_bytes=64)
+        def held(shape, dtype, name, after=""):
+            return keep.tile(shape, dtype, name=name, tag=after or name, align_bytes=64)
 
-        fold_list = lists.tile([P, S // 16], U16, name="fold_list")
-        query_list = lists.tile([P, S // 16], U16, name="query_list")
+        fold_list = lists.tile([P, S // GROUP], U16, name="fold_list")
+        query_list = lists.tile([P, S // GROUP], U16, name="query_list")
 
         fold_bytes = held([P, T], U8, "fold_bytes")
         query_bytes = held([P, T], U8, "query_bytes")
         fold_plane = held([P, S], U8, "fold_plane")
         wm_raw = held([P, 2 * H], U8, "wm_raw")
-        wm_raw_scales = held([P, H], U8, "wm_raw_scales")
+        wm_raw_plane = held([P, H], U8, "wm_raw_plane")
         gain_cols = held([P, R_PASSES, PACK], F32, "gain_cols")
         blanks = [held([P, S // 4], I32, "blank%d" % u) for u in range(2)]
 
@@ -64,14 +70,13 @@ def tile_list_fold_match_evidence_kernel(
             nc.gpsimd.memset(blank[:], 0)
         nc.vector.memset(query_bytes[:].bitcast(I32), 0)
         nc.vector.tensor_copy(fold_plane[:].bitcast(I32), blanks[0][:])
-        nc.vector.tensor_copy(wm_raw_scales[:].bitcast(I32), blanks[1][:])
+        nc.vector.tensor_copy(wm_raw_plane[:].bitcast(I32), blanks[1][:])
 
-        we_first = held([P, PASS // WE_COLS, PACK, WE_COLS], F32, "we_first", tag="blank0")
-        fold_words = held([P, T], U32, "fold_words", tag="blank1")
+        we_first = held([P, PASS // WE_COLS, PACK, WE_COLS], F32, "we_first", after="blank0")
+        fold_words = held([P, T], U32, "fold_words", after="blank1")
 
         def load_we(dst, c0, width):
-            cols = we[:, c0:c0 + width]
-            nc.sync.dma_start(out=dst, in_=cols.rearrange("(p i) w -> p i w", i=PACK))
+            nc.sync.dma_start(out=dst, in_=we[:, c0:c0 + width].rearrange("(p i) w -> p i w", i=PACK))
 
         def load_words(dst, words):
             nc.sync.dma_start(out=dst[:].bitcast(I32),
@@ -79,16 +84,16 @@ def tile_list_fold_match_evidence_kernel(
 
         nc.sync.dma_start(fold_list[:], offs)
         nc.sync.dma_start(out=wm_raw[:].bitcast(I32), in_=wm_words[0].bitcast(I32))
-        nc.sync.dma_start(out=fold_bytes[0:P:8, :].bitcast(I32), in_=tab_scales[0].bitcast(I32))
+        nc.sync.dma_start(out=fold_bytes[0:P:BLOCK_ROWS, :].bitcast(I32), in_=tab_scales[0].bitcast(I32))
         nc.sync.dma_start(query_list[:], offs2)
         nc.sync.dma_start(out=gain_cols[:], in_=gain.rearrange("(g p t) -> p g t", p=P, t=PACK))
         for part in range(PASS // WE_COLS):
             load_we(we_first[:, part], part * WE_COLS, WE_COLS)
         load_words(fold_words, tab_words)
-        for rows, scales in ((query_bytes, tab2_scales), (wm_raw_scales, wm_scales)):
-            for d in range(4):
+        for plane_rows, scales in ((query_bytes, tab2_scales), (wm_raw_plane, wm_scales)):
+            for d in range(QUADS):
                 nc.gpsimd.dma_start(
-                    out=rows[32 * d:32 * d + 4, :].bitcast(I32),
+                    out=plane_rows[QUAD * d:QUAD * d + 4, :].bitcast(I32),
                     in_=scales[0, 4 * d:4 * d + 4, :].bitcast(I32),
                 )
 
@@ -100,12 +105,12 @@ def tile_list_fold_match_evidence_kernel(
 
         fold_picked = held([P, S], U8, "fold_picked")
         nc.vector.tensor_copy(fold_picked[:], fold_bytes[:].indirect(fold_list[:]))
-        for r in range(4):
-            nc.sync.dma_start(out=fold_plane[r:P:32, :].bitcast(I32),
-                              in_=fold_picked[8 * r:P:32, :].bitcast(I32))
-        we_second = held([P, PACK, PASS], F32, "we_second", tag="fold_bytes")
+        for u in range(QUAD // BLOCK_ROWS):
+            nc.sync.dma_start(out=fold_plane[u:P:QUAD, :].bitcast(I32),
+                              in_=fold_picked[BLOCK_ROWS * u:P:QUAD, :].bitcast(I32))
+        we_second = held([P, PACK, PASS], F32, "we_second", after="fold_bytes")
         load_we(we_second[:], PASS, PASS)
-        query_words = held([P, T], U32, "query_words", tag="fold_picked")
+        query_words = held([P, T], U32, "query_words", after="fold_picked")
         load_words(query_words, tab2_words)
 
         we_bf = [held([P, PACK, P, PACK], BF16, "we_bf%d" % g) for g in range(R_PASSES)]
@@ -113,9 +118,9 @@ def tile_list_fold_match_evidence_kernel(
         we_plane = [held([P, PASS], U8, "we_plane%d" % g) for g in range(R_PASSES)]
 
         def round_we_first(part):
-            width = WE_COLS // PACK
+            per_t = WE_COLS // PACK
             nc.scalar.activation(
-                we_bf[0][:, :, part * width:(part + 1) * width, :].rearrange("p t m i -> p m i t"),
+                we_bf[0][:, :, part * per_t:(part + 1) * per_t, :].rearrange("p t m i -> p m i t"),
                 we_first[:, part].rearrange("p i (m t) -> p m i t", t=PACK),
                 ACT.Copy,
             )
@@ -128,15 +133,15 @@ def tile_list_fold_match_evidence_kernel(
             )
 
         def gather_words(dst, words, picks, j):
-            per = HALF // 16
-            nc.vector.tensor_copy(dst[j][:], words[:].indirect(picks[:, j * per:(j + 1) * per]))
+            per_half = HALF // GROUP
+            nc.vector.tensor_copy(dst[j][:], words[:].indirect(picks[:, j * per_half:(j + 1) * per_half]))
 
         evidence = [[held([P, PACK, HALF], F32, "evidence%d%d" % (g, j)) for j in range(HALVES)]
                     for g in range(R_PASSES)]
         match = [[held([P, PACK, HALF], F32, "match%d%d" % (g, j)) for j in range(HALVES)]
                  for g in range(R_PASSES)]
 
-        def evidence_rows(g, j):
+        def evidence_tiles(g, j):
             for t in range(PACK):
                 e = next_bank(HALF)
                 nc.tensor.matmul_mx(
@@ -147,9 +152,9 @@ def tile_list_fold_match_evidence_kernel(
                     rhs_scale=fold_plane[:, j * HALF:(j + 1) * HALF],
                     start=True, stop=True,
                 )
-                col = g * PACK + t
+                tile_no = g * PACK + t
                 nc.scalar.activation(evidence[g][j][:, t, :], e[:], ACT.Tanh,
-                                     scale=row_factor[:, col:col + 1])
+                                     scale=row_factor[:, tile_no:tile_no + 1])
 
         for part in range(PASS // WE_COLS):
             round_we_first(part)
@@ -163,83 +168,83 @@ def tile_list_fold_match_evidence_kernel(
         fold_cols = [held([P, HALF], U32, "fold_cols%d" % j) for j in range(HALVES)]
         query_cols = [held([P, HALF], U32, "query_cols%d" % j) for j in range(HALVES)]
 
+        second_pair = (0, 0, PACK - 1)
+        last_tile = (R_PASSES - 1, HALVES - 1, PACK - 1)
+
         def subtract(g, j, t, a, b_out):
             nc.vector.tensor_tensor(match[g][j][:, t, :], a[:], b_out[:], ALU.subtract)
             if t % 2 == 1:
-                both = match[g][j][:, t - 1:t + 1, :]
-                if (g, j, t) not in (second_pair, last_rows):
-                    nc.gpsimd.tensor_tensor(both, both, both, ALU.mult)
+                pair = match[g][j][:, t - 1:t + 1, :]
+                if (g, j, t) in (second_pair, last_tile):
+                    nc.scalar.activation(pair, pair, ACT.Square)
                 else:
-                    nc.scalar.activation(both, both, ACT.Square)
+                    nc.gpsimd.tensor_tensor(pair, pair, pair, ALU.mult)
 
-        second_pair = (0, 0, PACK - 1)
-        last_rows = (R_PASSES - 1, HALVES - 1, PACK - 1)
-
-        def difference_rows(g, j, slots):
+        def difference_tiles(g, j, t_range):
             copied = {}
-            for t in slots:
-                col = g * PACK + t
+            for t in t_range:
+                tile_no = g * PACK + t
                 b = next_bank(HALF)
                 a = next_bank(HALF)
-                for acc, cols, plane in ((b, query_cols, query_plane), (a, fold_cols, fold_plane)):
+                for acc, picked, plane in ((b, query_cols, query_plane), (a, fold_cols, fold_plane)):
                     nc.tensor.matmul_mx(
                         out=acc[:],
-                        lhsT=wm_codes[:, 2 * P * col:2 * P * (col + 1)].bitcast(FP4X4),
-                        lhsT_scale=wm_plane[:, P * col:P * (col + 1)],
-                        rhs=cols[j][:].bitcast(FP8X4),
+                        lhsT=wm_codes[:, 2 * P * tile_no:2 * P * (tile_no + 1)].bitcast(FP4X4),
+                        lhsT_scale=wm_plane[:, P * tile_no:P * (tile_no + 1)],
+                        rhs=picked[j][:].bitcast(FP8X4),
                         rhs_scale=plane[:, j * HALF:(j + 1) * HALF],
                         start=True, stop=True,
                     )
-                if (g, j, t) == last_rows:
+                if (g, j, t) == last_tile:
                     b_out = held([P, HALF], F32, "b_last")
                 else:
                     b_out = ring.tile([P, HALF], F32, name="b_out")
                 nc.vector.tensor_copy(b_out[:], b[:])
                 copied[t] = (a, b_out)
-                if t > slots.start:
+                if t > t_range.start:
                     subtract(g, j, t - 1, *copied[t - 1])
-            subtract(g, j, slots.stop - 1, *copied[slots.stop - 1])
+            subtract(g, j, t_range.stop - 1, *copied[t_range.stop - 1])
 
         gather_words(fold_cols, fold_words, fold_list, 0)
-        evidence_rows(0, 0)
+        evidence_tiles(0, 0)
         gather_words(fold_cols, fold_words, fold_list, 1)
-        evidence_rows(0, 1)
-        query_plane = held([P, S], U8, "query_plane", tag="blank1")
+        evidence_tiles(0, 1)
+        query_plane = held([P, S], U8, "query_plane", after="blank1")
         nc.vector.tensor_copy(query_plane[:], query_bytes[:].indirect(query_list[:]))
         nc.vector.tensor_copy(
             we_bf[1][:].rearrange("p t m i -> p m i t"),
             we_second[:].rearrange("p i (m t) -> p m i t", t=PACK),
         )
         quantize_we(1)
-        evidence_rows(1, 0)
-        wm_plane = held([P, H], U8, "wm_plane", tag="we_bf1")
+        evidence_tiles(1, 0)
+        wm_plane = held([P, H], U8, "wm_plane", after="we_bf1")
         nc.vector.tensor_copy(
             wm_plane[:].rearrange("p (g t m) -> p g t m", g=R_PASSES, t=PACK),
-            wm_raw_scales[:].rearrange("p (g m t) -> p g t m", g=R_PASSES, t=PACK),
+            wm_raw_plane[:].rearrange("p (g m t) -> p g t m", g=R_PASSES, t=PACK),
         )
         gather_words(query_cols, query_words, query_list, 0)
-        gain_abs = held([P, R_PASSES * PACK], F32, "gain_abs", tag="wm_raw_scales")
+        gain_abs = held([P, R_PASSES * PACK], F32, "gain_abs")
         nc.vector.scalar_tensor_tensor(gain_abs[:], gain_flat, -1.0, gain_flat, ALU.mult, ALU.max)
         nc.vector.tensor_scalar_max(gain_floor[:], gain_abs[:], TINY)
         nc.vector.reciprocal(gain_inv[:], gain_floor[:])
         gather_words(query_cols, query_words, query_list, 1)
-        difference_rows(0, 0, range(0, 2))
-        evidence_rows(1, 1)
-        difference_rows(0, 0, range(2, PACK))
-        difference_rows(1, 0, range(PACK))
-        difference_rows(0, 1, range(PACK))
-        difference_rows(1, 1, range(PACK))
+        difference_tiles(0, 0, range(0, 2))
+        evidence_tiles(1, 1)
+        difference_tiles(0, 0, range(2, PACK))
+        difference_tiles(1, 0, range(PACK))
+        difference_tiles(0, 1, range(PACK))
+        difference_tiles(1, 1, range(PACK))
 
-        wc_codes = held([P, R_PASSES, N], U32, "wc_codes", tag="fold_picked")
-        wc_plane = held([P, R_PASSES, N], U8, "wc_plane", tag="query_bytes")
+        wc_codes = held([P, R_PASSES, N], U32, "wc_codes", after="fold_picked")
+        wc_plane = held([P, R_PASSES, N], U8, "wc_plane", after="query_bytes")
         nc.sync.dma_start(
             out=wc_codes[:].bitcast(I32),
             in_=wc_words.rearrange("g p n i -> p g (n i)").bitcast(I32),
         )
         nc.gpsimd.memset(wc_plane[:].rearrange("p g n -> p (g n)").bitcast(I32), 0)
-        for d in range(4):
+        for d in range(QUADS):
             nc.sync.dma_start(
-                out=wc_plane[32 * d:32 * d + 4, :, :].bitcast(I32),
+                out=wc_plane[QUAD * d:QUAD * d + 4, :, :].bitcast(I32),
                 in_=wc_scales[:, 4 * d:4 * d + 4, :].rearrange("g q n -> q g n").bitcast(I32),
             )
 
@@ -247,55 +252,55 @@ def tile_list_fold_match_evidence_kernel(
         for j in range(HALVES):
             for g in range(R_PASSES):
                 for t in range(PACK):
-                    factor = row_factor[:, g * PACK + t:g * PACK + t + 1]
-                    rows = match[g][j][:, t, :]
-                    nc.scalar.activation(rows, rows, ACT.Abs_reciprocal_sqrt, bias=factor, scale=factor)
-                for half, c0, width in PIECES:
-                    if half == j:
-                        agree = match[g][j][:, :, c0:c0 + width]
-                        nc.scalar.activation(agree, agree, ACT.Square)
+                    inv = row_factor[:, g * PACK + t:g * PACK + t + 1]
+                    squares = match[g][j][:, t, :]
+                    nc.scalar.activation(squares, squares, ACT.Abs_reciprocal_sqrt, bias=inv, scale=inv)
+                for c0 in range(0, HALF, QUARTER):
+                    roots = match[g][j][:, :, c0:c0 + QUARTER]
+                    nc.scalar.activation(roots, roots, ACT.Square)
 
         h_shape = [P, R_PASSES, HALF, PACK]
-        h_halves = [held(h_shape, BF16, "h_half0", tag="b_last"), held(h_shape, BF16, "h_half1")]
+        h_halves = [held(h_shape, BF16, "h_half0", after="b_last"), held(h_shape, BF16, "h_half1")]
         n_tiles = N // P
-        for q, (j, c0, width) in enumerate(PIECES):
-            cols = slice(c0, c0 + width)
-            last = q == len(PIECES) - 1
+        for q in range(S // QUARTER):
+            j, c0 = divmod(q * QUARTER, HALF)
+            cols = slice(c0, c0 + QUARTER)
+            last = q == S // QUARTER - 1
             for g in range(R_PASSES):
                 nc.vector.tensor_tensor(
-                    h_halves[j][:, g, cols, :].rearrange("p (c i) t -> p c t i", i=4),
-                    match[g][j][:, :, cols].rearrange("p t (c i) -> p c t i", i=4),
-                    evidence[g][j][:, :, cols].rearrange("p t (c i) -> p c t i", i=4),
+                    h_halves[j][:, g, cols, :].rearrange("p (c i) t -> p c t i", i=LINE),
+                    match[g][j][:, :, cols].rearrange("p t (c i) -> p c t i", i=LINE),
+                    evidence[g][j][:, :, cols].rearrange("p t (c i) -> p c t i", i=LINE),
                     ALU.mult,
                 )
-            h_codes = [held([P, width], U32, "h_codes%d%d" % (q, g)) for g in range(R_PASSES)]
-            h_plane = [held([P, width], U8, "h_plane%d%d" % (q, g)) for g in range(R_PASSES)]
+            h_codes = [held([P, QUARTER], U32, "h_codes%d%d" % (q, g)) for g in range(R_PASSES)]
+            h_plane = [held([P, QUARTER], U8, "h_plane%d%d" % (q, g)) for g in range(R_PASSES)]
             for g in range(R_PASSES):
                 nc.vector.quantize_mx(out=h_codes[g][:].bitcast(FP8X4), scales=h_plane[g][:],
                                       in_=h_halves[j][:, g, cols, :].rearrange("p j t -> p (j t)"))
 
-            per_bank = 1 if last else HALF // width
-            banks = [next_bank(per_bank * width) for n in range(0, n_tiles, per_bank)]
-            for slot in range(per_bank):
+            per_bank = 1 if last else HALF // QUARTER
+            banks = [next_bank(per_bank * QUARTER) for n in range(0, n_tiles, per_bank)]
+            for place in range(per_bank):
                 for g in range(R_PASSES):
                     for u, bank in enumerate(banks):
-                        n0 = (u * per_bank + slot) * P
+                        n0 = (u * per_bank + place) * P
                         nc.tensor.matmul_mx(
-                            out=bank[:, slot * width:(slot + 1) * width],
+                            out=bank[:, place * QUARTER:(place + 1) * QUARTER],
                             lhsT=wc_codes[:, g, n0:n0 + P].bitcast(FP8X4),
                             lhsT_scale=wc_plane[:, g, n0:n0 + P],
                             rhs=h_codes[g][:].bitcast(FP8X4),
                             rhs_scale=h_plane[g][:],
                             start=(g == 0), stop=(g == R_PASSES - 1),
                         )
-            per_store = 2 if last else per_bank
-            for n in range(0, n_tiles, per_store):
-                result = ring.tile([P, per_store * width], F32, name="result")
+            for n in range(0, n_tiles, 2):
+                result = ring.tile([P, 2 * QUARTER], F32, name="result")
                 if last:
-                    nc.scalar.copy(result[:, 0:width], banks[n][:])
-                    nc.vector.tensor_copy(result[:, width:2 * width], banks[n + 1][:])
+                    nc.scalar.copy(result[:, 0:QUARTER], banks[n][:])
+                    nc.vector.tensor_copy(result[:, QUARTER:2 * QUARTER], banks[n + 1][:])
                 else:
                     nc.scalar.copy(result[:], banks[n // per_bank][:])
-                rows = out[n * P:(n + per_store) * P, j * HALF + c0:j * HALF + c0 + width]
-                nc.sync.dma_start(out=rows.rearrange("(u p) j -> p u j", p=P),
-                                  in_=result[:].rearrange("p (u j) -> p u j", u=per_store))
+                dst = out[n * P:(n + 2) * P, q * QUARTER:(q + 1) * QUARTER]
+                queue = nc.scalar if last and n > 0 else nc.sync
+                queue.dma_start(out=dst.rearrange("(u p) j -> p u j", p=P),
+                                in_=result[:].rearrange("p (u j) -> p u j", u=2))

@@ -31,6 +31,7 @@ WE_COLS = 256
 LINE = 4
 BANKS = 8
 RING = 4
+SCALAR_B_PAIR = 2
 TINY = 2.0 ** -100
 
 
@@ -63,17 +64,13 @@ def tile_list_fold_match_evidence_kernel(
         wm_raw = held([P, 2 * H], U8, "wm_raw")
         wm_raw_plane = held([P, H], U8, "wm_raw_plane")
         gain_cols = held([P, R_PASSES, PACK], F32, "gain_cols")
-        blanks = [held([P, S // 4], I32, "blank%d" % u) for u in range(2)]
 
-        nc.gpsimd.memset(fold_bytes[:].bitcast(I32), 0)
-        for blank in blanks:
-            nc.gpsimd.memset(blank[:], 0)
         nc.vector.memset(query_bytes[:].bitcast(I32), 0)
-        nc.vector.tensor_copy(fold_plane[:].bitcast(I32), blanks[0][:])
-        nc.vector.tensor_copy(wm_raw_plane[:].bitcast(I32), blanks[1][:])
+        nc.vector.memset(wm_raw_plane[:].bitcast(I32), 0)
+        nc.vector.memset(fold_plane[:].bitcast(I32), 0)
 
-        we_first = held([P, PASS // WE_COLS, PACK, WE_COLS], F32, "we_first", after="blank0")
-        fold_words = held([P, T], U32, "fold_words", after="blank1")
+        we_first = held([P, PASS // WE_COLS, PACK, WE_COLS], F32, "we_first")
+        fold_words = held([P, T], U32, "fold_words")
 
         def load_we(dst, c0, width):
             nc.sync.dma_start(out=dst, in_=we[:, c0:c0 + width].rearrange("(p i) w -> p i w", i=PACK))
@@ -83,13 +80,16 @@ def tile_list_fold_match_evidence_kernel(
                               in_=words[0].rearrange("p t i -> p (t i)").bitcast(I32))
 
         nc.sync.dma_start(fold_list[:], offs)
-        nc.sync.dma_start(out=wm_raw[:].bitcast(I32), in_=wm_words[0].bitcast(I32))
-        nc.sync.dma_start(out=fold_bytes[0:P:BLOCK_ROWS, :].bitcast(I32), in_=tab_scales[0].bitcast(I32))
-        nc.sync.dma_start(query_list[:], offs2)
-        nc.sync.dma_start(out=gain_cols[:], in_=gain.rearrange("(g p t) -> p g t", p=P, t=PACK))
+        nc.sync.dma_start(
+            out=fold_bytes[:].bitcast(I32),
+            in_=tab_scales[0].bitcast(I32).unsqueeze(1).to_broadcast([P // BLOCK_ROWS, BLOCK_ROWS, T // 4]),
+        )
+        load_words(fold_words, tab_words)
         for part in range(PASS // WE_COLS):
             load_we(we_first[:, part], part * WE_COLS, WE_COLS)
-        load_words(fold_words, tab_words)
+        nc.sync.dma_start(query_list[:], offs2)
+        nc.sync.dma_start(out=gain_cols[:], in_=gain.rearrange("(g p t) -> p g t", p=P, t=PACK))
+        nc.sync.dma_start(out=wm_raw[:].bitcast(I32), in_=wm_words[0].bitcast(I32))
         for plane_rows, scales in ((query_bytes, tab2_scales), (wm_raw_plane, wm_scales)):
             for d in range(QUADS):
                 nc.gpsimd.dma_start(
@@ -141,82 +141,44 @@ def tile_list_fold_match_evidence_kernel(
         match = [[held([P, PACK, HALF], F32, "match%d%d" % (g, j)) for j in range(HALVES)]
                  for g in range(R_PASSES)]
 
-        def evidence_tiles(g, j):
-            for t in range(PACK):
-                e = next_bank(HALF)
-                nc.tensor.matmul_mx(
-                    out=e[:],
-                    lhsT=we_codes[g][:, t * P:(t + 1) * P].bitcast(FP8X4),
-                    lhsT_scale=we_plane[g][:, t * P:(t + 1) * P],
-                    rhs=fold_cols[j][:].bitcast(FP8X4),
-                    rhs_scale=fold_plane[:, j * HALF:(j + 1) * HALF],
-                    start=True, stop=True,
-                )
-                tile_no = g * PACK + t
-                nc.scalar.activation(evidence[g][j][:, t, :], e[:], ACT.Tanh,
-                                     scale=row_factor[:, tile_no:tile_no + 1])
-
-        for part in range(PASS // WE_COLS):
-            round_we_first(part)
-        wm_codes = held([P, 2 * H], U8, "wm_codes")
-        nc.vector.tensor_copy(
-            wm_codes[:].bitcast(U16).rearrange("p (g t m) -> p g t m", g=R_PASSES, t=PACK),
-            wm_raw[:].bitcast(U16).rearrange("p (g m t) -> p g t m", g=R_PASSES, t=PACK),
-        )
-        quantize_we(0)
+        def evidence_tile(g, j, t):
+            e = next_bank(HALF)
+            nc.tensor.matmul_mx(
+                out=e[:],
+                lhsT=we_codes[g][:, t * P:(t + 1) * P].bitcast(FP8X4),
+                lhsT_scale=we_plane[g][:, t * P:(t + 1) * P],
+                rhs=fold_cols[j][:].bitcast(FP8X4),
+                rhs_scale=fold_plane[:, j * HALF:(j + 1) * HALF],
+                start=True, stop=True,
+            )
+            tile_no = g * PACK + t
+            nc.scalar.activation(evidence[g][j][:, t, :], e[:], ACT.Tanh,
+                                 scale=row_factor[:, tile_no:tile_no + 1])
 
         fold_cols = [held([P, HALF], U32, "fold_cols%d" % j) for j in range(HALVES)]
         query_cols = [held([P, HALF], U32, "query_cols%d" % j) for j in range(HALVES)]
-
-        second_pair = (0, 0, PACK - 1)
-        last_tile = (R_PASSES - 1, HALVES - 1, PACK - 1)
-
-        def subtract(g, j, t, a, b_out):
-            nc.vector.tensor_tensor(match[g][j][:, t, :], a[:], b_out[:], ALU.subtract)
-            if t % 2 == 1:
-                pair = match[g][j][:, t - 1:t + 1, :]
-                if (g, j, t) in (second_pair, last_tile):
-                    nc.scalar.activation(pair, pair, ACT.Square)
-                else:
-                    nc.gpsimd.tensor_tensor(pair, pair, pair, ALU.mult)
-
-        def difference_tiles(g, j, t_range):
-            copied = {}
-            for t in t_range:
-                tile_no = g * PACK + t
-                b = next_bank(HALF)
-                a = next_bank(HALF)
-                for acc, picked, plane in ((b, query_cols, query_plane), (a, fold_cols, fold_plane)):
-                    nc.tensor.matmul_mx(
-                        out=acc[:],
-                        lhsT=wm_codes[:, 2 * P * tile_no:2 * P * (tile_no + 1)].bitcast(FP4X4),
-                        lhsT_scale=wm_plane[:, P * tile_no:P * (tile_no + 1)],
-                        rhs=picked[j][:].bitcast(FP8X4),
-                        rhs_scale=plane[:, j * HALF:(j + 1) * HALF],
-                        start=True, stop=True,
-                    )
-                if (g, j, t) == last_tile:
-                    b_out = held([P, HALF], F32, "b_last")
-                else:
-                    b_out = ring.tile([P, HALF], F32, name="b_out")
-                nc.vector.tensor_copy(b_out[:], b[:])
-                copied[t] = (a, b_out)
-                if t > t_range.start:
-                    subtract(g, j, t - 1, *copied[t - 1])
-            subtract(g, j, t_range.stop - 1, *copied[t_range.stop - 1])
-
-        gather_words(fold_cols, fold_words, fold_list, 0)
-        evidence_tiles(0, 0)
-        gather_words(fold_cols, fold_words, fold_list, 1)
-        evidence_tiles(0, 1)
-        query_plane = held([P, S], U8, "query_plane", after="blank1")
+        for j in range(HALVES):
+            gather_words(fold_cols, fold_words, fold_list, j)
+        for part in range(PASS // WE_COLS):
+            round_we_first(part)
+        quantize_we(0)
+        for j in range(HALVES):
+            for t in range(PACK):
+                evidence_tile(0, j, t)
+        query_plane = held([P, S], U8, "query_plane", after="fold_words")
         nc.vector.tensor_copy(query_plane[:], query_bytes[:].indirect(query_list[:]))
         nc.vector.tensor_copy(
             we_bf[1][:].rearrange("p t m i -> p m i t"),
             we_second[:].rearrange("p i (m t) -> p m i t", t=PACK),
         )
+        wm_codes = held([P, 2 * H], U8, "wm_codes", after="we_first")
+        nc.vector.tensor_copy(
+            wm_codes[:].bitcast(U16).rearrange("p (g t m) -> p g t m", g=R_PASSES, t=PACK),
+            wm_raw[:].bitcast(U16).rearrange("p (g m t) -> p g t m", g=R_PASSES, t=PACK),
+        )
         quantize_we(1)
-        evidence_tiles(1, 0)
+        for t in range(PACK):
+            evidence_tile(1, 0, t)
         wm_plane = held([P, H], U8, "wm_plane", after="we_bf1")
         nc.vector.tensor_copy(
             wm_plane[:].rearrange("p (g t m) -> p g t m", g=R_PASSES, t=PACK),
@@ -224,16 +186,81 @@ def tile_list_fold_match_evidence_kernel(
         )
         gather_words(query_cols, query_words, query_list, 0)
         gain_abs = held([P, R_PASSES * PACK], F32, "gain_abs")
-        nc.vector.scalar_tensor_tensor(gain_abs[:], gain_flat, -1.0, gain_flat, ALU.mult, ALU.max)
+        nc.scalar.activation(gain_abs[:], gain_flat, ACT.Abs)
         nc.vector.tensor_scalar_max(gain_floor[:], gain_abs[:], TINY)
-        nc.vector.reciprocal(gain_inv[:], gain_floor[:])
         gather_words(query_cols, query_words, query_list, 1)
-        difference_tiles(0, 0, range(0, 2))
-        evidence_tiles(1, 1)
-        difference_tiles(0, 0, range(2, PACK))
-        difference_tiles(1, 0, range(PACK))
-        difference_tiles(0, 1, range(PACK))
-        difference_tiles(1, 1, range(PACK))
+        nc.vector.reciprocal(gain_inv[:], gain_floor[:])
+
+        pairs = [(j, g, t) for j in range(HALVES) for g in range(R_PASSES) for t in range(0, PACK, 2)]
+        b_last = held([P, HALF], F32, "b_last")
+
+        def wm_product(g, t, picked, plane, j):
+            acc = next_bank(HALF)
+            tile_no = g * PACK + t
+            nc.tensor.matmul_mx(
+                out=acc[:],
+                lhsT=wm_codes[:, 2 * P * tile_no:2 * P * (tile_no + 1)].bitcast(FP4X4),
+                lhsT_scale=wm_plane[:, P * tile_no:P * (tile_no + 1)],
+                rhs=picked[j][:].bitcast(FP8X4),
+                rhs_scale=plane[:, j * HALF:(j + 1) * HALF],
+                start=True, stop=True,
+            )
+            return acc
+
+        def b_place(n, u):
+            j, g, t = pairs[n]
+            return b_last[:] if (n, u) == (len(pairs) - 1, 1) else match[g][j][:, t + u, :]
+
+        def copy_b(n, u):
+            j, g, t = pairs[n]
+            b = wm_product(g, t + u, query_cols, query_plane, j)
+            if n == SCALAR_B_PAIR:
+                nc.scalar.copy(b_place(n, u), b[:])
+            else:
+                nc.vector.tensor_copy(b_place(n, u), b[:])
+
+        def subtract(n, u):
+            j, g, t = pairs[n]
+            a = wm_product(g, t + u, fold_cols, fold_plane, j)
+            nc.vector.tensor_tensor(match[g][j][:, t + u, :], a[:], b_place(n, u), ALU.subtract)
+
+        def square(n):
+            j, g, t = pairs[n]
+            pair = match[g][j][:, t:t + 2, :]
+            if n == len(pairs) - 1:
+                nc.scalar.activation(pair, pair, ACT.Square)
+            else:
+                nc.gpsimd.tensor_tensor(pair, pair, pair, ALU.mult)
+
+        def inverse_roots(n):
+            j, g, t = pairs[n]
+            for u in range(2):
+                inv = row_factor[:, g * PACK + t + u:g * PACK + t + u + 1]
+                squares = match[g][j][:, t + u, :]
+                nc.scalar.activation(squares, squares, ACT.Abs_reciprocal_sqrt, bias=inv, scale=inv)
+
+        def square_roots(roots):
+            nc.scalar.activation(roots, roots, ACT.Square)
+
+        for u in range(2):
+            copy_b(0, u)
+        for u in range(2):
+            evidence_tile(1, 1, u)
+            subtract(0, u)
+        square(0)
+        for u in range(2):
+            evidence_tile(1, 1, 2 + u)
+            copy_b(1, u)
+        for n in range(1, len(pairs)):
+            if n + 1 == SCALAR_B_PAIR:
+                for u in range(2):
+                    copy_b(n + 1, u)
+            if n not in (1, SCALAR_B_PAIR):
+                for u in range(2):
+                    copy_b(n, u)
+            for u in range(2):
+                subtract(n, u)
+            square(n)
 
         wc_codes = held([P, R_PASSES, N], U32, "wc_codes", after="fold_picked")
         wc_plane = held([P, R_PASSES, N], U8, "wc_plane", after="query_bytes")
@@ -249,15 +276,14 @@ def tile_list_fold_match_evidence_kernel(
             )
 
         nc.scalar.copy(row_factor[:], gain_inv[:])
-        for j in range(HALVES):
-            for g in range(R_PASSES):
-                for t in range(PACK):
-                    inv = row_factor[:, g * PACK + t:g * PACK + t + 1]
-                    squares = match[g][j][:, t, :]
-                    nc.scalar.activation(squares, squares, ACT.Abs_reciprocal_sqrt, bias=inv, scale=inv)
-                for c0 in range(0, HALF, QUARTER):
-                    roots = match[g][j][:, :, c0:c0 + QUARTER]
-                    nc.scalar.activation(roots, roots, ACT.Square)
+        for n in range(len(pairs) - 2):
+            j, g, t = pairs[n]
+            inverse_roots(n)
+            square_roots(match[g][j][:, t:t + 2, :])
+        for n in range(len(pairs) - 2, len(pairs)):
+            inverse_roots(n)
+        for c0 in range(0, HALF, QUARTER):
+            square_roots(match[R_PASSES - 1][HALVES - 1][:, :, c0:c0 + QUARTER])
 
         h_shape = [P, R_PASSES, HALF, PACK]
         h_halves = [held(h_shape, BF16, "h_half0", after="b_last"), held(h_shape, BF16, "h_half1")]

@@ -28,10 +28,9 @@ HALF = 512
 HALVES = S // HALF
 QUARTER = 256
 WE_COLS = 256
+STEPS = (HALF, QUARTER, QUARTER)
 LINE = 4
 BANKS = 8
-RING = 4
-SCALAR_B_PAIR = 2
 TINY = 2.0 ** -100
 
 
@@ -43,7 +42,6 @@ def tile_list_fold_match_evidence_kernel(
     with ExitStack() as ctx:
         lists = ctx.enter_context(tc.tile_pool(name="lists", bufs=1))
         keep = ctx.enter_context(tc.tile_pool(name="keep", bufs=1))
-        ring = ctx.enter_context(tc.tile_pool(name="ring", bufs=RING))
         psum = ctx.enter_context(tc.psum_pool(name="psum", bufs=1))
         taken = []
 
@@ -62,11 +60,9 @@ def tile_list_fold_match_evidence_kernel(
         query_bytes = held([P, T], U8, "query_bytes")
         fold_plane = held([P, S], U8, "fold_plane")
         wm_raw = held([P, 2 * H], U8, "wm_raw")
-        wm_raw_plane = held([P, H], U8, "wm_raw_plane")
         gain_cols = held([P, R_PASSES, PACK], F32, "gain_cols")
 
-        nc.vector.memset(query_bytes[:].bitcast(I32), 0)
-        nc.vector.memset(wm_raw_plane[:].bitcast(I32), 0)
+        nc.gpsimd.memset(query_bytes[:].bitcast(I32), 0)
         nc.vector.memset(fold_plane[:].bitcast(I32), 0)
 
         we_first = held([P, PASS // WE_COLS, PACK, WE_COLS], F32, "we_first")
@@ -84,18 +80,21 @@ def tile_list_fold_match_evidence_kernel(
             out=fold_bytes[:].bitcast(I32),
             in_=tab_scales[0].bitcast(I32).unsqueeze(1).to_broadcast([P // BLOCK_ROWS, BLOCK_ROWS, T // 4]),
         )
+        nc.sync.dma_start(out=gain_cols[:], in_=gain.rearrange("(g p t) -> p g t", p=P, t=PACK))
         load_words(fold_words, tab_words)
         for part in range(PASS // WE_COLS):
             load_we(we_first[:, part], part * WE_COLS, WE_COLS)
         nc.sync.dma_start(query_list[:], offs2)
-        nc.sync.dma_start(out=gain_cols[:], in_=gain.rearrange("(g p t) -> p g t", p=P, t=PACK))
         nc.sync.dma_start(out=wm_raw[:].bitcast(I32), in_=wm_words[0].bitcast(I32))
-        for plane_rows, scales in ((query_bytes, tab2_scales), (wm_raw_plane, wm_scales)):
+
+        def load_scale_rows(queue, plane_rows, scales):
             for d in range(QUADS):
-                nc.gpsimd.dma_start(
+                queue.dma_start(
                     out=plane_rows[QUAD * d:QUAD * d + 4, :].bitcast(I32),
                     in_=scales[0, 4 * d:4 * d + 4, :].bitcast(I32),
                 )
+
+        load_scale_rows(nc.gpsimd, query_bytes, tab2_scales)
 
         gain_flat = gain_cols[:].rearrange("p g t -> p (g t)")
         row_factor = held([P, R_PASSES * PACK], F32, "row_factor")
@@ -113,17 +112,18 @@ def tile_list_fold_match_evidence_kernel(
         query_words = held([P, T], U32, "query_words", after="fold_picked")
         load_words(query_words, tab2_words)
 
-        we_bf = [held([P, PACK, P, PACK], BF16, "we_bf%d" % g) for g in range(R_PASSES)]
+        we_bf = [held([P, PACK, P, PACK], BF16, "we_bf0"), held([P, PACK, P, PACK], BF16, "we_bf1", after="query_bytes")]
         we_codes = [held([P, PASS], U32, "we_codes%d" % g) for g in range(R_PASSES)]
         we_plane = [held([P, PASS], U8, "we_plane%d" % g) for g in range(R_PASSES)]
 
         def round_we_first(part):
             per_t = WE_COLS // PACK
-            nc.scalar.activation(
-                we_bf[0][:, :, part * per_t:(part + 1) * per_t, :].rearrange("p t m i -> p m i t"),
-                we_first[:, part].rearrange("p i (m t) -> p m i t", t=PACK),
-                ACT.Copy,
-            )
+            rounded = we_bf[0][:, :, part * per_t:(part + 1) * per_t, :].rearrange("p t m i -> p m i t")
+            loaded = we_first[:, part].rearrange("p i (m t) -> p m i t", t=PACK)
+            if part == 0:
+                nc.scalar.activation(rounded, loaded, ACT.Copy)
+            else:
+                nc.vector.tensor_copy(rounded, loaded)
 
         def quantize_we(g):
             nc.vector.quantize_mx(
@@ -159,19 +159,22 @@ def tile_list_fold_match_evidence_kernel(
         query_cols = [held([P, HALF], U32, "query_cols%d" % j) for j in range(HALVES)]
         for j in range(HALVES):
             gather_words(fold_cols, fold_words, fold_list, j)
+        wm_raw_plane = held([P, H], U8, "wm_raw_plane", after="fold_words")
+        nc.gpsimd.memset(wm_raw_plane[:].bitcast(I32), 0)
+        load_scale_rows(nc.sync, wm_raw_plane, wm_scales)
         for part in range(PASS // WE_COLS):
             round_we_first(part)
         quantize_we(0)
         for j in range(HALVES):
             for t in range(PACK):
                 evidence_tile(0, j, t)
-        query_plane = held([P, S], U8, "query_plane", after="fold_words")
+        query_plane = held([P, S], U8, "query_plane", after="we_bf0")
         nc.vector.tensor_copy(query_plane[:], query_bytes[:].indirect(query_list[:]))
         nc.vector.tensor_copy(
             we_bf[1][:].rearrange("p t m i -> p m i t"),
             we_second[:].rearrange("p i (m t) -> p m i t", t=PACK),
         )
-        wm_codes = held([P, 2 * H], U8, "wm_codes", after="we_first")
+        wm_codes = held([P, 2 * H], U8, "wm_codes", after="fold_bytes")
         nc.vector.tensor_copy(
             wm_codes[:].bitcast(U16).rearrange("p (g t m) -> p g t m", g=R_PASSES, t=PACK),
             wm_raw[:].bitcast(U16).rearrange("p (g m t) -> p g t m", g=R_PASSES, t=PACK),
@@ -179,7 +182,7 @@ def tile_list_fold_match_evidence_kernel(
         quantize_we(1)
         for t in range(PACK):
             evidence_tile(1, 0, t)
-        wm_plane = held([P, H], U8, "wm_plane", after="we_bf1")
+        wm_plane = held([P, H], U8, "wm_plane", after="query_bytes")
         nc.vector.tensor_copy(
             wm_plane[:].rearrange("p (g t m) -> p g t m", g=R_PASSES, t=PACK),
             wm_raw_plane[:].rearrange("p (g m t) -> p g t m", g=R_PASSES, t=PACK),
@@ -192,6 +195,8 @@ def tile_list_fold_match_evidence_kernel(
         nc.vector.reciprocal(gain_inv[:], gain_floor[:])
 
         pairs = [(j, g, t) for j in range(HALVES) for g in range(R_PASSES) for t in range(0, PACK, 2)]
+        last_pair = len(pairs) - 1
+        squared = {}
         b_last = held([P, HALF], F32, "b_last")
 
         def wm_product(g, t, picked, plane, j):
@@ -202,7 +207,7 @@ def tile_list_fold_match_evidence_kernel(
                 lhsT=wm_codes[:, 2 * P * tile_no:2 * P * (tile_no + 1)].bitcast(FP4X4),
                 lhsT_scale=wm_plane[:, P * tile_no:P * (tile_no + 1)],
                 rhs=picked[j][:].bitcast(FP8X4),
-                rhs_scale=plane[:, j * HALF:(j + 1) * HALF],
+                rhs_scale=plane,
                 start=True, stop=True,
             )
             return acc
@@ -213,31 +218,31 @@ def tile_list_fold_match_evidence_kernel(
 
         def copy_b(n, u):
             j, g, t = pairs[n]
-            b = wm_product(g, t + u, query_cols, query_plane, j)
-            if n == SCALAR_B_PAIR:
-                nc.scalar.copy(b_place(n, u), b[:])
-            else:
-                nc.vector.tensor_copy(b_place(n, u), b[:])
+            b = wm_product(g, t + u, query_cols, query_plane[:, j * HALF:(j + 1) * HALF], j)
+            nc.vector.tensor_copy(b_place(n, u), b[:])
 
         def subtract(n, u):
             j, g, t = pairs[n]
-            a = wm_product(g, t + u, fold_cols, fold_plane, j)
+            a = wm_product(g, t + u, fold_cols, fold_plane[:, j * HALF:(j + 1) * HALF], j)
             nc.vector.tensor_tensor(match[g][j][:, t + u, :], a[:], b_place(n, u), ALU.subtract)
 
         def square(n):
             j, g, t = pairs[n]
             pair = match[g][j][:, t:t + 2, :]
-            if n == len(pairs) - 1:
-                nc.scalar.activation(pair, pair, ACT.Square)
+            squared[n] = pair
+            if n in (last_pair - 2, last_pair):
+                squared[n] = held([P, 2, HALF], F32, "squares_aside")[:]
+            if n in (1, last_pair):
+                nc.scalar.activation(squared[n], pair, ACT.Square)
             else:
-                nc.gpsimd.tensor_tensor(pair, pair, pair, ALU.mult)
+                nc.gpsimd.tensor_tensor(squared[n], pair, pair, ALU.mult)
 
         def inverse_roots(n):
             j, g, t = pairs[n]
             for u in range(2):
                 inv = row_factor[:, g * PACK + t + u:g * PACK + t + u + 1]
-                squares = match[g][j][:, t + u, :]
-                nc.scalar.activation(squares, squares, ACT.Abs_reciprocal_sqrt, bias=inv, scale=inv)
+                nc.scalar.activation(match[g][j][:, t + u, :], squared[n][:, u, :], ACT.Abs_reciprocal_sqrt,
+                                     bias=inv, scale=inv)
 
         def square_roots(roots):
             nc.scalar.activation(roots, roots, ACT.Square)
@@ -252,18 +257,16 @@ def tile_list_fold_match_evidence_kernel(
             evidence_tile(1, 1, 2 + u)
             copy_b(1, u)
         for n in range(1, len(pairs)):
-            if n + 1 == SCALAR_B_PAIR:
-                for u in range(2):
-                    copy_b(n + 1, u)
-            if n not in (1, SCALAR_B_PAIR):
+            if n > 1:
                 for u in range(2):
                     copy_b(n, u)
             for u in range(2):
                 subtract(n, u)
-            square(n)
+            if 1 < n < last_pair:
+                square(n)
 
         wc_codes = held([P, R_PASSES, N], U32, "wc_codes", after="fold_picked")
-        wc_plane = held([P, R_PASSES, N], U8, "wc_plane", after="query_bytes")
+        wc_plane = held([P, R_PASSES, N], U8, "wc_plane", after="we_first")
         nc.sync.dma_start(
             out=wc_codes[:].bitcast(I32),
             in_=wc_words.rearrange("g p n i -> p g (n i)").bitcast(I32),
@@ -279,54 +282,61 @@ def tile_list_fold_match_evidence_kernel(
         for n in range(len(pairs) - 2):
             j, g, t = pairs[n]
             inverse_roots(n)
+            if n == 0:
+                square(1)
             square_roots(match[g][j][:, t:t + 2, :])
+        square(last_pair)
         for n in range(len(pairs) - 2, len(pairs)):
             inverse_roots(n)
         for c0 in range(0, HALF, QUARTER):
             square_roots(match[R_PASSES - 1][HALVES - 1][:, :, c0:c0 + QUARTER])
 
-        h_shape = [P, R_PASSES, HALF, PACK]
-        h_halves = [held(h_shape, BF16, "h_half0", after="b_last"), held(h_shape, BF16, "h_half1")]
         n_tiles = N // P
-        for q in range(S // QUARTER):
-            j, c0 = divmod(q * QUARTER, HALF)
-            cols = slice(c0, c0 + QUARTER)
-            last = q == S // QUARTER - 1
+        j0 = 0
+        for step, width in enumerate(STEPS):
+            j, c0 = divmod(j0, HALF)
+            cols = slice(c0, c0 + width)
+            last = step == len(STEPS) - 1
+            h_step = held([P, R_PASSES, width, PACK], BF16, "h_step%d" % step, after="b_last" if step == 0 else "")
             for g in range(R_PASSES):
                 nc.vector.tensor_tensor(
-                    h_halves[j][:, g, cols, :].rearrange("p (c i) t -> p c t i", i=LINE),
+                    h_step[:, g].rearrange("p (c i) t -> p c t i", i=LINE),
                     match[g][j][:, :, cols].rearrange("p t (c i) -> p c t i", i=LINE),
                     evidence[g][j][:, :, cols].rearrange("p t (c i) -> p c t i", i=LINE),
                     ALU.mult,
                 )
-            h_codes = [held([P, QUARTER], U32, "h_codes%d%d" % (q, g)) for g in range(R_PASSES)]
-            h_plane = [held([P, QUARTER], U8, "h_plane%d%d" % (q, g)) for g in range(R_PASSES)]
+            h_codes = [held([P, width], U32, "h_codes%d%d" % (step, g)) for g in range(R_PASSES)]
+            h_plane = [held([P, width], U8, "h_plane%d%d" % (step, g)) for g in range(R_PASSES)]
             for g in range(R_PASSES):
                 nc.vector.quantize_mx(out=h_codes[g][:].bitcast(FP8X4), scales=h_plane[g][:],
-                                      in_=h_halves[j][:, g, cols, :].rearrange("p j t -> p (j t)"))
+                                      in_=h_step[:, g].rearrange("p j t -> p (j t)"))
 
-            per_bank = 1 if last else HALF // QUARTER
-            banks = [next_bank(per_bank * QUARTER) for n in range(0, n_tiles, per_bank)]
+            per_bank = 1 if last else HALF // width
+            banks = [next_bank(per_bank * width) for n in range(0, n_tiles, per_bank)]
             for place in range(per_bank):
                 for g in range(R_PASSES):
                     for u, bank in enumerate(banks):
                         n0 = (u * per_bank + place) * P
                         nc.tensor.matmul_mx(
-                            out=bank[:, place * QUARTER:(place + 1) * QUARTER],
+                            out=bank[:, place * width:(place + 1) * width],
                             lhsT=wc_codes[:, g, n0:n0 + P].bitcast(FP8X4),
                             lhsT_scale=wc_plane[:, g, n0:n0 + P],
                             rhs=h_codes[g][:].bitcast(FP8X4),
                             rhs_scale=h_plane[g][:],
                             start=(g == 0), stop=(g == R_PASSES - 1),
                         )
+            results = held([P, n_tiles, width], F32, "results%d" % step, after="squares_aside" if step == 0 else "")
             for n in range(0, n_tiles, 2):
-                result = ring.tile([P, 2 * QUARTER], F32, name="result")
+                result = results[:, n:n + 2, :]
                 if last:
-                    nc.scalar.copy(result[:, 0:QUARTER], banks[n][:])
-                    nc.vector.tensor_copy(result[:, QUARTER:2 * QUARTER], banks[n + 1][:])
+                    nc.scalar.copy(result[:, 0, :], banks[n][:])
+                    nc.vector.tensor_copy(result[:, 1, :], banks[n + 1][:])
+                elif per_bank == 1:
+                    for u in range(2):
+                        nc.scalar.copy(result[:, u, :], banks[n + u][:])
                 else:
-                    nc.scalar.copy(result[:], banks[n // per_bank][:])
-                dst = out[n * P:(n + 2) * P, q * QUARTER:(q + 1) * QUARTER]
+                    nc.scalar.copy(result.rearrange("p u j -> p (u j)"), banks[n // per_bank][:])
+                dst = out[n * P:(n + 2) * P, j0:j0 + width]
                 queue = nc.scalar if last and n > 0 else nc.sync
-                queue.dma_start(out=dst.rearrange("(u p) j -> p u j", p=P),
-                                in_=result[:].rearrange("p (u j) -> p u j", u=2))
+                queue.dma_start(out=dst.rearrange("(u p) j -> p u j", p=P), in_=result)
+            j0 += width

@@ -224,7 +224,7 @@ def tile_list_fold_match_evidence_kernel(
         def subtract(n, u):
             j, g, t = pairs[n]
             a = wm_product(g, t + u, fold_cols, fold_plane[:, j * HALF:(j + 1) * HALF], j)
-            nc.vector.tensor_tensor(match[g][j][:, t + u, :], a[:], b_place(n, u), ALU.subtract)
+            nc.vector.tensor_tensor(match[g][j][:, t + u, :], b_place(n, u), a[:], ALU.subtract)
 
         def square(n):
             j, g, t = pairs[n]

@@ -28,9 +28,10 @@ HALF = 512
 HALVES = S // HALF
 QUARTER = 256
 WE_COLS = 256
-STEPS = (HALF, QUARTER, QUARTER)
+STEPS = (QUARTER,) * (S // QUARTER)
 LINE = 4
 BANKS = 8
+SCALAR_B_PAIR = 2
 TINY = 2.0 ** -100
 
 
@@ -59,11 +60,11 @@ def tile_list_fold_match_evidence_kernel(
         fold_bytes = held([P, T], U8, "fold_bytes")
         query_bytes = held([P, T], U8, "query_bytes")
         fold_plane = held([P, S], U8, "fold_plane")
-        wm_raw = held([P, 2 * H], U8, "wm_raw")
+        query_plane = held([P, S], U8, "query_plane")
         gain_cols = held([P, R_PASSES, PACK], F32, "gain_cols")
 
-        nc.gpsimd.memset(query_bytes[:].bitcast(I32), 0)
-        nc.vector.memset(fold_plane[:].bitcast(I32), 0)
+        for plane in (fold_plane, query_plane):
+            nc.vector.memset(plane[:].bitcast(I32), 0)
 
         we_first = held([P, PASS // WE_COLS, PACK, WE_COLS], F32, "we_first")
         fold_words = held([P, T], U32, "fold_words")
@@ -75,17 +76,17 @@ def tile_list_fold_match_evidence_kernel(
             nc.sync.dma_start(out=dst[:].bitcast(I32),
                               in_=words[0].rearrange("p t i -> p (t i)").bitcast(I32))
 
-        nc.sync.dma_start(fold_list[:], offs)
-        nc.sync.dma_start(
-            out=fold_bytes[:].bitcast(I32),
-            in_=tab_scales[0].bitcast(I32).unsqueeze(1).to_broadcast([P // BLOCK_ROWS, BLOCK_ROWS, T // 4]),
-        )
+        for picks, list_in, window, scales in ((fold_list, offs, fold_bytes, tab_scales),
+                                               (query_list, offs2, query_bytes, tab2_scales)):
+            nc.sync.dma_start(picks[:], list_in)
+            nc.sync.dma_start(
+                out=window[:].bitcast(I32),
+                in_=scales[0].bitcast(I32).unsqueeze(1).to_broadcast([P // BLOCK_ROWS, BLOCK_ROWS, T // 4]),
+            )
         nc.sync.dma_start(out=gain_cols[:], in_=gain.rearrange("(g p t) -> p g t", p=P, t=PACK))
-        load_words(fold_words, tab_words)
         for part in range(PASS // WE_COLS):
             load_we(we_first[:, part], part * WE_COLS, WE_COLS)
-        nc.sync.dma_start(query_list[:], offs2)
-        nc.sync.dma_start(out=wm_raw[:].bitcast(I32), in_=wm_words[0].bitcast(I32))
+        load_words(fold_words, tab_words)
 
         def load_scale_rows(queue, plane_rows, scales):
             for d in range(QUADS):
@@ -94,7 +95,6 @@ def tile_list_fold_match_evidence_kernel(
                     in_=scales[0, 4 * d:4 * d + 4, :].bitcast(I32),
                 )
 
-        load_scale_rows(nc.gpsimd, query_bytes, tab2_scales)
 
         gain_flat = gain_cols[:].rearrange("p g t -> p (g t)")
         row_factor = held([P, R_PASSES * PACK], F32, "row_factor")
@@ -102,17 +102,23 @@ def tile_list_fold_match_evidence_kernel(
         gain_inv = held([P, R_PASSES * PACK], F32, "gain_inv")
         nc.scalar.activation(row_factor[:], gain_flat, ACT.Sign)
 
-        fold_picked = held([P, S], U8, "fold_picked")
-        nc.vector.tensor_copy(fold_picked[:], fold_bytes[:].indirect(fold_list[:]))
-        for u in range(QUAD // BLOCK_ROWS):
-            nc.sync.dma_start(out=fold_plane[u:P:QUAD, :].bitcast(I32),
-                              in_=fold_picked[BLOCK_ROWS * u:P:QUAD, :].bitcast(I32))
+        def gather_scales(plane, window, picks, name):
+            picked = held([P, S], U8, name)
+            nc.vector.tensor_copy(picked[:], window[:].indirect(picks[:]))
+            for u in range(QUAD // BLOCK_ROWS):
+                nc.sync.dma_start(out=plane[u:P:QUAD, :].bitcast(I32),
+                                  in_=picked[BLOCK_ROWS * u:P:QUAD, :].bitcast(I32))
+
+        gather_scales(fold_plane, fold_bytes, fold_list, "fold_picked")
         we_second = held([P, PACK, PASS], F32, "we_second", after="fold_bytes")
         load_we(we_second[:], PASS, PASS)
+        gather_scales(query_plane, query_bytes, query_list, "query_picked")
+        wm_raw = held([P, 2 * H], U8, "wm_raw", after="query_bytes")
+        nc.sync.dma_start(out=wm_raw[:].bitcast(I32), in_=wm_words[0].bitcast(I32))
         query_words = held([P, T], U32, "query_words", after="fold_picked")
         load_words(query_words, tab2_words)
 
-        we_bf = [held([P, PACK, P, PACK], BF16, "we_bf0"), held([P, PACK, P, PACK], BF16, "we_bf1", after="query_bytes")]
+        we_bf = [held([P, PACK, P, PACK], BF16, "we_bf0"), held([P, PACK, P, PACK], BF16, "we_bf1", after="fold_words")]
         we_codes = [held([P, PASS], U32, "we_codes%d" % g) for g in range(R_PASSES)]
         we_plane = [held([P, PASS], U8, "we_plane%d" % g) for g in range(R_PASSES)]
 
@@ -120,10 +126,7 @@ def tile_list_fold_match_evidence_kernel(
             per_t = WE_COLS // PACK
             rounded = we_bf[0][:, :, part * per_t:(part + 1) * per_t, :].rearrange("p t m i -> p m i t")
             loaded = we_first[:, part].rearrange("p i (m t) -> p m i t", t=PACK)
-            if part == 0:
-                nc.scalar.activation(rounded, loaded, ACT.Copy)
-            else:
-                nc.vector.tensor_copy(rounded, loaded)
+            nc.scalar.activation(rounded, loaded, ACT.Copy)
 
         def quantize_we(g):
             nc.vector.quantize_mx(
@@ -157,19 +160,16 @@ def tile_list_fold_match_evidence_kernel(
 
         fold_cols = [held([P, HALF], U32, "fold_cols%d" % j) for j in range(HALVES)]
         query_cols = [held([P, HALF], U32, "query_cols%d" % j) for j in range(HALVES)]
-        for j in range(HALVES):
-            gather_words(fold_cols, fold_words, fold_list, j)
-        wm_raw_plane = held([P, H], U8, "wm_raw_plane", after="fold_words")
+        wm_raw_plane = held([P, H], U8, "wm_raw_plane", after="query_picked")
         nc.gpsimd.memset(wm_raw_plane[:].bitcast(I32), 0)
         load_scale_rows(nc.sync, wm_raw_plane, wm_scales)
         for part in range(PASS // WE_COLS):
             round_we_first(part)
         quantize_we(0)
         for j in range(HALVES):
+            gather_words(fold_cols, fold_words, fold_list, j)
             for t in range(PACK):
                 evidence_tile(0, j, t)
-        query_plane = held([P, S], U8, "query_plane", after="we_bf0")
-        nc.vector.tensor_copy(query_plane[:], query_bytes[:].indirect(query_list[:]))
         nc.vector.tensor_copy(
             we_bf[1][:].rearrange("p t m i -> p m i t"),
             we_second[:].rearrange("p i (m t) -> p m i t", t=PACK),
@@ -182,7 +182,7 @@ def tile_list_fold_match_evidence_kernel(
         quantize_we(1)
         for t in range(PACK):
             evidence_tile(1, 0, t)
-        wm_plane = held([P, H], U8, "wm_plane", after="query_bytes")
+        wm_plane = held([P, H], U8, "wm_plane", after="fold_words")
         nc.vector.tensor_copy(
             wm_plane[:].rearrange("p (g t m) -> p g t m", g=R_PASSES, t=PACK),
             wm_raw_plane[:].rearrange("p (g m t) -> p g t m", g=R_PASSES, t=PACK),
@@ -219,7 +219,10 @@ def tile_list_fold_match_evidence_kernel(
         def copy_b(n, u):
             j, g, t = pairs[n]
             b = wm_product(g, t + u, query_cols, query_plane[:, j * HALF:(j + 1) * HALF], j)
-            nc.vector.tensor_copy(b_place(n, u), b[:])
+            if n == SCALAR_B_PAIR:
+                nc.scalar.copy(b_place(n, u), b[:])
+            else:
+                nc.vector.tensor_copy(b_place(n, u), b[:])
 
         def subtract(n, u):
             j, g, t = pairs[n]
@@ -257,7 +260,10 @@ def tile_list_fold_match_evidence_kernel(
             evidence_tile(1, 1, 2 + u)
             copy_b(1, u)
         for n in range(1, len(pairs)):
-            if n > 1:
+            if n + 1 == SCALAR_B_PAIR:
+                for u in range(2):
+                    copy_b(n + 1, u)
+            if n not in (1, SCALAR_B_PAIR):
                 for u in range(2):
                     copy_b(n, u)
             for u in range(2):
@@ -288,11 +294,13 @@ def tile_list_fold_match_evidence_kernel(
         square(last_pair)
         for n in range(len(pairs) - 2, len(pairs)):
             inverse_roots(n)
-        for c0 in range(0, HALF, QUARTER):
-            square_roots(match[R_PASSES - 1][HALVES - 1][:, :, c0:c0 + QUARTER])
+        last_roots = match[R_PASSES - 1][HALVES - 1]
+        square_roots(last_roots[:, :, 0:QUARTER])
 
         n_tiles = N // P
         j0 = 0
+        results = [held([P, HALF // QUARTER, n_tiles, QUARTER], F32, "results0", after="squares_aside"),
+                   held([P, HALF // QUARTER, n_tiles, QUARTER], F32, "results1")]
         for step, width in enumerate(STEPS):
             j, c0 = divmod(j0, HALF)
             cols = slice(c0, c0 + width)
@@ -325,18 +333,16 @@ def tile_list_fold_match_evidence_kernel(
                             rhs_scale=h_plane[g][:],
                             start=(g == 0), stop=(g == R_PASSES - 1),
                         )
-            results = held([P, n_tiles, width], F32, "results%d" % step, after="squares_aside" if step == 0 else "")
             for n in range(0, n_tiles, 2):
-                result = results[:, n:n + 2, :]
+                result = results[j][:, c0 // QUARTER, n:n + 2, :]
                 if last:
                     nc.scalar.copy(result[:, 0, :], banks[n][:])
                     nc.vector.tensor_copy(result[:, 1, :], banks[n + 1][:])
-                elif per_bank == 1:
-                    for u in range(2):
-                        nc.scalar.copy(result[:, u, :], banks[n + u][:])
                 else:
                     nc.scalar.copy(result.rearrange("p u j -> p (u j)"), banks[n // per_bank][:])
                 dst = out[n * P:(n + 2) * P, j0:j0 + width]
                 queue = nc.scalar if last and n > 0 else nc.sync
                 queue.dma_start(out=dst.rearrange("(u p) j -> p u j", p=P), in_=result)
+            if step == 0:
+                square_roots(last_roots[:, :, QUARTER:HALF])
             j0 += width

@@ -32,7 +32,7 @@ STEPS = (QUARTER,) * (S // QUARTER)
 LINE = 4
 BANKS = 8
 SCALAR_B_PAIR = 2
-TINY = 2.0 ** -100
+TINY = 2.0 ** -120
 
 
 def tile_list_fold_match_evidence_kernel(
@@ -98,9 +98,9 @@ def tile_list_fold_match_evidence_kernel(
 
         gain_flat = gain_cols[:].rearrange("p g t -> p (g t)")
         row_factor = held([P, R_PASSES * PACK], F32, "row_factor")
-        gain_floor = held([P, R_PASSES * PACK], F32, "gain_floor")
-        gain_inv = held([P, R_PASSES * PACK], F32, "gain_inv")
+        gain_squared = held([P, R_PASSES * PACK], F32, "gain_squared")
         nc.scalar.activation(row_factor[:], gain_flat, ACT.Sign)
+        nc.scalar.activation(gain_squared[:], gain_flat, ACT.Square)
 
         def gather_scales(plane, window, picks, name):
             picked = held([P, S], U8, name)
@@ -161,7 +161,7 @@ def tile_list_fold_match_evidence_kernel(
         fold_cols = [held([P, HALF], U32, "fold_cols%d" % j) for j in range(HALVES)]
         query_cols = [held([P, HALF], U32, "query_cols%d" % j) for j in range(HALVES)]
         wm_raw_plane = held([P, H], U8, "wm_raw_plane", after="query_picked")
-        nc.gpsimd.memset(wm_raw_plane[:].bitcast(I32), 0)
+        nc.vector.memset(wm_raw_plane[:].bitcast(I32), 0)
         load_scale_rows(nc.sync, wm_raw_plane, wm_scales)
         for part in range(PASS // WE_COLS):
             round_we_first(part)
@@ -188,16 +188,12 @@ def tile_list_fold_match_evidence_kernel(
             wm_raw_plane[:].rearrange("p (g m t) -> p g t m", g=R_PASSES, t=PACK),
         )
         gather_words(query_cols, query_words, query_list, 0)
-        gain_abs = held([P, R_PASSES * PACK], F32, "gain_abs")
-        nc.scalar.activation(gain_abs[:], gain_flat, ACT.Abs)
-        nc.vector.tensor_scalar_max(gain_floor[:], gain_abs[:], TINY)
         gather_words(query_cols, query_words, query_list, 1)
-        nc.vector.reciprocal(gain_inv[:], gain_floor[:])
 
         pairs = [(j, g, t) for j in range(HALVES) for g in range(R_PASSES) for t in range(0, PACK, 2)]
         last_pair = len(pairs) - 1
         squared = {}
-        b_last = held([P, HALF], F32, "b_last")
+        b_apart = {(1, 0): held([P, HALF], F32, "b_third"), (last_pair, 1): held([P, HALF], F32, "b_last")}
 
         def wm_product(g, t, picked, plane, j):
             acc = next_bank(HALF)
@@ -214,7 +210,7 @@ def tile_list_fold_match_evidence_kernel(
 
         def b_place(n, u):
             j, g, t = pairs[n]
-            return b_last[:] if (n, u) == (len(pairs) - 1, 1) else match[g][j][:, t + u, :]
+            return b_apart[(n, u)][:] if (n, u) in b_apart else match[g][j][:, t + u, :]
 
         def copy_b(n, u):
             j, g, t = pairs[n]
@@ -243,7 +239,7 @@ def tile_list_fold_match_evidence_kernel(
         def inverse_roots(n):
             j, g, t = pairs[n]
             for u in range(2):
-                inv = row_factor[:, g * PACK + t + u:g * PACK + t + u + 1]
+                inv = gain_inv[:, g * PACK + t + u:g * PACK + t + u + 1]
                 nc.scalar.activation(match[g][j][:, t + u, :], squared[n][:, u, :], ACT.Abs_reciprocal_sqrt,
                                      bias=inv, scale=inv)
 
@@ -272,7 +268,7 @@ def tile_list_fold_match_evidence_kernel(
                 square(n)
 
         wc_codes = held([P, R_PASSES, N], U32, "wc_codes", after="fold_picked")
-        wc_plane = held([P, R_PASSES, N], U8, "wc_plane", after="we_first")
+        wc_plane = held([P, R_PASSES, N], U8, "wc_plane", after="query_picked")
         nc.sync.dma_start(
             out=wc_codes[:].bitcast(I32),
             in_=wc_words.rearrange("g p n i -> p g (n i)").bitcast(I32),
@@ -284,7 +280,8 @@ def tile_list_fold_match_evidence_kernel(
                 in_=wc_scales[:, 4 * d:4 * d + 4, :].rearrange("g q n -> q g n").bitcast(I32),
             )
 
-        nc.scalar.copy(row_factor[:], gain_inv[:])
+        gain_inv = held([P, R_PASSES * PACK], F32, "gain_inv", after="b_third")
+        nc.scalar.activation(gain_inv[:], gain_squared[:], ACT.Abs_reciprocal_sqrt, bias=TINY)
         for n in range(len(pairs) - 2):
             j, g, t = pairs[n]
             inverse_roots(n)
@@ -299,13 +296,15 @@ def tile_list_fold_match_evidence_kernel(
 
         n_tiles = N // P
         j0 = 0
+        h_shape = [P, HALF // QUARTER, R_PASSES, QUARTER, PACK]
+        h_halves = [held(h_shape, BF16, "h_half0", after="b_last"), held(h_shape, BF16, "h_half1")]
         results = [held([P, HALF // QUARTER, n_tiles, QUARTER], F32, "results0", after="squares_aside"),
                    held([P, HALF // QUARTER, n_tiles, QUARTER], F32, "results1")]
         for step, width in enumerate(STEPS):
             j, c0 = divmod(j0, HALF)
             cols = slice(c0, c0 + width)
             last = step == len(STEPS) - 1
-            h_step = held([P, R_PASSES, width, PACK], BF16, "h_step%d" % step, after="b_last" if step == 0 else "")
+            h_step = h_halves[j][:, c0 // QUARTER]
             for g in range(R_PASSES):
                 nc.vector.tensor_tensor(
                     h_step[:, g].rearrange("p (c i) t -> p c t i", i=LINE),

@@ -225,23 +225,20 @@ def tile_list_fold_match_evidence_kernel(
             a = wm_product(g, t + u, fold_cols, fold_plane[:, j * HALF:(j + 1) * HALF], j)
             nc.vector.tensor_tensor(match[g][j][:, t + u, :], b_place(n, u), a[:], ALU.subtract)
 
-        def square(n):
-            j, g, t = pairs[n]
-            pair = match[g][j][:, t:t + 2, :]
-            squared[n] = pair
-            if n in (last_pair - 2, last_pair):
-                squared[n] = held([P, 2, HALF], F32, "squares_aside")[:]
-            if n in (1, last_pair):
-                nc.scalar.activation(squared[n], pair, ACT.Square)
+        def square(j, g, t0, t1, on_scalar=False, aside=False):
+            differences = match[g][j][:, t0:t1, :]
+            dst = held([P, t1 - t0, HALF], F32, "squares_aside")[:] if aside else differences
+            if on_scalar:
+                nc.scalar.activation(dst, differences, ACT.Square)
             else:
-                nc.gpsimd.tensor_tensor(squared[n], pair, pair, ALU.mult)
+                nc.gpsimd.tensor_tensor(dst, differences, differences, ALU.mult)
+            for t in range(t0, t1):
+                squared[(j, g, t)] = dst[:, t - t0, :]
 
-        def inverse_roots(n):
-            j, g, t = pairs[n]
-            for u in range(2):
-                inv = gain_inv[:, g * PACK + t + u:g * PACK + t + u + 1]
-                nc.scalar.activation(match[g][j][:, t + u, :], squared[n][:, u, :], ACT.Abs_reciprocal_sqrt,
-                                     bias=inv, scale=inv)
+        def inverse_root(j, g, t):
+            inv = gain_inv[:, g * PACK + t:g * PACK + t + 1]
+            nc.scalar.activation(match[g][j][:, t, :], squared[(j, g, t)], ACT.Abs_reciprocal_sqrt,
+                                 bias=inv, scale=inv)
 
         def square_roots(roots):
             nc.scalar.activation(roots, roots, ACT.Square)
@@ -251,7 +248,7 @@ def tile_list_fold_match_evidence_kernel(
         for u in range(2):
             evidence_tile(1, 1, u)
             subtract(0, u)
-        square(0)
+            square(0, 0, u, u + 1)
         for u in range(2):
             evidence_tile(1, 1, 2 + u)
             copy_b(1, u)
@@ -262,10 +259,13 @@ def tile_list_fold_match_evidence_kernel(
             if n not in (1, SCALAR_B_PAIR):
                 for u in range(2):
                     copy_b(n, u)
-            for u in range(2):
-                subtract(n, u)
-            if 1 < n < last_pair:
-                square(n)
+            j, g, t = pairs[n]
+            subtract(n, 0)
+            if n in (1, last_pair - 1):
+                square(j, g, t, t + 1)
+            subtract(n, 1)
+            if 1 < n < last_pair - 1:
+                square(j, g, t, t + 2, aside=(n == last_pair - 2))
 
         wc_codes = held([P, R_PASSES, N], U32, "wc_codes", after="fold_picked")
         wc_plane = held([P, R_PASSES, N], U8, "wc_plane", after="query_picked")
@@ -284,13 +284,14 @@ def tile_list_fold_match_evidence_kernel(
         nc.scalar.activation(gain_inv[:], gain_squared[:], ACT.Abs_reciprocal_sqrt, bias=TINY)
         for n in range(len(pairs) - 2):
             j, g, t = pairs[n]
-            inverse_roots(n)
+            for u in range(2):
+                inverse_root(j, g, t + u)
             if n == 0:
-                square(1)
+                square(0, 0, PACK - 1, PACK, on_scalar=True)
             square_roots(match[g][j][:, t:t + 2, :])
-        square(last_pair)
-        for n in range(len(pairs) - 2, len(pairs)):
-            inverse_roots(n)
+        square(HALVES - 1, R_PASSES - 1, 1, PACK, on_scalar=True, aside=True)
+        for t in range(PACK):
+            inverse_root(HALVES - 1, R_PASSES - 1, t)
         last_roots = match[R_PASSES - 1][HALVES - 1]
         square_roots(last_roots[:, :, 0:QUARTER])
 

@@ -63,6 +63,8 @@ def tile_list_fold_match_evidence_kernel(
         query_plane = held([P, S], U8, "query_plane")
         gain_cols = held([P, R_PASSES, PACK], F32, "gain_cols")
 
+        for p0, p1 in ((QUAD, 2 * QUAD), (2 * QUAD, P)):
+            nc.vector.memset(query_bytes[p0:p1, :].bitcast(I32), 0)
         for plane in (fold_plane, query_plane):
             nc.vector.memset(plane[:].bitcast(I32), 0)
 
@@ -76,24 +78,26 @@ def tile_list_fold_match_evidence_kernel(
             nc.sync.dma_start(out=dst[:].bitcast(I32),
                               in_=words[0].rearrange("p t i -> p (t i)").bitcast(I32))
 
-        for picks, list_in, window, scales in ((fold_list, offs, fold_bytes, tab_scales),
-                                               (query_list, offs2, query_bytes, tab2_scales)):
-            nc.sync.dma_start(picks[:], list_in)
-            nc.sync.dma_start(
-                out=window[:].bitcast(I32),
-                in_=scales[0].bitcast(I32).unsqueeze(1).to_broadcast([P // BLOCK_ROWS, BLOCK_ROWS, T // 4]),
-            )
+        nc.sync.dma_start(fold_list[:], offs)
+        nc.sync.dma_start(
+            out=fold_bytes[:].bitcast(I32),
+            in_=tab_scales[0].bitcast(I32).unsqueeze(1).to_broadcast([P // BLOCK_ROWS, BLOCK_ROWS, T // 4]),
+        )
+        nc.sync.dma_start(query_list[:], offs2)
+        nc.sync.dma_start(
+            out=query_bytes[0:QUAD, :].bitcast(I32),
+            in_=tab2_scales[0].bitcast(I32).unsqueeze(0).to_broadcast([QUAD // GROUP, GROUP, T // 4]),
+        )
         nc.sync.dma_start(out=gain_cols[:], in_=gain.rearrange("(g p t) -> p g t", p=P, t=PACK))
         for part in range(PASS // WE_COLS):
             load_we(we_first[:, part], part * WE_COLS, WE_COLS)
         load_words(fold_words, tab_words)
 
-        def load_scale_rows(queue, plane_rows, scales):
+        def load_scale_rows(plane, scales):
             for d in range(QUADS):
-                queue.dma_start(
-                    out=plane_rows[QUAD * d:QUAD * d + 4, :].bitcast(I32),
-                    in_=scales[0, 4 * d:4 * d + 4, :].bitcast(I32),
-                )
+                rows = scales[4 * d:4 * d + 4, :].bitcast(I32)
+                nc.sync.dma_start(out=plane[QUAD * d:QUAD * (d + 1), :].bitcast(I32),
+                                  in_=rows.unsqueeze(0).to_broadcast([QUAD // 4, 4, rows.shape[1]]))
 
 
         gain_flat = gain_cols[:].rearrange("p g t -> p (g t)")
@@ -102,17 +106,17 @@ def tile_list_fold_match_evidence_kernel(
         nc.scalar.activation(row_factor[:], gain_flat, ACT.Sign)
         nc.scalar.activation(gain_squared[:], gain_flat, ACT.Square)
 
-        def gather_scales(plane, window, picks, name):
+        def gather_scales(plane, window, picks, name, row_step):
             picked = held([P, S], U8, name)
             nc.vector.tensor_copy(picked[:], window[:].indirect(picks[:]))
-            for u in range(QUAD // BLOCK_ROWS):
-                nc.sync.dma_start(out=plane[u:P:QUAD, :].bitcast(I32),
-                                  in_=picked[BLOCK_ROWS * u:P:QUAD, :].bitcast(I32))
+            for d in range(QUADS):
+                rows = picked[4 * d * row_step:4 * (d + 1) * row_step:row_step, :]
+                nc.sync.dma_start(out=plane[QUAD * d:QUAD * d + 4, :].bitcast(I32), in_=rows.bitcast(I32))
 
-        gather_scales(fold_plane, fold_bytes, fold_list, "fold_picked")
+        gather_scales(fold_plane, fold_bytes, fold_list, "fold_picked", BLOCK_ROWS)
         we_second = held([P, PACK, PASS], F32, "we_second", after="fold_bytes")
         load_we(we_second[:], PASS, PASS)
-        gather_scales(query_plane, query_bytes, query_list, "query_picked")
+        gather_scales(query_plane, query_bytes, query_list, "query_picked", 1)
         wm_raw = held([P, 2 * H], U8, "wm_raw", after="query_bytes")
         nc.sync.dma_start(out=wm_raw[:].bitcast(I32), in_=wm_words[0].bitcast(I32))
         query_words = held([P, T], U32, "query_words", after="fold_picked")
@@ -161,8 +165,7 @@ def tile_list_fold_match_evidence_kernel(
         fold_cols = [held([P, HALF], U32, "fold_cols%d" % j) for j in range(HALVES)]
         query_cols = [held([P, HALF], U32, "query_cols%d" % j) for j in range(HALVES)]
         wm_raw_plane = held([P, H], U8, "wm_raw_plane", after="query_picked")
-        nc.vector.memset(wm_raw_plane[:].bitcast(I32), 0)
-        load_scale_rows(nc.sync, wm_raw_plane, wm_scales)
+        load_scale_rows(wm_raw_plane[:], wm_scales[0])
         for part in range(PASS // WE_COLS):
             round_we_first(part)
         quantize_we(0)
@@ -273,12 +276,8 @@ def tile_list_fold_match_evidence_kernel(
             out=wc_codes[:].bitcast(I32),
             in_=wc_words.rearrange("g p n i -> p g (n i)").bitcast(I32),
         )
-        nc.gpsimd.memset(wc_plane[:].rearrange("p g n -> p (g n)").bitcast(I32), 0)
-        for d in range(QUADS):
-            nc.sync.dma_start(
-                out=wc_plane[QUAD * d:QUAD * d + 4, :, :].bitcast(I32),
-                in_=wc_scales[:, 4 * d:4 * d + 4, :].rearrange("g q n -> q g n").bitcast(I32),
-            )
+        for g in range(R_PASSES):
+            load_scale_rows(wc_plane[:, g, :], wc_scales[g])
 
         gain_inv = held([P, R_PASSES * PACK], F32, "gain_inv", after="b_third")
         nc.scalar.activation(gain_inv[:], gain_squared[:], ACT.Abs_reciprocal_sqrt, bias=TINY)

@@ -28,10 +28,11 @@ HALF = 512
 HALVES = S // HALF
 QUARTER = 256
 WE_COLS = 256
+SCALAR_COLS = 384
 STEPS = (QUARTER,) * (S // QUARTER)
 LINE = 4
 BANKS = 8
-SCALAR_B_PAIR = 2
+SCALAR_B = ((2, 0), (2, 1), (3, 0))
 TINY = 2.0 ** -120
 
 
@@ -68,7 +69,7 @@ def tile_list_fold_match_evidence_kernel(
         for plane in (fold_plane, query_plane):
             nc.vector.memset(plane[:].bitcast(I32), 0)
 
-        we_first = held([P, PASS // WE_COLS, PACK, WE_COLS], F32, "we_first")
+        we_parts = [held([P, PACK, WE_COLS], F32, "we_part%d" % part) for part in range(PASS // WE_COLS)]
         fold_words = held([P, T], U32, "fold_words")
 
         def load_we(dst, c0, width):
@@ -78,27 +79,26 @@ def tile_list_fold_match_evidence_kernel(
             nc.sync.dma_start(out=dst[:].bitcast(I32),
                               in_=words[0].rearrange("p t i -> p (t i)").bitcast(I32))
 
-        nc.sync.dma_start(fold_list[:], offs)
-        nc.sync.dma_start(
-            out=fold_bytes[:].bitcast(I32),
-            in_=tab_scales[0].bitcast(I32).unsqueeze(1).to_broadcast([P // BLOCK_ROWS, BLOCK_ROWS, T // 4]),
-        )
-        nc.sync.dma_start(query_list[:], offs2)
-        nc.sync.dma_start(
-            out=query_bytes[0:QUAD, :].bitcast(I32),
-            in_=tab2_scales[0].bitcast(I32).unsqueeze(0).to_broadcast([QUAD // GROUP, GROUP, T // 4]),
-        )
-        nc.sync.dma_start(out=gain_cols[:], in_=gain.rearrange("(g p t) -> p g t", p=P, t=PACK))
-        for part in range(PASS // WE_COLS):
-            load_we(we_first[:, part], part * WE_COLS, WE_COLS)
-        load_words(fold_words, tab_words)
-
         def load_scale_rows(plane, scales):
             for d in range(QUADS):
                 rows = scales[4 * d:4 * d + 4, :].bitcast(I32)
                 nc.sync.dma_start(out=plane[QUAD * d:QUAD * (d + 1), :].bitcast(I32),
                                   in_=rows.unsqueeze(0).to_broadcast([QUAD // 4, 4, rows.shape[1]]))
 
+        nc.sync.dma_start(fold_list[:], offs)
+        nc.sync.dma_start(
+            out=fold_bytes[:].bitcast(I32),
+            in_=tab_scales[0].bitcast(I32).unsqueeze(1).to_broadcast([P // BLOCK_ROWS, BLOCK_ROWS, T // 4]),
+        )
+        nc.sync.dma_start(out=gain_cols[:], in_=gain.rearrange("(g p t) -> p g t", p=P, t=PACK))
+        load_words(fold_words, tab_words)
+        for part in range(PASS // WE_COLS):
+            load_we(we_parts[part][:], part * WE_COLS, WE_COLS)
+        nc.sync.dma_start(query_list[:], offs2)
+        nc.sync.dma_start(
+            out=query_bytes[0:QUAD, :].bitcast(I32),
+            in_=tab2_scales[0].bitcast(I32).unsqueeze(1).to_broadcast([GROUP, QUAD // GROUP, T // 4]),
+        )
 
         gain_flat = gain_cols[:].rearrange("p g t -> p (g t)")
         row_factor = held([P, R_PASSES * PACK], F32, "row_factor")
@@ -106,42 +106,43 @@ def tile_list_fold_match_evidence_kernel(
         nc.scalar.activation(row_factor[:], gain_flat, ACT.Sign)
         nc.scalar.activation(gain_squared[:], gain_flat, ACT.Square)
 
-        def gather_scales(plane, window, picks, name, row_step):
-            picked = held([P, S], U8, name)
+        def gather_scales(plane, window, picks, name, row_step, after=""):
+            picked = held([P, S], U8, name, after=after)
             nc.vector.tensor_copy(picked[:], window[:].indirect(picks[:]))
             for d in range(QUADS):
                 rows = picked[4 * d * row_step:4 * (d + 1) * row_step:row_step, :]
                 nc.sync.dma_start(out=plane[QUAD * d:QUAD * d + 4, :].bitcast(I32), in_=rows.bitcast(I32))
 
-        gather_scales(fold_plane, fold_bytes, fold_list, "fold_picked", BLOCK_ROWS)
-        we_second = held([P, PACK, PASS], F32, "we_second", after="fold_bytes")
-        load_we(we_second[:], PASS, PASS)
-        gather_scales(query_plane, query_bytes, query_list, "query_picked", 1)
-        wm_raw = held([P, 2 * H], U8, "wm_raw", after="query_bytes")
-        nc.sync.dma_start(out=wm_raw[:].bitcast(I32), in_=wm_words[0].bitcast(I32))
-        query_words = held([P, T], U32, "query_words", after="fold_picked")
-        load_words(query_words, tab2_words)
-
-        we_bf = [held([P, PACK, P, PACK], BF16, "we_bf0"), held([P, PACK, P, PACK], BF16, "we_bf1", after="fold_words")]
-        we_codes = [held([P, PASS], U32, "we_codes%d" % g) for g in range(R_PASSES)]
-        we_plane = [held([P, PASS], U8, "we_plane%d" % g) for g in range(R_PASSES)]
-
-        def round_we_first(part):
-            per_t = WE_COLS // PACK
-            rounded = we_bf[0][:, :, part * per_t:(part + 1) * per_t, :].rearrange("p t m i -> p m i t")
-            loaded = we_first[:, part].rearrange("p i (m t) -> p m i t", t=PACK)
-            nc.scalar.activation(rounded, loaded, ACT.Copy)
-
-        def quantize_we(g):
-            nc.vector.quantize_mx(
-                out=we_codes[g][:].bitcast(FP8X4),
-                scales=we_plane[g][:],
-                in_=we_bf[g][:].rearrange("p t m i -> p (t m i)"),
-            )
-
         def gather_words(dst, words, picks, j):
             per_half = HALF // GROUP
             nc.vector.tensor_copy(dst[j][:], words[:].indirect(picks[:, j * per_half:(j + 1) * per_half]))
+
+        gather_scales(fold_plane, fold_bytes, fold_list, "fold_picked", BLOCK_ROWS)
+        we_second = held([P, PACK, PASS], F32, "we_second", after="fold_bytes")
+        load_we(we_second[:], PASS, PASS)
+        fold_cols = [held([P, HALF], U32, "fold_cols%d" % j) for j in range(HALVES)]
+        for j in range(HALVES):
+            gather_words(fold_cols, fold_words, fold_list, j)
+
+        we_bf = [held([P, PACK, P, PACK], BF16, "we_bf0")]
+        we_codes = [held([P, PASS], U32, "we_codes%d" % g) for g in range(R_PASSES)]
+        we_plane = [held([P, PASS], U8, "we_plane%d" % g) for g in range(R_PASSES)]
+
+        def round_we_first(c0, c1, on_scalar):
+            part, w0 = divmod(c0, WE_COLS)
+            rounded = we_bf[0][:, :, c0 // PACK:c1 // PACK, :].rearrange("p t m i -> p m i t")
+            loaded = we_parts[part][:, :, w0:w0 + c1 - c0].rearrange("p i (m t) -> p m i t", t=PACK)
+            if on_scalar:
+                nc.scalar.activation(rounded, loaded, ACT.Copy)
+            else:
+                nc.vector.tensor_copy(rounded, loaded)
+
+        def quantize_we(g, t0, t1):
+            nc.vector.quantize_mx(
+                out=we_codes[g][:, t0 * P:t1 * P].bitcast(FP8X4),
+                scales=we_plane[g][:, t0 * P:t1 * P],
+                in_=we_bf[g][:, t0:t1].rearrange("p t m i -> p (t m i)"),
+            )
 
         evidence = [[held([P, PACK, HALF], F32, "evidence%d%d" % (g, j)) for j in range(HALVES)]
                     for g in range(R_PASSES)]
@@ -162,17 +163,24 @@ def tile_list_fold_match_evidence_kernel(
             nc.scalar.activation(evidence[g][j][:, t, :], e[:], ACT.Tanh,
                                  scale=row_factor[:, tile_no:tile_no + 1])
 
-        fold_cols = [held([P, HALF], U32, "fold_cols%d" % j) for j in range(HALVES)]
-        query_cols = [held([P, HALF], U32, "query_cols%d" % j) for j in range(HALVES)]
-        wm_raw_plane = held([P, H], U8, "wm_raw_plane", after="query_picked")
-        load_scale_rows(wm_raw_plane[:], wm_scales[0])
-        for part in range(PASS // WE_COLS):
-            round_we_first(part)
-        quantize_we(0)
+        round_we_first(0, WE_COLS, True)
+        round_we_first(WE_COLS, SCALAR_COLS, True)
+        round_we_first(SCALAR_COLS, PASS, False)
+        quantize_we(0, 0, 1)
+        quantize_we(0, 1, PACK)
         for j in range(HALVES):
-            gather_words(fold_cols, fold_words, fold_list, j)
             for t in range(PACK):
                 evidence_tile(0, j, t)
+
+        wm_raw = held([P, 2 * H], U8, "wm_raw", after="we_part0")
+        nc.sync.dma_start(out=wm_raw[:].bitcast(I32), in_=wm_words[0].bitcast(I32))
+        wm_raw_plane = held([P, H], U8, "wm_raw_plane", after="fold_words")
+        load_scale_rows(wm_raw_plane[:], wm_scales[0])
+        query_words = held([P, T], U32, "query_words", after="fold_picked")
+        load_words(query_words, tab2_words)
+
+        gather_scales(query_plane, query_bytes, query_list, "query_picked", QUAD // GROUP, after="we_bf0")
+        we_bf.append(held([P, PACK, P, PACK], BF16, "we_bf1", after="we_part1"))
         nc.vector.tensor_copy(
             we_bf[1][:].rearrange("p t m i -> p m i t"),
             we_second[:].rearrange("p i (m t) -> p m i t", t=PACK),
@@ -182,14 +190,17 @@ def tile_list_fold_match_evidence_kernel(
             wm_codes[:].bitcast(U16).rearrange("p (g t m) -> p g t m", g=R_PASSES, t=PACK),
             wm_raw[:].bitcast(U16).rearrange("p (g m t) -> p g t m", g=R_PASSES, t=PACK),
         )
-        quantize_we(1)
-        for t in range(PACK):
-            evidence_tile(1, 0, t)
-        wm_plane = held([P, H], U8, "wm_plane", after="fold_words")
+        quantize_we(1, 0, PACK)
+        for j in range(HALVES):
+            for t in range(PACK):
+                evidence_tile(1, j, t)
+        wm_plane = held([P, H], U8, "wm_plane", after="we_part1")
         nc.vector.tensor_copy(
             wm_plane[:].rearrange("p (g t m) -> p g t m", g=R_PASSES, t=PACK),
             wm_raw_plane[:].rearrange("p (g m t) -> p g t m", g=R_PASSES, t=PACK),
         )
+        query_cols = [held([P, HALF], U32, "query_cols0", after="fold_words"),
+                      held([P, HALF], U32, "query_cols1", after="we_part0")]
         gather_words(query_cols, query_words, query_list, 0)
         gather_words(query_cols, query_words, query_list, 1)
 
@@ -218,7 +229,7 @@ def tile_list_fold_match_evidence_kernel(
         def copy_b(n, u):
             j, g, t = pairs[n]
             b = wm_product(g, t + u, query_cols, query_plane[:, j * HALF:(j + 1) * HALF], j)
-            if n == SCALAR_B_PAIR:
+            if (n, u) in SCALAR_B:
                 nc.scalar.copy(b_place(n, u), b[:])
             else:
                 nc.vector.tensor_copy(b_place(n, u), b[:])
@@ -246,32 +257,24 @@ def tile_list_fold_match_evidence_kernel(
         def square_roots(roots):
             nc.scalar.activation(roots, roots, ACT.Square)
 
-        for u in range(2):
-            copy_b(0, u)
-        for u in range(2):
-            evidence_tile(1, 1, u)
-            subtract(0, u)
-            square(0, 0, u, u + 1)
-        for u in range(2):
-            evidence_tile(1, 1, 2 + u)
-            copy_b(1, u)
-        for n in range(1, len(pairs)):
-            if n + 1 == SCALAR_B_PAIR:
-                for u in range(2):
-                    copy_b(n + 1, u)
-            if n not in (1, SCALAR_B_PAIR):
-                for u in range(2):
+        for n, (j, g, t) in enumerate(pairs):
+            for u in range(2):
+                if (n, u) not in SCALAR_B:
                     copy_b(n, u)
-            j, g, t = pairs[n]
+            if n == 1:
+                for m, u in SCALAR_B:
+                    copy_b(m, u)
             subtract(n, 0)
-            if n in (1, last_pair - 1):
+            if n in (0, 1, last_pair - 1):
                 square(j, g, t, t + 1)
             subtract(n, 1)
+            if n == 0:
+                square(j, g, t + 1, t + 2)
             if 1 < n < last_pair - 1:
                 square(j, g, t, t + 2, aside=(n == last_pair - 2))
 
-        wc_codes = held([P, R_PASSES, N], U32, "wc_codes", after="fold_picked")
-        wc_plane = held([P, R_PASSES, N], U8, "wc_plane", after="query_picked")
+        wc_codes = held([P, R_PASSES, N], U32, "wc_codes", after="we_bf0")
+        wc_plane = held([P, R_PASSES, N], U8, "wc_plane", after="query_bytes")
         nc.sync.dma_start(
             out=wc_codes[:].bitcast(I32),
             in_=wc_words.rearrange("g p n i -> p g (n i)").bitcast(I32),

@@ -32,7 +32,8 @@ SCALAR_COLS = 384
 STEPS = (QUARTER,) * (S // QUARTER)
 LINE = 4
 BANKS = 8
-SCALAR_B = ((2, 0), (2, 1), (3, 0))
+TABLE_HOLD = 2
+SCALAR_B = (3, 4, 5)
 TINY = 2.0 ** -120
 
 
@@ -61,12 +62,12 @@ def tile_list_fold_match_evidence_kernel(
         fold_bytes = held([P, T], U8, "fold_bytes")
         query_bytes = held([P, T], U8, "query_bytes")
         fold_plane = held([P, S], U8, "fold_plane")
-        query_plane = held([P, S], U8, "query_plane")
+        query_plane = [held([P, HALF], U8, "query_plane%d" % j) for j in range(HALVES)]
         gain_cols = held([P, R_PASSES, PACK], F32, "gain_cols")
 
         for p0, p1 in ((QUAD, 2 * QUAD), (2 * QUAD, P)):
             nc.vector.memset(query_bytes[p0:p1, :].bitcast(I32), 0)
-        for plane in (fold_plane, query_plane):
+        for plane in [fold_plane] + query_plane:
             nc.vector.memset(plane[:].bitcast(I32), 0)
 
         we_parts = [held([P, PACK, WE_COLS], F32, "we_part%d" % part) for part in range(PASS // WE_COLS)]
@@ -91,14 +92,14 @@ def tile_list_fold_match_evidence_kernel(
             in_=tab_scales[0].bitcast(I32).unsqueeze(1).to_broadcast([P // BLOCK_ROWS, BLOCK_ROWS, T // 4]),
         )
         nc.sync.dma_start(out=gain_cols[:], in_=gain.rearrange("(g p t) -> p g t", p=P, t=PACK))
-        load_words(fold_words, tab_words)
-        for part in range(PASS // WE_COLS):
-            load_we(we_parts[part][:], part * WE_COLS, WE_COLS)
         nc.sync.dma_start(query_list[:], offs2)
         nc.sync.dma_start(
             out=query_bytes[0:QUAD, :].bitcast(I32),
             in_=tab2_scales[0].bitcast(I32).unsqueeze(1).to_broadcast([GROUP, QUAD // GROUP, T // 4]),
         )
+        load_words(fold_words, tab_words)
+        for part in range(PASS // WE_COLS):
+            load_we(we_parts[part][:], part * WE_COLS, WE_COLS)
 
         gain_flat = gain_cols[:].rearrange("p g t -> p (g t)")
         row_factor = held([P, R_PASSES * PACK], F32, "row_factor")
@@ -106,9 +107,9 @@ def tile_list_fold_match_evidence_kernel(
         nc.scalar.activation(row_factor[:], gain_flat, ACT.Sign)
         nc.scalar.activation(gain_squared[:], gain_flat, ACT.Square)
 
-        def gather_scales(plane, window, picks, name, row_step, after=""):
-            picked = held([P, S], U8, name, after=after)
-            nc.vector.tensor_copy(picked[:], window[:].indirect(picks[:]))
+        def gather_scales(plane, window, picks, name, row_step, j0, j1, after=""):
+            picked = held([P, j1 - j0], U8, name, after=after)
+            nc.vector.tensor_copy(picked[:], window[:].indirect(picks[:, j0 // GROUP:j1 // GROUP]))
             for d in range(QUADS):
                 rows = picked[4 * d * row_step:4 * (d + 1) * row_step:row_step, :]
                 nc.sync.dma_start(out=plane[QUAD * d:QUAD * d + 4, :].bitcast(I32), in_=rows.bitcast(I32))
@@ -117,12 +118,12 @@ def tile_list_fold_match_evidence_kernel(
             per_half = HALF // GROUP
             nc.vector.tensor_copy(dst[j][:], words[:].indirect(picks[:, j * per_half:(j + 1) * per_half]))
 
-        gather_scales(fold_plane, fold_bytes, fold_list, "fold_picked", BLOCK_ROWS)
+        gather_scales(fold_plane, fold_bytes, fold_list, "fold_picked", BLOCK_ROWS, 0, S)
         we_second = held([P, PACK, PASS], F32, "we_second", after="fold_bytes")
         load_we(we_second[:], PASS, PASS)
-        fold_cols = [held([P, HALF], U32, "fold_cols%d" % j) for j in range(HALVES)]
-        for j in range(HALVES):
-            gather_words(fold_cols, fold_words, fold_list, j)
+        fold_cols = [held([P, HALF], U32, "fold_cols0")]
+        gather_words(fold_cols, fold_words, fold_list, 0)
+        gather_scales(query_plane[0], query_bytes, query_list, "query_picked0", QUAD // GROUP, 0, HALF)
 
         we_bf = [held([P, PACK, P, PACK], BF16, "we_bf0")]
         we_codes = [held([P, PASS], U32, "we_codes%d" % g) for g in range(R_PASSES)]
@@ -168,46 +169,53 @@ def tile_list_fold_match_evidence_kernel(
         round_we_first(SCALAR_COLS, PASS, False)
         quantize_we(0, 0, 1)
         quantize_we(0, 1, PACK)
+        fold_cols.append(held([P, HALF], U32, "fold_cols1", after="we_bf0"))
+        gather_words(fold_cols, fold_words, fold_list, 1)
         for j in range(HALVES):
             for t in range(PACK):
                 evidence_tile(0, j, t)
 
         wm_raw = held([P, 2 * H], U8, "wm_raw", after="we_part0")
         nc.sync.dma_start(out=wm_raw[:].bitcast(I32), in_=wm_words[0].bitcast(I32))
-        wm_raw_plane = held([P, H], U8, "wm_raw_plane", after="fold_words")
-        load_scale_rows(wm_raw_plane[:], wm_scales[0])
         query_words = held([P, T], U32, "query_words", after="fold_picked")
         load_words(query_words, tab2_words)
+        wm_raw_plane = held([P, H], U8, "wm_raw_plane", after="we_part1")
+        load_scale_rows(wm_raw_plane[:], wm_scales[0])
 
-        gather_scales(query_plane, query_bytes, query_list, "query_picked", QUAD // GROUP, after="we_bf0")
-        we_bf.append(held([P, PACK, P, PACK], BF16, "we_bf1", after="we_part1"))
+        we_bf.append(held([P, PACK, P, PACK], BF16, "we_bf1", after="fold_words"))
         nc.vector.tensor_copy(
             we_bf[1][:].rearrange("p t m i -> p m i t"),
             we_second[:].rearrange("p i (m t) -> p m i t", t=PACK),
-        )
-        wm_codes = held([P, 2 * H], U8, "wm_codes", after="fold_bytes")
-        nc.vector.tensor_copy(
-            wm_codes[:].bitcast(U16).rearrange("p (g t m) -> p g t m", g=R_PASSES, t=PACK),
-            wm_raw[:].bitcast(U16).rearrange("p (g m t) -> p g t m", g=R_PASSES, t=PACK),
         )
         quantize_we(1, 0, PACK)
         for j in range(HALVES):
             for t in range(PACK):
                 evidence_tile(1, j, t)
-        wm_plane = held([P, H], U8, "wm_plane", after="we_part1")
-        nc.vector.tensor_copy(
-            wm_plane[:].rearrange("p (g t m) -> p g t m", g=R_PASSES, t=PACK),
-            wm_raw_plane[:].rearrange("p (g m t) -> p g t m", g=R_PASSES, t=PACK),
-        )
-        query_cols = [held([P, HALF], U32, "query_cols0", after="fold_words"),
-                      held([P, HALF], U32, "query_cols1", after="we_part0")]
+        wm_both = held([P, 3 * H], U8, "wm_both", after="fold_words")
+        wm_codes = wm_both[:, 0:2 * H]
+        wm_plane = wm_both[:, 2 * H:3 * H]
+        for g in range(R_PASSES):
+            cols = slice(g * PASS, (g + 1) * PASS)
+            pairs_of_bytes = slice(2 * g * PASS, 2 * (g + 1) * PASS)
+            nc.gpsimd.tensor_copy(
+                wm_codes[:, pairs_of_bytes].rearrange("p (t m b) -> p t m b", t=PACK, b=2),
+                wm_raw[:, pairs_of_bytes].rearrange("p (m t b) -> p t m b", t=PACK, b=2),
+            )
+            nc.gpsimd.tensor_copy(
+                wm_plane[:, cols].rearrange("p (t m) -> p t m", t=PACK),
+                wm_raw_plane[:, cols].rearrange("p (m t) -> p t m", t=PACK),
+            )
+        gather_scales(query_plane[1], query_bytes, query_list, "query_picked1", QUAD // GROUP, HALF, S,
+                      after="fold_bytes")
+        query_cols = [held([P, HALF], U32, "query_cols0", after="query_bytes"),
+                      held([P, HALF], U32, "query_cols1", after="query_picked0")]
         gather_words(query_cols, query_words, query_list, 0)
         gather_words(query_cols, query_words, query_list, 1)
 
-        pairs = [(j, g, t) for j in range(HALVES) for g in range(R_PASSES) for t in range(0, PACK, 2)]
-        last_pair = len(pairs) - 1
+        tiles = [(j, g, t) for j in range(HALVES) for g in range(R_PASSES) for t in range(PACK)]
+        last_tile = len(tiles) - 1
         squared = {}
-        b_apart = {(1, 0): held([P, HALF], F32, "b_third"), (last_pair, 1): held([P, HALF], F32, "b_last")}
+        b_apart = {TABLE_HOLD: held([P, HALF], F32, "b_hold"), last_tile: held([P, HALF], F32, "b_last")}
 
         def wm_product(g, t, picked, plane, j):
             acc = next_bank(HALF)
@@ -222,59 +230,57 @@ def tile_list_fold_match_evidence_kernel(
             )
             return acc
 
-        def b_place(n, u):
-            j, g, t = pairs[n]
-            return b_apart[(n, u)][:] if (n, u) in b_apart else match[g][j][:, t + u, :]
+        def b_place(k):
+            j, g, t = tiles[k]
+            return b_apart[k][:] if k in b_apart else match[g][j][:, t, :]
 
-        def copy_b(n, u):
-            j, g, t = pairs[n]
-            b = wm_product(g, t + u, query_cols, query_plane[:, j * HALF:(j + 1) * HALF], j)
-            if (n, u) in SCALAR_B:
-                nc.scalar.copy(b_place(n, u), b[:])
+        def copy_b(k):
+            j, g, t = tiles[k]
+            b = wm_product(g, t, query_cols, query_plane[j][:], j)
+            if k in SCALAR_B:
+                nc.scalar.copy(b_place(k), b[:])
             else:
-                nc.vector.tensor_copy(b_place(n, u), b[:])
+                nc.vector.tensor_copy(b_place(k), b[:])
 
-        def subtract(n, u):
-            j, g, t = pairs[n]
-            a = wm_product(g, t + u, fold_cols, fold_plane[:, j * HALF:(j + 1) * HALF], j)
-            nc.vector.tensor_tensor(match[g][j][:, t + u, :], b_place(n, u), a[:], ALU.subtract)
+        def subtract(k):
+            j, g, t = tiles[k]
+            a = wm_product(g, t, fold_cols, fold_plane[:, j * HALF:(j + 1) * HALF], j)
+            nc.vector.tensor_tensor(match[g][j][:, t, :], b_place(k), a[:], ALU.subtract)
 
-        def square(j, g, t0, t1, on_scalar=False, aside=False):
-            differences = match[g][j][:, t0:t1, :]
-            dst = held([P, t1 - t0, HALF], F32, "squares_aside")[:] if aside else differences
+        def square(k0, k1, on_scalar=False, aside=False):
+            j, g, t0 = tiles[k0]
+            differences = match[g][j][:, t0:t0 + k1 - k0, :]
+            dst = held([P, k1 - k0, HALF], F32, "squares_aside")[:] if aside else differences
             if on_scalar:
                 nc.scalar.activation(dst, differences, ACT.Square)
             else:
                 nc.gpsimd.tensor_tensor(dst, differences, differences, ALU.mult)
-            for t in range(t0, t1):
-                squared[(j, g, t)] = dst[:, t - t0, :]
+            for k in range(k0, k1):
+                squared[k] = dst[:, k - k0, :]
 
-        def inverse_root(j, g, t):
+        def inverse_root(k):
+            j, g, t = tiles[k]
             inv = gain_inv[:, g * PACK + t:g * PACK + t + 1]
-            nc.scalar.activation(match[g][j][:, t, :], squared[(j, g, t)], ACT.Abs_reciprocal_sqrt,
-                                 bias=inv, scale=inv)
+            nc.scalar.activation(match[g][j][:, t, :], squared[k], ACT.Abs_reciprocal_sqrt, bias=inv, scale=inv)
 
         def square_roots(roots):
             nc.scalar.activation(roots, roots, ACT.Square)
 
-        for n, (j, g, t) in enumerate(pairs):
-            for u in range(2):
-                if (n, u) not in SCALAR_B:
-                    copy_b(n, u)
-            if n == 1:
-                for m, u in SCALAR_B:
-                    copy_b(m, u)
-            subtract(n, 0)
-            if n in (0, 1, last_pair - 1):
-                square(j, g, t, t + 1)
-            subtract(n, 1)
-            if n == 0:
-                square(j, g, t + 1, t + 2)
-            if 1 < n < last_pair - 1:
-                square(j, g, t, t + 2, aside=(n == last_pair - 2))
+        copy_b(0)
+        for k in range(len(tiles)):
+            if k < last_tile and k + 1 not in SCALAR_B:
+                copy_b(k + 1)
+            subtract(k)
+            if k + 2 == SCALAR_B[0]:
+                for m in SCALAR_B:
+                    copy_b(m)
+            if k < PACK - 1 or k == 3 * PACK:
+                square(k, k + 1)
+            elif PACK <= k < 3 * PACK and k % 2 == 1:
+                square(k - 1, k + 1, aside=(k == 3 * PACK - 1))
 
-        wc_codes = held([P, R_PASSES, N], U32, "wc_codes", after="we_bf0")
-        wc_plane = held([P, R_PASSES, N], U8, "wc_plane", after="query_bytes")
+        wc_codes = held([P, R_PASSES, N], U32, "wc_codes", after="fold_picked")
+        wc_plane = held([P, R_PASSES, N], U8, "wc_plane", after="we_part1")
         nc.sync.dma_start(
             out=wc_codes[:].bitcast(I32),
             in_=wc_words.rearrange("g p n i -> p g (n i)").bitcast(I32),
@@ -282,69 +288,88 @@ def tile_list_fold_match_evidence_kernel(
         for g in range(R_PASSES):
             load_scale_rows(wc_plane[:, g, :], wc_scales[g])
 
-        gain_inv = held([P, R_PASSES * PACK], F32, "gain_inv", after="b_third")
+        gain_inv = held([P, R_PASSES * PACK], F32, "gain_inv", after="b_hold")
         nc.scalar.activation(gain_inv[:], gain_squared[:], ACT.Abs_reciprocal_sqrt, bias=TINY)
-        for n in range(len(pairs) - 2):
-            j, g, t = pairs[n]
-            for u in range(2):
-                inverse_root(j, g, t + u)
-            if n == 0:
-                square(0, 0, PACK - 1, PACK, on_scalar=True)
-            square_roots(match[g][j][:, t:t + 2, :])
-        square(HALVES - 1, R_PASSES - 1, 1, PACK, on_scalar=True, aside=True)
-        for t in range(PACK):
-            inverse_root(HALVES - 1, R_PASSES - 1, t)
-        last_roots = match[R_PASSES - 1][HALVES - 1]
-        square_roots(last_roots[:, :, 0:QUARTER])
+
+        def group_roots(n):
+            j, g, t = tiles[n * PACK]
+            return match[g][j]
+
+        for k in range(3 * PACK):
+            inverse_root(k)
+            if k == 1:
+                square(PACK - 1, PACK, on_scalar=True)
+            if k == 3 * PACK - 1:
+                square(3 * PACK + 1, 4 * PACK, on_scalar=True, aside=True)
+            if k % 2 == 1:
+                square_roots(group_roots(k // PACK)[:, k % PACK - 1:k % PACK + 1, :])
+        for k in range(3 * PACK, 4 * PACK):
+            inverse_root(k)
+        last_roots = group_roots(3)
 
         n_tiles = N // P
-        j0 = 0
+        steps = S // QUARTER
         h_shape = [P, HALF // QUARTER, R_PASSES, QUARTER, PACK]
         h_halves = [held(h_shape, BF16, "h_half0", after="b_last"), held(h_shape, BF16, "h_half1")]
         results = [held([P, HALF // QUARTER, n_tiles, QUARTER], F32, "results0", after="squares_aside"),
                    held([P, HALF // QUARTER, n_tiles, QUARTER], F32, "results1")]
-        for step, width in enumerate(STEPS):
-            j, c0 = divmod(j0, HALF)
-            cols = slice(c0, c0 + width)
-            last = step == len(STEPS) - 1
-            h_step = h_halves[j][:, c0 // QUARTER]
-            for g in range(R_PASSES):
-                nc.vector.tensor_tensor(
-                    h_step[:, g].rearrange("p (c i) t -> p c t i", i=LINE),
-                    match[g][j][:, :, cols].rearrange("p t (c i) -> p c t i", i=LINE),
-                    evidence[g][j][:, :, cols].rearrange("p t (c i) -> p c t i", i=LINE),
-                    ALU.mult,
-                )
-            h_codes = [held([P, width], U32, "h_codes%d%d" % (step, g)) for g in range(R_PASSES)]
-            h_plane = [held([P, width], U8, "h_plane%d%d" % (step, g)) for g in range(R_PASSES)]
-            for g in range(R_PASSES):
-                nc.vector.quantize_mx(out=h_codes[g][:].bitcast(FP8X4), scales=h_plane[g][:],
-                                      in_=h_step[:, g].rearrange("p j t -> p (j t)"))
+        h_codes = [[held([P, QUARTER], U32, "h_codes%d%d" % (step, g)) for g in range(R_PASSES)]
+                   for step in range(steps)]
+        h_plane = [[held([P, QUARTER], U8, "h_plane%d%d" % (step, g)) for g in range(R_PASSES)]
+                   for step in range(steps)]
+        banks = {}
 
-            per_bank = 1 if last else HALF // width
-            banks = [next_bank(per_bank * width) for n in range(0, n_tiles, per_bank)]
-            for place in range(per_bank):
-                for g in range(R_PASSES):
-                    for u, bank in enumerate(banks):
-                        n0 = (u * per_bank + place) * P
-                        nc.tensor.matmul_mx(
-                            out=bank[:, place * width:(place + 1) * width],
-                            lhsT=wc_codes[:, g, n0:n0 + P].bitcast(FP8X4),
-                            lhsT_scale=wc_plane[:, g, n0:n0 + P],
-                            rhs=h_codes[g][:].bitcast(FP8X4),
-                            rhs_scale=h_plane[g][:],
-                            start=(g == 0), stop=(g == R_PASSES - 1),
-                        )
+        def h_step(step):
+            return h_halves[step * QUARTER // HALF][:, step % (HALF // QUARTER)]
+
+        def product(step, g):
+            j, c0 = divmod(step * QUARTER, HALF)
+            cols = slice(c0, c0 + QUARTER)
+            nc.vector.tensor_tensor(
+                h_step(step)[:, g].rearrange("p (c i) t -> p c t i", i=LINE),
+                match[g][j][:, :, cols].rearrange("p t (c i) -> p c t i", i=LINE),
+                evidence[g][j][:, :, cols].rearrange("p t (c i) -> p c t i", i=LINE),
+                ALU.mult,
+            )
+
+        def quantize_and_multiply(step, g):
+            nc.vector.quantize_mx(out=h_codes[step][g][:].bitcast(FP8X4), scales=h_plane[step][g][:],
+                                  in_=h_step(step)[:, g].rearrange("p j t -> p (j t)"))
+            per_bank = 1 if step == steps - 1 else HALF // QUARTER
+            if g == 0:
+                banks[step] = [next_bank(per_bank * QUARTER) for n in range(0, n_tiles, per_bank)]
+            for u, bank in enumerate(banks[step]):
+                for place in range(per_bank):
+                    n0 = (u * per_bank + place) * P
+                    nc.tensor.matmul_mx(
+                        out=bank[:, place * QUARTER:(place + 1) * QUARTER],
+                        lhsT=wc_codes[:, g, n0:n0 + P].bitcast(FP8X4),
+                        lhsT_scale=wc_plane[:, g, n0:n0 + P],
+                        rhs=h_codes[step][g][:].bitcast(FP8X4),
+                        rhs_scale=h_plane[step][g][:],
+                        start=(g == 0 and place == 0), stop=(g == R_PASSES - 1 and place == per_bank - 1),
+                    )
+
+        def store(step, n):
+            last = step == steps - 1
+            j, c0 = divmod(step * QUARTER, HALF)
+            result = results[j][:, c0 // QUARTER, n:n + 2, :]
+            if last:
+                nc.scalar.copy(result[:, 0, :], banks[step][n][:])
+                nc.vector.tensor_copy(result[:, 1, :], banks[step][n + 1][:])
+            else:
+                nc.scalar.copy(result.rearrange("p u j -> p (u j)"), banks[step][n // 2][:])
+            dst = out[n * P:(n + 2) * P, step * QUARTER:(step + 1) * QUARTER]
+            queue = nc.scalar if last and n > 0 else nc.sync
+            queue.dma_start(out=dst.rearrange("(u p) j -> p u j", p=P), in_=result)
+
+        square_roots(last_roots[:, :, 0:QUARTER])
+        for step in range(steps):
+            for g in range(R_PASSES):
+                product(step, g)
+            for g in range(R_PASSES):
+                quantize_and_multiply(step, g)
             for n in range(0, n_tiles, 2):
-                result = results[j][:, c0 // QUARTER, n:n + 2, :]
-                if last:
-                    nc.scalar.copy(result[:, 0, :], banks[n][:])
-                    nc.vector.tensor_copy(result[:, 1, :], banks[n + 1][:])
-                else:
-                    nc.scalar.copy(result.rearrange("p u j -> p (u j)"), banks[n // per_bank][:])
-                dst = out[n * P:(n + 2) * P, j0:j0 + width]
-                queue = nc.scalar if last and n > 0 else nc.sync
-                queue.dma_start(out=dst.rearrange("(u p) j -> p u j", p=P), in_=result)
+                store(step, n)
             if step == 0:
                 square_roots(last_roots[:, :, QUARTER:HALF])
-            j0 += width

@@ -30,10 +30,12 @@ QUARTER = 256
 WE_COLS = 256
 SCALAR_COLS = 384
 STEPS = (QUARTER,) * (S // QUARTER)
+EARLY_SCALES = 768
+WE_BYTES = PACK * PASS * 4
 LINE = 4
 BANKS = 8
-TABLE_HOLD = 2
-SCALAR_B = (3, 4, 5)
+TABLE_HOLD = 3
+SCALAR_B = (4, 5, 6)
 TINY = 2.0 ** -120
 
 
@@ -45,6 +47,7 @@ def tile_list_fold_match_evidence_kernel(
     with ExitStack() as ctx:
         lists = ctx.enter_context(tc.tile_pool(name="lists", bufs=1))
         keep = ctx.enter_context(tc.tile_pool(name="keep", bufs=1))
+        reused = ctx.enter_context(tc.tile_pool(name="reused", bufs=1))
         psum = ctx.enter_context(tc.psum_pool(name="psum", bufs=1))
         taken = []
 
@@ -56,22 +59,25 @@ def tile_list_fold_match_evidence_kernel(
         def held(shape, dtype, name, after=""):
             return keep.tile(shape, dtype, name=name, tag=after or name, align_bytes=64)
 
+        def placed(shape, dtype, name, offset):
+            return reused.tile(shape, dtype, name=name, offset=offset, align_bytes=64)
+
         fold_list = lists.tile([P, S // GROUP], U16, name="fold_list")
         query_list = lists.tile([P, S // GROUP], U16, name="query_list")
 
-        fold_bytes = held([P, T], U8, "fold_bytes")
+        fold_bytes = placed([P, T], U8, "fold_bytes", WE_BYTES - T // 2)
         query_bytes = held([P, T], U8, "query_bytes")
         fold_plane = held([P, S], U8, "fold_plane")
-        query_plane = [held([P, HALF], U8, "query_plane%d" % j) for j in range(HALVES)]
+        query_plane = [held([P, HALF], U8, "query_plane0")]
         gain_cols = held([P, R_PASSES, PACK], F32, "gain_cols")
 
         for p0, p1 in ((QUAD, 2 * QUAD), (2 * QUAD, P)):
             nc.vector.memset(query_bytes[p0:p1, :].bitcast(I32), 0)
-        for plane in [fold_plane] + query_plane:
+        for plane in (fold_plane, query_plane[0]):
             nc.vector.memset(plane[:].bitcast(I32), 0)
 
         we_parts = [held([P, PACK, WE_COLS], F32, "we_part%d" % part) for part in range(PASS // WE_COLS)]
-        fold_words = held([P, T], U32, "fold_words")
+        fold_words = placed([P, T], U32, "fold_words", 2 * WE_BYTES)
 
         def load_we(dst, c0, width):
             nc.sync.dma_start(out=dst, in_=we[:, c0:c0 + width].rearrange("(p i) w -> p i w", i=PACK))
@@ -97,9 +103,9 @@ def tile_list_fold_match_evidence_kernel(
             out=query_bytes[0:QUAD, :].bitcast(I32),
             in_=tab2_scales[0].bitcast(I32).unsqueeze(1).to_broadcast([GROUP, QUAD // GROUP, T // 4]),
         )
-        load_words(fold_words, tab_words)
         for part in range(PASS // WE_COLS):
             load_we(we_parts[part][:], part * WE_COLS, WE_COLS)
+        load_words(fold_words, tab_words)
 
         gain_flat = gain_cols[:].rearrange("p g t -> p (g t)")
         row_factor = held([P, R_PASSES * PACK], F32, "row_factor")
@@ -107,9 +113,10 @@ def tile_list_fold_match_evidence_kernel(
         nc.scalar.activation(row_factor[:], gain_flat, ACT.Sign)
         nc.scalar.activation(gain_squared[:], gain_flat, ACT.Square)
 
-        def gather_scales(plane, window, picks, name, row_step, j0, j1, after=""):
-            picked = held([P, j1 - j0], U8, name, after=after)
+        def gather_scales(picked, window, picks, j0, j1):
             nc.vector.tensor_copy(picked[:], window[:].indirect(picks[:, j0 // GROUP:j1 // GROUP]))
+
+        def move_scales(plane, picked, row_step):
             for d in range(QUADS):
                 rows = picked[4 * d * row_step:4 * (d + 1) * row_step:row_step, :]
                 nc.sync.dma_start(out=plane[QUAD * d:QUAD * d + 4, :].bitcast(I32), in_=rows.bitcast(I32))
@@ -118,12 +125,17 @@ def tile_list_fold_match_evidence_kernel(
             per_half = HALF // GROUP
             nc.vector.tensor_copy(dst[j][:], words[:].indirect(picks[:, j * per_half:(j + 1) * per_half]))
 
-        gather_scales(fold_plane, fold_bytes, fold_list, "fold_picked", BLOCK_ROWS, 0, S)
-        we_second = held([P, PACK, PASS], F32, "we_second", after="fold_bytes")
+        fold_picked = held([P, S], U8, "fold_picked")
+        gather_scales(fold_picked, fold_bytes, fold_list, 0, S)
+        move_scales(fold_plane[:], fold_picked[:], BLOCK_ROWS)
+        wm_raw = placed([P, 2 * H], U8, "wm_raw", WE_BYTES)
+        nc.sync.dma_start(out=wm_raw[:].bitcast(I32), in_=wm_words[0].bitcast(I32))
+        we_second = placed([P, PACK, PASS], F32, "we_second", 0)
         load_we(we_second[:], PASS, PASS)
         fold_cols = [held([P, HALF], U32, "fold_cols0")]
-        gather_words(fold_cols, fold_words, fold_list, 0)
-        gather_scales(query_plane[0], query_bytes, query_list, "query_picked0", QUAD // GROUP, 0, HALF)
+        early_picked = held([P, EARLY_SCALES], U8, "early_picked")
+        gather_scales(early_picked, query_bytes, query_list, 0, EARLY_SCALES)
+        move_scales(query_plane[0][:], early_picked[:, 0:HALF], QUAD // GROUP)
 
         we_bf = [held([P, PACK, P, PACK], BF16, "we_bf0")]
         we_codes = [held([P, PASS], U32, "we_codes%d" % g) for g in range(R_PASSES)]
@@ -150,39 +162,55 @@ def tile_list_fold_match_evidence_kernel(
         match = [[held([P, PACK, HALF], F32, "match%d%d" % (g, j)) for j in range(HALVES)]
                  for g in range(R_PASSES)]
 
-        def evidence_tile(g, j, t):
-            e = next_bank(HALF)
+        def evidence_tile(g, j, t, c0=0, c1=HALF):
+            e = next_bank(c1 - c0)
             nc.tensor.matmul_mx(
                 out=e[:],
                 lhsT=we_codes[g][:, t * P:(t + 1) * P].bitcast(FP8X4),
                 lhsT_scale=we_plane[g][:, t * P:(t + 1) * P],
-                rhs=fold_cols[j][:].bitcast(FP8X4),
-                rhs_scale=fold_plane[:, j * HALF:(j + 1) * HALF],
+                rhs=fold_cols[j][:, c0:c1].bitcast(FP8X4),
+                rhs_scale=fold_plane[:, j * HALF + c0:j * HALF + c1],
                 start=True, stop=True,
             )
             tile_no = g * PACK + t
-            nc.scalar.activation(evidence[g][j][:, t, :], e[:], ACT.Tanh,
+            nc.scalar.activation(evidence[g][j][:, t, c0:c1], e[:], ACT.Tanh,
                                  scale=row_factor[:, tile_no:tile_no + 1])
 
         round_we_first(0, WE_COLS, True)
-        round_we_first(WE_COLS, SCALAR_COLS, True)
-        round_we_first(SCALAR_COLS, PASS, False)
-        quantize_we(0, 0, 1)
-        quantize_we(0, 1, PACK)
-        fold_cols.append(held([P, HALF], U32, "fold_cols1", after="we_bf0"))
+        round_we_first(WE_COLS, PASS, True)
+        quantize_we(0, 0, PACK)
+        for c0 in (0, QUARTER):
+            nc.vector.tensor_copy(fold_cols[0][:, c0:c0 + QUARTER],
+                                  fold_words[:].indirect(fold_list[:, c0 // GROUP:(c0 + QUARTER) // GROUP]))
+            for t in range(2):
+                evidence_tile(0, 0, t, c0, c0 + QUARTER)
+        fold_cols.append(held([P, HALF], U32, "fold_cols1"))
         gather_words(fold_cols, fold_words, fold_list, 1)
         for j in range(HALVES):
-            for t in range(PACK):
+            for t in range(2 if j == 0 else 0, PACK):
                 evidence_tile(0, j, t)
 
-        wm_raw = held([P, 2 * H], U8, "wm_raw", after="we_part0")
-        nc.sync.dma_start(out=wm_raw[:].bitcast(I32), in_=wm_words[0].bitcast(I32))
         query_words = held([P, T], U32, "query_words", after="fold_picked")
         load_words(query_words, tab2_words)
         wm_raw_plane = held([P, H], U8, "wm_raw_plane", after="we_part1")
         load_scale_rows(wm_raw_plane[:], wm_scales[0])
 
-        we_bf.append(held([P, PACK, P, PACK], BF16, "we_bf1", after="fold_words"))
+        def reorder_words(g):
+            nc.gpsimd.tensor_copy(
+                wm_codes[g].rearrange("p (t m b) -> p t m b", t=PACK, b=2),
+                wm_raw[:, 2 * g * PASS:2 * (g + 1) * PASS].rearrange("p (m t b) -> p t m b", t=PACK, b=2),
+            )
+
+        def reorder_plane(g):
+            cols = slice(g * PASS, (g + 1) * PASS)
+            nc.gpsimd.tensor_copy(
+                wm_plane[:, cols].rearrange("p (t m) -> p t m", t=PACK),
+                wm_raw_plane[:, cols].rearrange("p (m t) -> p t m", t=PACK),
+            )
+
+        wm_codes = [held([P, H], U8, "wm_early", after="we_bf0")[:]]
+        reorder_words(0)
+        we_bf.append(placed([P, PACK, P, PACK], BF16, "we_bf1", 2 * WE_BYTES))
         nc.vector.tensor_copy(
             we_bf[1][:].rearrange("p t m i -> p m i t"),
             we_second[:].rearrange("p i (m t) -> p m i t", t=PACK),
@@ -191,38 +219,34 @@ def tile_list_fold_match_evidence_kernel(
         for j in range(HALVES):
             for t in range(PACK):
                 evidence_tile(1, j, t)
-        wm_both = held([P, 3 * H], U8, "wm_both", after="fold_words")
-        wm_codes = wm_both[:, 0:2 * H]
-        wm_plane = wm_both[:, 2 * H:3 * H]
-        for g in range(R_PASSES):
-            cols = slice(g * PASS, (g + 1) * PASS)
-            pairs_of_bytes = slice(2 * g * PASS, 2 * (g + 1) * PASS)
-            nc.gpsimd.tensor_copy(
-                wm_codes[:, pairs_of_bytes].rearrange("p (t m b) -> p t m b", t=PACK, b=2),
-                wm_raw[:, pairs_of_bytes].rearrange("p (m t b) -> p t m b", t=PACK, b=2),
-            )
-            nc.gpsimd.tensor_copy(
-                wm_plane[:, cols].rearrange("p (t m) -> p t m", t=PACK),
-                wm_raw_plane[:, cols].rearrange("p (m t) -> p t m", t=PACK),
-            )
-        gather_scales(query_plane[1], query_bytes, query_list, "query_picked1", QUAD // GROUP, HALF, S,
-                      after="fold_bytes")
+        query_plane.append(placed([P, HALF], U8, "query_plane1", 2 * WE_BYTES + 2 * H))
+        wm_late = placed([P, 2 * H], U8, "wm_late", 2 * WE_BYTES)
+        wm_plane = wm_late[:, 0:H]
+        wm_codes.append(wm_late[:, H:2 * H])
+        reorder_plane(0)
+        nc.gpsimd.memset(query_plane[1][:].bitcast(I32), 0)
+        reorder_words(1)
+        reorder_plane(1)
+        late_picked = placed([P, S - EARLY_SCALES], U8, "late_picked", 0)
+        gather_scales(late_picked, query_bytes, query_list, EARLY_SCALES, S)
+        move_scales(query_plane[1][:, 0:EARLY_SCALES - HALF], early_picked[:, HALF:], QUAD // GROUP)
+        move_scales(query_plane[1][:, EARLY_SCALES - HALF:], late_picked[:], QUAD // GROUP)
         query_cols = [held([P, HALF], U32, "query_cols0", after="query_bytes"),
-                      held([P, HALF], U32, "query_cols1", after="query_picked0")]
+                      held([P, HALF], U32, "query_cols1")]
         gather_words(query_cols, query_words, query_list, 0)
         gather_words(query_cols, query_words, query_list, 1)
 
         tiles = [(j, g, t) for j in range(HALVES) for g in range(R_PASSES) for t in range(PACK)]
         last_tile = len(tiles) - 1
         squared = {}
-        b_apart = {TABLE_HOLD: held([P, HALF], F32, "b_hold"), last_tile: held([P, HALF], F32, "b_last")}
+        b_apart = {TABLE_HOLD: held([P, HALF], F32, "b_hold"), last_tile: placed([P, HALF], F32, "b_last", 4 * WE_BYTES - H)}
 
         def wm_product(g, t, picked, plane, j):
             acc = next_bank(HALF)
             tile_no = g * PACK + t
             nc.tensor.matmul_mx(
                 out=acc[:],
-                lhsT=wm_codes[:, 2 * P * tile_no:2 * P * (tile_no + 1)].bitcast(FP4X4),
+                lhsT=wm_codes[g][:, 2 * P * t:2 * P * (t + 1)].bitcast(FP4X4),
                 lhsT_scale=wm_plane[:, P * tile_no:P * (tile_no + 1)],
                 rhs=picked[j][:].bitcast(FP8X4),
                 rhs_scale=plane,
@@ -271,13 +295,17 @@ def tile_list_fold_match_evidence_kernel(
             if k < last_tile and k + 1 not in SCALAR_B:
                 copy_b(k + 1)
             subtract(k)
-            if k + 2 == SCALAR_B[0]:
+            if k + 3 == SCALAR_B[0]:
                 for m in SCALAR_B:
                     copy_b(m)
-            if k < PACK - 1 or k == 3 * PACK:
+            if k < PACK - 1:
                 square(k, k + 1)
             elif PACK <= k < 3 * PACK and k % 2 == 1:
                 square(k - 1, k + 1, aside=(k == 3 * PACK - 1))
+
+        squared[3 * PACK] = placed([P, HALF], F32, "vector_squares", 4 * WE_BYTES)[:]
+        first_of_last = match[R_PASSES - 1][HALVES - 1][:, 0, :]
+        nc.vector.tensor_tensor(squared[3 * PACK], first_of_last, first_of_last, ALU.mult)
 
         wc_codes = held([P, R_PASSES, N], U32, "wc_codes", after="fold_picked")
         wc_plane = held([P, R_PASSES, N], U8, "wc_plane", after="we_part1")
@@ -310,7 +338,7 @@ def tile_list_fold_match_evidence_kernel(
         n_tiles = N // P
         steps = S // QUARTER
         h_shape = [P, HALF // QUARTER, R_PASSES, QUARTER, PACK]
-        h_halves = [held(h_shape, BF16, "h_half0", after="b_last"), held(h_shape, BF16, "h_half1")]
+        h_halves = [placed(h_shape, BF16, "h_half0", 3 * WE_BYTES), held(h_shape, BF16, "h_half1")]
         results = [held([P, HALF // QUARTER, n_tiles, QUARTER], F32, "results0", after="squares_aside"),
                    held([P, HALF // QUARTER, n_tiles, QUARTER], F32, "results1")]
         h_codes = [[held([P, QUARTER], U32, "h_codes%d%d" % (step, g)) for g in range(R_PASSES)]

@@ -22,14 +22,11 @@ PASS = P * PACK
 R_PASSES = H // PASS
 QUAD = 32
 QUADS = P // QUAD
-BLOCK_ROWS = 8
 GROUP = 16
 HALF = 512
 HALVES = S // HALF
 QUARTER = 256
 WE_COLS = 256
-SCALAR_COLS = 384
-STEPS = (QUARTER,) * (S // QUARTER)
 EARLY_SCALES = 768
 WE_BYTES = PACK * PASS * 4
 LINE = 4
@@ -71,6 +68,7 @@ def tile_list_fold_match_evidence_kernel(
         query_plane = [held([P, HALF], U8, "query_plane0")]
         gain_cols = held([P, R_PASSES, PACK], F32, "gain_cols")
 
+        nc.gpsimd.memset(fold_bytes[:].bitcast(I32), 0)
         for p0, p1 in ((QUAD, 2 * QUAD), (2 * QUAD, P)):
             nc.vector.memset(query_bytes[p0:p1, :].bitcast(I32), 0)
         for plane in (fold_plane, query_plane[0]):
@@ -93,10 +91,8 @@ def tile_list_fold_match_evidence_kernel(
                                   in_=rows.unsqueeze(0).to_broadcast([QUAD // 4, 4, rows.shape[1]]))
 
         nc.sync.dma_start(fold_list[:], offs)
-        nc.sync.dma_start(
-            out=fold_bytes[:].bitcast(I32),
-            in_=tab_scales[0].bitcast(I32).unsqueeze(1).to_broadcast([P // BLOCK_ROWS, BLOCK_ROWS, T // 4]),
-        )
+        for u in range(2):
+            nc.sync.dma_start(out=fold_bytes[u:P:GROUP, :].bitcast(I32), in_=tab_scales[0][u:GROUP:2, :].bitcast(I32))
         nc.sync.dma_start(out=gain_cols[:], in_=gain.rearrange("(g p t) -> p g t", p=P, t=PACK))
         nc.sync.dma_start(query_list[:], offs2)
         nc.sync.dma_start(
@@ -127,7 +123,9 @@ def tile_list_fold_match_evidence_kernel(
 
         fold_picked = held([P, S], U8, "fold_picked")
         gather_scales(fold_picked, fold_bytes, fold_list, 0, S)
-        move_scales(fold_plane[:], fold_picked[:], BLOCK_ROWS)
+        for r in range(4):
+            rows = fold_picked[GROUP * (r // 2) + r % 2:P:QUAD, :]
+            nc.sync.dma_start(out=fold_plane[r:P:QUAD, :].bitcast(I32), in_=rows.bitcast(I32))
         wm_raw = placed([P, 2 * H], U8, "wm_raw", WE_BYTES)
         nc.sync.dma_start(out=wm_raw[:].bitcast(I32), in_=wm_words[0].bitcast(I32))
         we_second = placed([P, PACK, PASS], F32, "we_second", 0)

@@ -348,19 +348,19 @@ def tile_list_fold_match_evidence_kernel(
         def h_step(step):
             return h_halves[step * QUARTER // HALF][:, step % (HALF // QUARTER)]
 
-        def product(step, g):
+        def product(step, g, w0=0, w1=QUARTER):
             j, c0 = divmod(step * QUARTER, HALF)
-            cols = slice(c0, c0 + QUARTER)
+            cols = slice(c0 + w0, c0 + w1)
             nc.vector.tensor_tensor(
-                h_step(step)[:, g].rearrange("p (c i) t -> p c t i", i=LINE),
+                h_step(step)[:, g, w0:w1].rearrange("p (c i) t -> p c t i", i=LINE),
                 match[g][j][:, :, cols].rearrange("p t (c i) -> p c t i", i=LINE),
                 evidence[g][j][:, :, cols].rearrange("p t (c i) -> p c t i", i=LINE),
                 ALU.mult,
             )
 
-        def quantize_and_multiply(step, g):
-            nc.vector.quantize_mx(out=h_codes[step][g][:].bitcast(FP8X4), scales=h_plane[step][g][:],
-                                  in_=h_step(step)[:, g].rearrange("p j t -> p (j t)"))
+        def quantize_and_multiply(step, g, w0=0, w1=QUARTER):
+            nc.vector.quantize_mx(out=h_codes[step][g][:, w0:w1].bitcast(FP8X4), scales=h_plane[step][g][:, w0:w1],
+                                  in_=h_step(step)[:, g, w0:w1].rearrange("p j t -> p (j t)"))
             per_bank = 1 if step == steps - 1 else HALF // QUARTER
             if g == 0:
                 banks[step] = [next_bank(per_bank * QUARTER) for n in range(0, n_tiles, per_bank)]
@@ -368,12 +368,13 @@ def tile_list_fold_match_evidence_kernel(
                 for place in range(per_bank):
                     n0 = (u * per_bank + place) * P
                     nc.tensor.matmul_mx(
-                        out=bank[:, place * QUARTER:(place + 1) * QUARTER],
+                        out=bank[:, place * QUARTER + w0:place * QUARTER + w1],
                         lhsT=wc_codes[:, g, n0:n0 + P].bitcast(FP8X4),
                         lhsT_scale=wc_plane[:, g, n0:n0 + P],
-                        rhs=h_codes[step][g][:].bitcast(FP8X4),
-                        rhs_scale=h_plane[step][g][:],
-                        start=(g == 0 and place == 0), stop=(g == R_PASSES - 1 and place == per_bank - 1),
+                        rhs=h_codes[step][g][:, w0:w1].bitcast(FP8X4),
+                        rhs_scale=h_plane[step][g][:, w0:w1],
+                        start=(g == 0 and place == 0),
+                        stop=(g == R_PASSES - 1 and place == per_bank - 1 and w1 == QUARTER),
                     )
 
         def store(step, n):
@@ -391,10 +392,18 @@ def tile_list_fold_match_evidence_kernel(
 
         square_roots(last_roots[:, :, 0:QUARTER])
         for step in range(steps):
-            for g in range(R_PASSES):
-                product(step, g)
-            for g in range(R_PASSES):
-                quantize_and_multiply(step, g)
+            if step < steps - 1:
+                for g in range(R_PASSES):
+                    product(step, g)
+                for g in range(R_PASSES):
+                    quantize_and_multiply(step, g)
+            else:
+                product(step, 0)
+                product(step, 1, 0, P)
+                quantize_and_multiply(step, 0)
+                product(step, 1, P, QUARTER)
+                quantize_and_multiply(step, 1, 0, P)
+                quantize_and_multiply(step, 1, P, QUARTER)
             for n in range(0, n_tiles, 2):
                 store(step, n)
             if step == 0:

@@ -22,6 +22,7 @@ PASS = P * PACK
 R_PASSES = H // PASS
 QUAD = 32
 QUADS = P // QUAD
+BLOCK_ROWS = 8
 GROUP = 16
 HALF = 512
 HALVES = S // HALF
@@ -91,8 +92,7 @@ def tile_list_fold_match_evidence_kernel(
                                   in_=rows.unsqueeze(0).to_broadcast([QUAD // 4, 4, rows.shape[1]]))
 
         nc.sync.dma_start(fold_list[:], offs)
-        for u in range(2):
-            nc.sync.dma_start(out=fold_bytes[u:P:GROUP, :].bitcast(I32), in_=tab_scales[0][u:GROUP:2, :].bitcast(I32))
+        nc.sync.dma_start(out=fold_bytes[0:P:BLOCK_ROWS, :].bitcast(I32), in_=tab_scales[0].bitcast(I32))
         nc.sync.dma_start(out=gain_cols[:], in_=gain.rearrange("(g p t) -> p g t", p=P, t=PACK))
         nc.sync.dma_start(query_list[:], offs2)
         nc.sync.dma_start(
@@ -123,9 +123,7 @@ def tile_list_fold_match_evidence_kernel(
 
         fold_picked = held([P, S], U8, "fold_picked")
         gather_scales(fold_picked, fold_bytes, fold_list, 0, S)
-        for r in range(4):
-            rows = fold_picked[GROUP * (r // 2) + r % 2:P:QUAD, :]
-            nc.sync.dma_start(out=fold_plane[r:P:QUAD, :].bitcast(I32), in_=rows.bitcast(I32))
+        move_scales(fold_plane[:], fold_picked[:], BLOCK_ROWS)
         wm_raw = placed([P, 2 * H], U8, "wm_raw", WE_BYTES)
         nc.sync.dma_start(out=wm_raw[:].bitcast(I32), in_=wm_words[0].bitcast(I32))
         we_second = placed([P, PACK, PASS], F32, "we_second", 0)

from contextlib import ExitStack

import concourse.mybir as mybir

K, T, S, H, N = 512, 2048, 1024, 1024, 512
FLOPS = 2 * (3 * K * H * S + H * N * S)

F32 = mybir.dt.float32
BF16 = mybir.dt.bfloat16
I32 = mybir.dt.int32
U32 = mybir.dt.uint32
U16 = mybir.dt.uint16
U8 = mybir.dt.uint8
FP8X4 = mybir.dt.float8_e4m3fn_x4
FP4X4 = mybir.dt.float4_e2m1fn_x4
ACT = mybir.ActivationFunctionType
ALU = mybir.AluOpType

P = 128
PACK = 4
PASS = P * PACK
R_PASSES = H // PASS
QUAD = 32
QUADS = P // QUAD
BLOCK_ROWS = 8
GROUP = 16
HALF = 512
HALVES = S // HALF
QUARTER = 256
WE_COLS = 256
EARLY_SCALES = 768
WE_BYTES = PACK * PASS * 4
LINE = 4
BANKS = 8
TABLE_HOLD = 3
SCALAR_B = (4, 5, 6)
TINY = 2.0 ** -120


def tile_list_fold_match_evidence_kernel(
    tc, tab_words, tab_scales, tab2_words, tab2_scales, wm_words, wm_scales,
    we, gain, wc_words, wc_scales, offs, offs2, out,
):
    nc = tc.nc
    with ExitStack() as ctx:
        lists = ctx.enter_context(tc.tile_pool(name="lists", bufs=1))
        keep = ctx.enter_context(tc.tile_pool(name="keep", bufs=1))
        reused = ctx.enter_context(tc.tile_pool(name="reused", bufs=1))
        psum = ctx.enter_context(tc.psum_pool(name="psum", bufs=1))
        taken = []

        def next_bank(width):
            bank = psum.tile([P, width], F32, name="sums", tag="bank%d" % (len(taken) % BANKS))
            taken.append(bank)
            return bank

        def held(shape, dtype, name, after=""):
            return keep.tile(shape, dtype, name=name, tag=after or name, align_bytes=64)

        def placed(shape, dtype, name, offset):
            return reused.tile(shape, dtype, name=name, offset=offset, align_bytes=64)

        fold_list = lists.tile([P, S // GROUP], U16, name="fold_list")
        query_list = lists.tile([P, S // GROUP], U16, name="query_list")

        fold_bytes = placed([P, T], U8, "fold_bytes", WE_BYTES - T // 2)
        query_bytes = held([P, T], U8, "query_bytes")
        fold_plane = held([P, S], U8, "fold_plane")
        query_plane = [held([P, HALF], U8, "query_plane0")]
        gain_cols = held([P, R_PASSES, PACK], F32, "gain_cols")

        nc.gpsimd.memset(fold_bytes[:].bitcast(I32), 0)
        for p0, p1 in ((QUAD, 2 * QUAD), (2 * QUAD, P)):
            nc.vector.memset(query_bytes[p0:p1, :].bitcast(I32), 0)
        for plane in (fold_plane, query_plane[0]):
            nc.vector.memset(plane[:].bitcast(I32), 0)

        we_parts = [held([P, PACK, WE_COLS], F32, "we_part%d" % part) for part in range(PASS // WE_COLS)]
        fold_words = placed([P, T], U32, "fold_words", 2 * WE_BYTES)

        def load_we(dst, c0, width):
            nc.sync.dma_start(out=dst, in_=we[:, c0:c0 + width].rearrange("(p i) w -> p i w", i=PACK))

        def load_words(dst, words):
            nc.sync.dma_start(out=dst[:].bitcast(I32),
                              in_=words[0].rearrange("p t i -> p (t i)").bitcast(I32))

        def load_scale_rows(plane, scales):
            for d in range(QUADS):
                rows = scales[4 * d:4 * d + 4, :].bitcast(I32)
                nc.sync.dma_start(out=plane[QUAD * d:QUAD * (d + 1), :].bitcast(I32),
                                  in_=rows.unsqueeze(0).to_broadcast([QUAD // 4, 4, rows.shape[1]]))

        nc.sync.dma_start(fold_list[:], offs)
        nc.sync.dma_start(out=fold_bytes[0:P:BLOCK_ROWS, :].bitcast(I32), in_=tab_scales[0].bitcast(I32))
        nc.sync.dma_start(out=gain_cols[:], in_=gain.rearrange("(g p t) -> p g t", p=P, t=PACK))
        nc.sync.dma_start(query_list[:], offs2)
        nc.sync.dma_start(
            out=query_bytes[0:QUAD, :].bitcast(I32),
            in_=tab2_scales[0].bitcast(I32).unsqueeze(1).to_broadcast([GROUP, QUAD // GROUP, T // 4]),
        )
        for part in range(PASS // WE_COLS):
            load_we(we_parts[part][:], part * WE_COLS, WE_COLS)
        load_words(fold_words, tab_words)

        gain_flat = gain_cols[:].rearrange("p g t -> p (g t)")
        row_factor = held([P, R_PASSES * PACK], F32, "row_factor")
        gain_squared = held([P, R_PASSES * PACK], F32, "gain_squared")
        nc.scalar.activation(row_factor[:], gain_flat, ACT.Sign)
        nc.scalar.activation(gain_squared[:], gain_flat, ACT.Square)

        def gather_scales(picked, window, picks, j0, j1):
            nc.vector.tensor_copy(picked[:], window[:].indirect(picks[:, j0 // GROUP:j1 // GROUP]))

        def move_scales(plane, picked, row_step):
            for d in range(QUADS):
                rows = picked[4 * d * row_step:4 * (d + 1) * row_step:row_step, :]
                nc.sync.dma_start(out=plane[QUAD * d:QUAD * d + 4, :].bitcast(I32), in_=rows.bitcast(I32))

        def gather_words(dst, words, picks, j):
            per_half = HALF // GROUP
            nc.vector.tensor_copy(dst[j][:], words[:].indirect(picks[:, j * per_half:(j + 1) * per_half]))

        fold_picked = held([P, S], U8, "fold_picked")
        gather_scales(fold_picked, fold_bytes, fold_list, 0, S)
        move_scales(fold_plane[:], fold_picked[:], BLOCK_ROWS)
        wm_raw = placed([P, 2 * H], U8, "wm_raw", WE_BYTES)
        nc.sync.dma_start(out=wm_raw[:].bitcast(I32), in_=wm_words[0].bitcast(I32))
        we_second = placed([P, PACK, PASS], F32, "we_second", 0)
        load_we(we_second[:], PASS, PASS)
        fold_cols = [held([P, HALF], U32, "fold_cols0")]
        early_picked = held([P, EARLY_SCALES], U8, "early_picked")
        gather_scales(early_picked, query_bytes, query_list, 0, EARLY_SCALES)
        move_scales(query_plane[0][:], early_picked[:, 0:HALF], QUAD // GROUP)

        we_bf = [held([P, PACK, P, PACK], BF16, "we_bf0")]
        we_codes = [held([P, PASS], U32, "we_codes%d" % g) for g in range(R_PASSES)]
        we_plane = [held([P, PASS], U8, "we_plane%d" % g) for g in range(R_PASSES)]

        def round_we_first(c0, c1, on_scalar):
            part, w0 = divmod(c0, WE_COLS)
            rounded = we_bf[0][:, :, c0 // PACK:c1 // PACK, :].rearrange("p t m i -> p m i t")
            loaded = we_parts[part][:, :, w0:w0 + c1 - c0].rearrange("p i (m t) -> p m i t", t=PACK)
            if on_scalar:
                nc.scalar.activation(rounded, loaded, ACT.Copy)
            else:
                nc.vector.tensor_copy(rounded, loaded)

        def quantize_we(g, t0, t1):
            nc.vector.quantize_mx(
                out=we_codes[g][:, t0 * P:t1 * P].bitcast(FP8X4),
                scales=we_plane[g][:, t0 * P:t1 * P],
                in_=we_bf[g][:, t0:t1].rearrange("p t m i -> p (t m i)"),
            )

        evidence = [[held([P, PACK, HALF], F32, "evidence%d%d" % (g, j)) for j in range(HALVES)]
                    for g in range(R_PASSES)]
        match = [[held([P, PACK, HALF], F32, "match%d%d" % (g, j)) for j in range(HALVES)]
                 for g in range(R_PASSES)]

        def evidence_tile(g, j, t, c0=0, c1=HALF):
            e = next_bank(c1 - c0)
            nc.tensor.matmul_mx(
                out=e[:],
                lhsT=we_codes[g][:, t * P:(t + 1) * P].bitcast(FP8X4),
                lhsT_scale=we_plane[g][:, t * P:(t + 1) * P],
                rhs=fold_cols[j][:, c0:c1].bitcast(FP8X4),
                rhs_scale=fold_plane[:, j * HALF + c0:j * HALF + c1],
                start=True, stop=True,
            )
            tile_no = g * PACK + t
            nc.scalar.activation(evidence[g][j][:, t, c0:c1], e[:], ACT.Tanh,
                                 scale=row_factor[:, tile_no:tile_no + 1])

        round_we_first(0, WE_COLS, True)
        round_we_first(WE_COLS, PASS, True)
        quantize_we(0, 0, PACK)
        for c0 in (0, QUARTER):
            nc.vector.tensor_copy(fold_cols[0][:, c0:c0 + QUARTER],
                                  fold_words[:].indirect(fold_list[:, c0 // GROUP:(c0 + QUARTER) // GROUP]))
            for t in range(2):
                evidence_tile(0, 0, t, c0, c0 + QUARTER)
        fold_cols.append(held([P, HALF], U32, "fold_cols1"))
        gather_words(fold_cols, fold_words, fold_list, 1)
        for j in range(HALVES):
            for t in range(2 if j == 0 else 0, PACK):
                evidence_tile(0, j, t)

        query_words = held([P, T], U32, "query_words", after="fold_picked")
        load_words(query_words, tab2_words)
        wm_raw_plane = held([P, H], U8, "wm_raw_plane", after="we_part1")
        load_scale_rows(wm_raw_plane[:], wm_scales[0])

        def reorder_words(g):
            nc.gpsimd.tensor_copy(
                wm_codes[g].rearrange("p (t m b) -> p t m b", t=PACK, b=2),
                wm_raw[:, 2 * g * PASS:2 * (g + 1) * PASS].rearrange("p (m t b) -> p t m b", t=PACK, b=2),
            )

        def reorder_plane(g):
            cols = slice(g * PASS, (g + 1) * PASS)
            nc.gpsimd.tensor_copy(
                wm_plane[:, cols].rearrange("p (t m) -> p t m", t=PACK),
                wm_raw_plane[:, cols].rearrange("p (m t) -> p t m", t=PACK),
            )

        wm_codes = [held([P, H], U8, "wm_early", after="we_bf0")[:]]
        reorder_words(0)
        we_bf.append(placed([P, PACK, P, PACK], BF16, "we_bf1", 2 * WE_BYTES))
        nc.vector.tensor_copy(
            we_bf[1][:].rearrange("p t m i -> p m i t"),
            we_second[:].rearrange("p i (m t) -> p m i t", t=PACK),
        )
        quantize_we(1, 0, PACK)
        for j in range(HALVES):
            for t in range(PACK):
                evidence_tile(1, j, t)
        query_plane.append(placed([P, HALF], U8, "query_plane1", 2 * WE_BYTES + 2 * H))
        wm_late = placed([P, 2 * H], U8, "wm_late", 2 * WE_BYTES)
        wm_plane = wm_late[:, 0:H]
        wm_codes.append(wm_late[:, H:2 * H])
        reorder_plane(0)
        nc.gpsimd.memset(query_plane[1][:].bitcast(I32), 0)
        reorder_words(1)
        reorder_plane(1)
        late_picked = placed([P, S - EARLY_SCALES], U8, "late_picked", 0)
        gather_scales(late_picked, query_bytes, query_list, EARLY_SCALES, S)
        move_scales(query_plane[1][:, 0:EARLY_SCALES - HALF], early_picked[:, HALF:], QUAD // GROUP)
        move_scales(query_plane[1][:, EARLY_SCALES - HALF:], late_picked[:], QUAD // GROUP)
        query_cols = [held([P, HALF], U32, "query_cols0", after="query_bytes"),
                      held([P, HALF], U32, "query_cols1")]
        gather_words(query_cols, query_words, query_list, 0)
        gather_words(query_cols, query_words, query_list, 1)

        tiles = [(j, g, t) for j in range(HALVES) for g in range(R_PASSES) for t in range(PACK)]
        last_tile = len(tiles) - 1
        squared = {}
        b_apart = {TABLE_HOLD: held([P, HALF], F32, "b_hold"), last_tile: placed([P, HALF], F32, "b_last", 4 * WE_BYTES - H)}

        def wm_product(g, t, picked, plane, j):
            acc = next_bank(HALF)
            tile_no = g * PACK + t
            nc.tensor.matmul_mx(
                out=acc[:],
                lhsT=wm_codes[g][:, 2 * P * t:2 * P * (t + 1)].bitcast(FP4X4),
                lhsT_scale=wm_plane[:, P * tile_no:P * (tile_no + 1)],
                rhs=picked[j][:].bitcast(FP8X4),
                rhs_scale=plane,
                start=True, stop=True,
            )
            return acc

        def b_place(k):
            j, g, t = tiles[k]
            return b_apart[k][:] if k in b_apart else match[g][j][:, t, :]

        def copy_b(k):
            j, g, t = tiles[k]
            b = wm_product(g, t, query_cols, query_plane[j][:], j)
            if k in SCALAR_B:
                nc.scalar.copy(b_place(k), b[:])
            else:
                nc.vector.tensor_copy(b_place(k), b[:])

        def subtract(k):
            j, g, t = tiles[k]
            a = wm_product(g, t, fold_cols, fold_plane[:, j * HALF:(j + 1) * HALF], j)
            nc.vector.tensor_tensor(match[g][j][:, t, :], b_place(k), a[:], ALU.subtract)

        def square(k0, k1, on_scalar=False, aside=False):
            j, g, t0 = tiles[k0]
            differences = match[g][j][:, t0:t0 + k1 - k0, :]
            dst = held([P, k1 - k0, HALF], F32, "squares_aside")[:] if aside else differences
            if on_scalar:
                nc.scalar.activation(dst, differences, ACT.Square)
            else:
                nc.gpsimd.tensor_tensor(dst, differences, differences, ALU.mult)
            for k in range(k0, k1):
                squared[k] = dst[:, k - k0, :]

        def inverse_root(k):
            j, g, t = tiles[k]
            inv = gain_inv[:, g * PACK + t:g * PACK + t + 1]
            nc.scalar.activation(match[g][j][:, t, :], squared[k], ACT.Abs_reciprocal_sqrt, bias=inv, scale=inv)

        def square_roots(roots):
            nc.scalar.activation(roots, roots, ACT.Square)

        copy_b(0)
        for k in range(len(tiles)):
            if k < last_tile and k + 1 not in SCALAR_B:
                copy_b(k + 1)
            subtract(k)
            if k + 3 == SCALAR_B[0]:
                for m in SCALAR_B:
                    copy_b(m)
            if k < PACK - 1:
                square(k, k + 1)
            elif PACK <= k < 3 * PACK and k % 2 == 1:
                square(k - 1, k + 1, aside=(k == 3 * PACK - 1))

        squared[3 * PACK] = placed([P, HALF], F32, "vector_squares", 4 * WE_BYTES)[:]
        first_of_last = match[R_PASSES - 1][HALVES - 1][:, 0, :]
        nc.vector.tensor_tensor(squared[3 * PACK], first_of_last, first_of_last, ALU.mult)

        wc_codes = held([P, R_PASSES, N], U32, "wc_codes", after="fold_picked")
        wc_plane = held([P, R_PASSES, N], U8, "wc_plane", after="we_part1")
        nc.sync.dma_start(
            out=wc_codes[:].bitcast(I32),
            in_=wc_words.rearrange("g p n i -> p g (n i)").bitcast(I32),
        )
        for g in range(R_PASSES):
            load_scale_rows(wc_plane[:, g, :], wc_scales[g])

        gain_inv = held([P, R_PASSES * PACK], F32, "gain_inv", after="b_hold")
        nc.scalar.activation(gain_inv[:], gain_squared[:], ACT.Abs_reciprocal_sqrt, bias=TINY)

        def group_roots(n):
            j, g, t = tiles[n * PACK]
            return match[g][j]

        for k in range(3 * PACK):
            inverse_root(k)
            if k == 1:
                square(PACK - 1, PACK, on_scalar=True)
            if k == 3 * PACK - 1:
                square(3 * PACK + 1, 4 * PACK, on_scalar=True, aside=True)
            if k % 2 == 1:
                square_roots(group_roots(k // PACK)[:, k % PACK - 1:k % PACK + 1, :])
        for k in range(3 * PACK, 4 * PACK):
            inverse_root(k)
        last_roots = group_roots(3)

        n_tiles = N // P
        steps = S // QUARTER
        h_shape = [P, HALF // QUARTER, R_PASSES, QUARTER, PACK]
        h_halves = [placed(h_shape, BF16, "h_half0", 3 * WE_BYTES), held(h_shape, BF16, "h_half1")]
        results = [held([P, HALF // QUARTER, n_tiles, QUARTER], F32, "results0", after="squares_aside"),
                   held([P, HALF // QUARTER, n_tiles, QUARTER], F32, "results1")]
        h_codes = [[held([P, QUARTER], U32, "h_codes%d%d" % (step, g)) for g in range(R_PASSES)]
                   for step in range(steps)]
        h_plane = [[held([P, QUARTER], U8, "h_plane%d%d" % (step, g)) for g in range(R_PASSES)]
                   for step in range(steps)]
        banks = {}

        def h_step(step):
            return h_halves[step * QUARTER // HALF][:, step % (HALF // QUARTER)]

        def product(step, g, w0=0, w1=QUARTER):
            j, c0 = divmod(step * QUARTER, HALF)
            cols = slice(c0 + w0, c0 + w1)
            nc.vector.tensor_tensor(
                h_step(step)[:, g, w0:w1].rearrange("p (c i) t -> p c t i", i=LINE),
                match[g][j][:, :, cols].rearrange("p t (c i) -> p c t i", i=LINE),
                evidence[g][j][:, :, cols].rearrange("p t (c i) -> p c t i", i=LINE),
                ALU.mult,
            )

        def quantize_and_multiply(step, g, w0=0, w1=QUARTER):
            nc.vector.quantize_mx(out=h_codes[step][g][:, w0:w1].bitcast(FP8X4), scales=h_plane[step][g][:, w0:w1],
                                  in_=h_step(step)[:, g, w0:w1].rearrange("p j t -> p (j t)"))
            per_bank = 1 if step == steps - 1 else HALF // QUARTER
            if g == 0:
                banks[step] = [next_bank(per_bank * QUARTER) for n in range(0, n_tiles, per_bank)]
            for u, bank in enumerate(banks[step]):
                for place in range(per_bank):
                    n0 = (u * per_bank + place) * P
                    nc.tensor.matmul_mx(
                        out=bank[:, place * QUARTER + w0:place * QUARTER + w1],
                        lhsT=wc_codes[:, g, n0:n0 + P].bitcast(FP8X4),
                        lhsT_scale=wc_plane[:, g, n0:n0 + P],
                        rhs=h_codes[step][g][:, w0:w1].bitcast(FP8X4),
                        rhs_scale=h_plane[step][g][:, w0:w1],
                        start=(g == 0 and place == 0),
                        stop=(g == R_PASSES - 1 and place == per_bank - 1 and w1 == QUARTER),
                    )

        def store(step, n):
            last = step == steps - 1
            j, c0 = divmod(step * QUARTER, HALF)
            result = results[j][:, c0 // QUARTER, n:n + 2, :]
            if last:
                nc.scalar.copy(result[:, 0, :], banks[step][n][:])
                nc.vector.tensor_copy(result[:, 1, :], banks[step][n + 1][:])
            else:
                nc.scalar.copy(result.rearrange("p u j -> p (u j)"), banks[step][n // 2][:])
            dst = out[n * P:(n + 2) * P, step * QUARTER:(step + 1) * QUARTER]
            queue = nc.scalar if last and n > 0 else nc.sync
            queue.dma_start(out=dst.rearrange("(u p) j -> p u j", p=P), in_=result)

        square_roots(last_roots[:, :, 0:QUARTER])
        for step in range(steps):
            if step < steps - 1:
                for g in range(R_PASSES):
                    product(step, g)
                for g in range(R_PASSES):
                    quantize_and_multiply(step, g)
            else:
                product(step, 0)
                product(step, 1, 0, P)
                quantize_and_multiply(step, 0)
                product(step, 1, P, QUARTER)
                quantize_and_multiply(step, 1, 0, P)
                quantize_and_multiply(step, 1, P, QUARTER)
            for n in range(0, n_tiles, 2):
                store(step, n)
            if step == 0:
                square_roots(last_roots[:, :, QUARTER:HALF])
